import numpy as np, ml_dtypes
CORES = [78,86,94,102,110,118]
N = 6
import mx_ref
BF = ml_dtypes.bfloat16
def entries(a):
    return np.ascontiguousarray(a.T).reshape(-1)
def table(e):
    return np.ascontiguousarray(np.reshape(e, (-1, 16)).T).astype(np.int32)
def cols(t, e):
    v = np.concatenate([t.reshape(128, -1, 4), np.zeros((128, 1, 4), BF)], axis=1)
    return np.ascontiguousarray(v[:, e]).reshape(128, -1)
def cut(t, i, w=512):
    return t[:, w * i:w * i + w]
def f(rng, *shape):
    return mx_ref.flush((rng.standard_normal(shape, dtype=np.float32) * np.exp2(rng.integers(-2, 3, shape[:-1] + (1,)))).astype(BF))
def wide(rng, *shape, cols=0):
    v = rng.standard_normal(shape, dtype=np.float32) * np.exp2(rng.integers(-12, 13, shape)).astype(np.float32)
    if cols: v *= np.repeat(np.exp2(rng.integers(-cols, cols + 1, shape[:-2] + (1, shape[-1] // 4))) * (rng.random(shape[:-2] + (1, shape[-1] // 4)) > 0.0625), 4, axis=-1).astype(np.float32)
    return mx_ref.flush(v.astype(BF))
T, V, M, CAPP, R, O = 384, 160, 256, 48, 3, 2
START = np.repeat(np.arange(N), V)
def loose(rng, at, to, who, but=-1):
    to = to.copy(); n = np.zeros((N, N), int); np.add.at(n, (at, to), 1)
    for i in rng.permutation(who):
        q = rng.integers(0, N)
        if q != but and n[:, q].sum() < M and (q == at[i] or n[at[i], q] < CAPP): n[at[i], to[i]] -= 1; n[at[i], q] += 1; to[i] = q
    return to
def turn(rng, at):
    to = at.copy(); far = 1 + rng.permutation(N - 1)
    for s in range(N):
        k = rng.permutation(np.flatnonzero(at == s))
        for i in range(min(N - 1, len(k) // CAPP)): to[k[CAPP * i:CAPP * i + CAPP]] = (s + far[i]) % N
    return to
def collect(rng, at, e):
    to = at.copy(); k = rng.permutation(np.flatnonzero(at == e))[M - (N - 1) * CAPP:]
    to[k] = (e + 1 + np.arange(len(k)) % (N - 1)) % N
    for s in range(N):
        if s != e: to[rng.permutation(np.flatnonzero(at == s))[:CAPP]] = e
    return to
def spill(rng, at, to, who, ranks):
    to = to.copy(); n = np.zeros((N, N), int); others = np.setdiff1d(np.arange(N * V), who); np.add.at(n, (at[others], to[others]), 1)
    for i in rng.permutation(who):
        q = ranks[np.argmin(np.where(n[at[i], ranks] < CAPP, n[:, ranks].sum(axis=0), N * V))]
        n[at[i], q] += 1; to[i] = q
    return to
def lists(rng, a, share=0.25):
    nx = rng.integers(0, N * T, (N, 2 * T)); free = [list(rng.permutation(2 * T)) for r in range(N)]
    way = np.zeros((R - 1, N * V), int)
    for k in range(R - 2, -1, -1):
        goal = a[k + 1] if k == R - 2 else a[k + 1] * T + way[k + 1] // 2
        known = {}
        for i in rng.permutation(N * V):
            s = int(a[k][i]); L = known.setdefault((s, int(goal[i])), [])
            if not L or rng.random() >= share:
                L.append(free[s].pop()); way[k, i] = L[-1]
            else: way[k, i] = L[rng.integers(0, len(L))]
        if k < R - 2: nx[a[k], way[k]] = goal
    nx[a[R - 2], way[R - 2]] = a[R - 1] * T + rng.integers(0, T, N * V)
    st = (way[0] // 2).reshape(N, V); bt = sum((way[k] % 2) << k for k in range(R - 1)).reshape(N, V)
    return {"nx": np.stack([table(e) for e in nx]), "st": np.stack([table(e) for e in st]), "bt": np.stack([table(e) for e in bt])}
def setup_inputs(rng):
    a = [START]
    for k in range(R - 1): a.append(loose(rng, a[k], a[k], np.arange(N * V)))
    return {"x": f(rng, N, 128, 4 * T), "w": f(rng, N, 128, R * O * 512), **lists(rng, a)}
def setup_inputs_through(rng):
    h = rng.integers(1, N); a = [START, START.copy(), (START + h) % N]
    for s in range(N):
        for g, k in enumerate(np.array_split(V * s + rng.permutation(V), -(-V // CAPP))): a[1][k] = (s + g) % N
    return {**setup_inputs(rng), **lists(rng, a)}
def setup_inputs_far(rng):
    a = [START]
    for k in range(R - 1): a.append(turn(rng, a[k]))
    a[R - 1] = loose(rng, a[R - 2], a[R - 1], np.flatnonzero(a[R - 1] == a[R - 2]))
    return {**setup_inputs(rng), **lists(rng, a)}
def setup_inputs_gather(rng):
    p = rng.permutation(N); home, end, bare = p[:3]; a = [START, START.copy()]
    for j, s in enumerate(p[2:]): a[1][rng.permutation(np.flatnonzero(START == s))[:min(CAPP, max(0, M - V - j * CAPP))]] = home
    to = collect(rng, a[1], end)
    to = spill(rng, a[1], to, np.flatnonzero(((a[1] == end) & (to != end)) | (to == bare)), np.append(p[3:], home))
    a.append(loose(rng, a[1], to, np.flatnonzero((to == a[1]) & (a[1] != end)), but=bare))
    return {**setup_inputs(rng), **lists(rng, a, share=0.75)}
def setup_inputs_stay(rng):
    p = rng.integers(0, N); a = [START, collect(rng, START, p)]
    a.append(loose(rng, a[1], a[1], np.flatnonzero(a[1] != p)))
    return {**setup_inputs(rng), **lists(rng, a)}
def setup_inputs_spread(rng):
    d = setup_inputs(rng); d["x"] = wide(rng, N, 128, 4 * T, cols=8); return d
def follow(nx, st, bt):
    n = np.concatenate([entries(t) for t in nx]); bits = np.concatenate([entries(t) for t in bt])
    at = [np.concatenate([entries(st[r]) + r * T for r in range(N)])]
    for k in range(R - 1): at.append(n[2 * at[k] + (bits >> k & 1)])
    return at
def check_inputs(d):
    b = []
    for name, top in (("nx", N * T), ("st", T), ("bt", 2 ** (R - 1))):
        if d[name].min() < 0 or d[name].max() >= top: b.append(name)
    if b: return b
    at = [t // T for t in follow(d["nx"], d["st"], d["bt"])]
    for k in range(R):
        if np.bincount(at[k], minlength=N).max() > M: b.append("walkers on a rank at step " + str(k))
    for k in range(R - 1):
        n = np.zeros((N, N), int); np.add.at(n, (at[k], at[k + 1]), 1); np.fill_diagonal(n, 0)
        if n.max() > CAPP: b.append("walkers from a rank to another from step " + str(k))
    return b
def reference(x, w, nx, st, bt):
    nodes = np.concatenate([x[r] for r in range(N)], axis=1)
    at = follow(nx, st, bt)
    y = np.zeros((N, 128, O * M), np.float32); ids = np.full((N, 2, M), -1, np.float32)
    for e in range(N):
        m = np.flatnonzero(at[R - 1] // T == e)
        ids[e, 0, :len(m)] = m // V; ids[e, 1, :len(m)] = m % V
        for k in range(R):
            c = np.full(M, -1); c[:len(m)] = at[k][m]
            q = mx_ref.quantize(cols(nodes, c))
            for o in range(O): y[e][:, M * o:M * o + M] += mx_ref.matmul(mx_ref.quantize(np.ascontiguousarray(cut(w[e], k * O + o))), q)
    return {"y": y, "id": ids}

@@ -1,0 +1,447 @@
+from concourse.bass import DstId, RemoteDMATransfer
+from concourse.mybir import dt, AluOpType, ActivationFunctionType
+
+N, TN, V, M, CAPP, NO = 6, 384, 160, 256, 48, 2
+REM = CAPP * (N - 1)
+N1 = REM + V
+N2 = REM + M
+GT = N * V + 1
+ZC = 128
+BN0, BH0, BH1 = ZC, ZC + 2 * REM, ZC + 2 * REM + M
+BW = BH1 + M
+
+_F, _I, _U, _C, _S = "float32", "int32", "uint16", "float8_e4m3fn_x4", "uint8"
+SCRATCH, POOL = {}, {}
+
+
+def _add(dtype, **shapes):
+    for name, shape in shapes.items():
+        SCRATCH[name] = ("sbuf", [128] + (list(shape) if isinstance(shape, tuple) else [shape]), dtype)
+
+
+def _pool(buf, dtype, **widths):
+    at = 0
+    for name, w in widths.items():
+        POOL[name] = (buf, at, w)
+        at += w
+    _add(dtype, **{buf: at})
+
+
+_add(_I, ci=40)
+_add(_F, cc=24, ones=1024, iot=1024, ctab=768, idw=1472, c1c=N2, c2a=N2, c2c=N2, ctw=TN, f16=N2, m16=N2, rmk=N2)
+_add(_I, st0=10, bt0=10, stA=10, nxr=768, nxB=768, ai0=V, s0i=10, pkw=32)
+_add(_F, n1r=V, Rr=V, nxa=V, Ra=V, mk0=V, cn0=V, pl5=V, pl0=V)
+_add(_U, offe=10, offR=10, offS=10, off0=10, offi=16, offj=10)
+_add(_F, zd0=(10, 32), zt0=(10, 32), za0=(10, 4), zb0=(10, 2), S0=800, S0t=800)
+_add(_I, m1=15, ai1=N1, s1i=25, f3w=15)
+_add(_F, nxT=800, nxm=768, nxn=768, t1=N1, pl1=N1, mk1=N1, cn1=N1)
+_add(_U, offE=26, offG=26, off1=26, off2=30, offc=16, offd=16)
+_add(_F, zd1=(25, 32), zt1=(25, 32), za1=(25, 4), zb1=(25, 2), S1=1792, S1t=992)
+_add(_I, m2=15, idr=M)
+_add(_F, PT=1472, PS=1472, pm=N2, P2a=N2, P2=N2, S2=1504, S2t=512, idg=M, ids=6 * M, yo0=M, yo1=M)
+_add(_U, offg2=32, offc2=32, offP=32, offF=64)
+_pool("pooli", _I, i0=50, s0h=10, s0k=10, pwa=15, pwb=10, xr=25, x2=25, x3=25, x4=25, xlo=25, xhi=25, g1=25, s1h=25, s1k=25,
+      f3s=16, sga=15, sgb=16, c1a=15, c1b=16, g2=31, h2=31, pwi=31, p2h=31, p2k=31)
+_pool("poolf", _F, e0=60, xiv=25, xp=25, xpp=25, GC=25, g1f=25, iv2=31, tr2=31, TC=31, gf2=31, ga=64)
+_add("bfloat16", xt=4 * (ZC + TN), wt=3072)
+for _n, _w in (("x", ZC + TN), ("w", 768), ("w0", V), ("sl1", REM), ("A", N1 + TN), ("sl2", 2 * REM), ("B", BW),
+               ("k0", M), ("k1", M), ("k2", M)):
+    SCRATCH[_n + "q"] = ("sbuf", [128, _w], _C)
+    SCRATCH[_n + "s"] = ("sbuf", [128, _w], _S)
+SCRATCH["ps0"] = ("psum", [128, 512], _F)
+SCRATCH["ps1"] = ("psum", [128, 512], _F)
+
+SEMAPHORES = ["qv", "qs", "qp", "qk", "dst0", "dbt0", "dnx", "dstA", "dx", "dw", "did", "dy0", "dy1", "am1", "ac1", "am2", "ac2", "loc"]
+
+add, sub, mul, mx, mn = AluOpType.add, AluOpType.subtract, AluOpType.mult, AluOpType.max, AluOpType.min
+eq, ge, gt, lt, ne = AluOpType.is_equal, AluOpType.is_ge, AluOpType.is_gt, AluOpType.is_lt, AluOpType.not_equal
+shr, band = AluOpType.arith_shift_right, AluOpType.bitwise_and
+Copy, Ident = ActivationFunctionType.Copy, ActivationFunctionType.Identity
+
+
+def rank_program(g, core, T, topo):
+    me = T.rank_of(core)
+    if me is None:
+        return
+    others = [(me + 1 + k) % N for k in range(N - 1)]
+
+    def pos(a, q):
+        return q if q < a else q - 1
+
+    eng = {"v": g.vector, "s": g.scalar, "p": g, "k": g.tensor, "y": g.sync}
+    know = {q: {} for q in eng}
+    count, wr, rd = {}, {}, {}
+
+    def need(q, evs):
+        for sem, val, snap in sorted(evs, key=lambda e: -len(e[2])):
+            if know[q].get(sem, 0) < val:
+                eng[q].wait_ge(T.sem[sem], val)
+                for a, b in list(snap.items()) + [(sem, val)]:
+                    if know[q].get(a, 0) < b:
+                        know[q][a] = b
+
+    def op(q, call, reads=(), writes=(), sem="", inc=1, total=None):
+        evs = []
+        for k in reads:
+            evs += wr.get(k, [])
+        for k in writes:
+            evs += wr.get(k, []) + rd.get(k, [])
+        best = {}
+        for e in evs:
+            if e[0] not in best or best[e[0]][1] < e[1]:
+                best[e[0]] = e
+        need(q, list(best.values()))
+        ins = call()
+        if sem is None:
+            return
+        sem = sem or "q" + q
+        ins.then_inc(T.sem[sem], inc)
+        count[sem] = count.get(sem, 0) + inc
+        ev = (sem, total or count[sem], dict(know[q]))
+        for k in writes:
+            wr[k] = [ev]
+            rd[k] = []
+        for k in reads:
+            rd.setdefault(k, []).append(ev)
+
+    def o(name, lo=None, hi=None, st=None, k=None, p=None):
+        ps = slice(None) if p is None else slice(p[0], p[1])
+        keys = (k,) if isinstance(k, str) else k or (name,)
+        if name in POOL:
+            name, at, w = POOL[name]
+            lo, hi = at + (lo or 0), at + (w if hi is None else hi)
+        return (keys, T[name][ps, slice(lo, hi, st)])
+
+    def o3(name, lo, hi, k=None):
+        return ((k or name,), T[name][:, :, lo:hi])
+
+    def ci(j, p=None):
+        return o("ci", j, j + 1, k="ci%d" % j, p=p)
+
+    def cc(j):
+        return o("cc", j, j + 1, k="cc%d" % j)
+
+    def ind(win, off):
+        return (win[0] + off[0], win[1].indirect(off[1]))
+
+    def cp(out, in_):
+        op("v", lambda: g.vector.tensor_copy(out[1], in_[1]), in_[0], out[0])
+
+    def ms(out, c):
+        op("v", lambda: g.vector.memset(out[1], c), (), out[0])
+
+    def tt(out, a, b, f):
+        op("v", lambda: g.vector.tensor_tensor(out[1], a[1], b[1], f), a[0] + b[0], out[0])
+
+    def ts(out, a, s1, f1, s2=None, f2=None):
+        rk = a[0] + (s1[0] if isinstance(s1, tuple) else ()) + (s2[0] if isinstance(s2, tuple) else ())
+        v1 = s1[1] if isinstance(s1, tuple) else s1
+        v2 = s2[1] if isinstance(s2, tuple) else s2
+        if f2 is None:
+            op("v", lambda: g.vector.tensor_scalar(out[1], a[1], v1, None, f1), rk, out[0])
+        else:
+            op("v", lambda: g.vector.tensor_scalar(out[1], a[1], v1, v2, f1, f2), rk, out[0])
+
+    def scan(out, d0, d1, init):
+        rk = d0[0] + d1[0] + (init[0] if isinstance(init, tuple) else ())
+        iv = init[1] if isinstance(init, tuple) else init
+        op("v", lambda: g.vector.tensor_tensor_scan(out[1], d0[1], d1[1], iv, mul, add), rk, out[0])
+
+    def tr(out, in_):
+        op("v", lambda: g.vector.transpose(out[1], in_[1]), in_[0], out[0])
+
+    def act(out, in_, f=Copy, more=(), **kw):
+        op("s", lambda: g.scalar.activation(out[1], in_[1], f, **kw), in_[0] + tuple(more), out[0])
+
+    def scatter(win, off, in_):
+        op("v", lambda: g.vector.tensor_copy(win[1].indirect(off[1]), in_[1]), win[0] + off[0] + in_[0], win[0])
+
+    def pick(outn, lo, hi, winn, off, key, wkeys):
+        op("v", lambda: g.vector.tensor_copy(T[outn + "q"][:, lo:hi].bitcast(dt.uint32), T[winn + "q"][:].bitcast(dt.uint32).indirect(off[1])),
+           tuple(x + "q" for x in wkeys) + off[0], (key + "q",))
+        op("s", lambda: g.scalar.activation(T[outn + "s"][:, lo:hi], T[winn + "s"][:].indirect(off[1]), Copy),
+           tuple(x + "s" for x in wkeys) + off[0], (key + "s",))
+
+    def quant(outn, lo, hi, src, a, b, skeys, key):
+        op("v", lambda: g.vector.quantize_mx(T[outn + "q"][:, lo:hi], T[outn + "s"][:, lo:hi], T[src][:, 4 * a:4 * b]), skeys, (key + "q", key + "s"))
+
+    def fan(reads, src, dst, rsem):
+        def call():
+            trs = []
+            for k, q in enumerate(others[:4]):
+                c = T.cores[q]
+                rid, pid, _ = topo.addr(c)
+                m = sum(1 << e for e in topo.engines(core, c)[k::4])
+                trs.append(RemoteDMATransfer(dst_ids=[DstId(rid=rid, pnc=pid)], dma_engine_mask=m, remote_sem=T.sem[rsem], src=src(q), dst=dst(q)))
+            g.remote_dma_fused(trs, local_sem=T.sem["loc"])
+            c = T.cores[others[4]]
+            rid, pid, _ = topo.addr(c)
+            g.remote_dma(dst(others[4]), src(others[4]), T.sem[rsem], T.sem["loc"], pid, rid, topo.mask(core, c))
+        op("p", call, reads, (), sem=None)
+        count["loc"] = count.get("loc", 0) + 16
+
+    def fan_numbers(name, key, land, rsem):
+        fan((key,), lambda q: T[name][:, 3 * pos(me, q):3 * pos(me, q) + 3], lambda q: T[land][:, 3 * pos(q, me):3 * pos(q, me) + 3], rsem)
+
+    def fan_columns(name, land, at, w, rsem):
+        def src(n, q):
+            return T[n][:, w * pos(me, q):w * pos(me, q) + w]
+
+        def dst(n, q):
+            return T[n][:, at + w * pos(q, me):at + w * pos(q, me) + w]
+        fan((name + "q",), lambda q: src(name + "q", q).bitcast(dt.uint8), lambda q: dst(land + "q", q).bitcast(dt.uint8), rsem)
+        fan((name + "s",), lambda q: src(name + "s", q), lambda q: dst(land + "s", q), rsem)
+
+    for s_, v_, ks in (("am1", 16, ("m1",)), ("ac1", 32, ("Alq", "Als")), ("am2", 16, ("m2",)), ("ac2", 32, ("Blq", "Bls"))):
+        count[s_] = v_
+        for k in ks:
+            wr[k] = [(s_, v_, {})]
+
+    def dma(q, out, in_, sem, total=None):
+        op(q, lambda: eng[q].dma_start(out[1], in_[1]), in_[0], out[0], sem=sem, inc=16, total=total)
+
+    P = (0, 16)
+    dma("y", o("st0", p=P), ((), T.st[:]), "dst0")
+    dma("s", o("bt0", p=P), ((), T.bt[:]), "dbt0")
+    ms(o("nxr"), 0)
+    dma("y", o("nxr", p=(0, 1)), ((), T.nx[:]), "dnx")
+    dma("y", o("xt", 4 * ZC, 4 * (ZC + TN), k="xtx"), ((), T.x[:]), "dx")
+    for k in range(8):
+        dma("ys"[k % 2], o("stA", p=(16 * k, 16 * k + 16), k="stA%d" % k), ((), T.st[:]), "dstA", 128)
+    stA = (tuple("stA%d" % k for k in range(8)), T.stA[:])
+
+    def iota(out, pattern, base=0, mult=0):
+        op("p", lambda: g.iota(out[1], pattern, base, mult, allow_small_or_imprecise_dtypes=True), (), out[0])
+    wc = o("ci", 8, 40, k="wc")
+    iota(ci(0), [[1, 1]], 0, 1)
+    iota(wc, [[16, 32]])
+    iota(o("ctab"), [[1, 8], [0, 2], [8, 48]])
+    iota(o("iot", 0, 512, k="iota"), [[1, 512]])
+    iot2 = ("iota", "iotb")
+
+    JF, P16, OD, DQ, BASE, F3, SG, C1, S1R, CF, R16, R256, RSS, SG1, C128 = range(15)
+    X1, X2, X3 = cc(20), cc(21), cc(22)
+    ms(o("offe"), 0)
+    ms(o("offR"), 0)
+    ts(ci(1), ci(0), 31, band)
+    ts(ci(2), ci(0), 15, band)
+    cp(cc(JF), ci(1))
+    cp(cc(P16), ci(2))
+    ts(o("e0", 50, 60, k="wi"), o("ci", 8, 18, k="wc"), cc(P16), add, 1.0, add)
+    ts(cc(OD), cc(JF), 16.0, ge, 16.0, mul)
+    ts(X1, cc(JF), 7.0, ge, 1000.0, mul)
+    ts(X2, cc(JF), float(me), gt, -48.0, mul)
+    ts(X3, cc(JF), float(me), eq, float(REM - CAPP * me), mul)
+    tt(cc(DQ), cc(JF), X1, add)
+    tt(X2, X2, X3, add)
+    ts(X3, cc(JF), 6.0, eq, 256.0, mul)
+    ts(X1, cc(JF), 48.0, mul, -1.0, add)
+    tt(X2, X2, X3, add)
+    tt(cc(BASE), X1, X2, add)
+    for k, r in ((F3, 8.0), (SG, 9.0), (C1, 10.0), (S1R, 11.0)):
+        ts(cc(k), cc(P16), r, eq)
+    ms(o("ones"), 1.0)
+    ms(o("S0"), 0.0)
+    ms(o("xt", 0, 4 * ZC, k="xtz"), 0.0)
+
+    def i0(j):
+        return o("i0", 10 * j, 10 * j + 10, k="i0%d" % j, p=P)
+
+    def e0(j):
+        return o("e0", 10 * j, 10 * j + 10, k="e0%d" % j, p=P)
+    ts(i0(0), o("bt0", p=P), 1, band)
+    ts(i0(1), o("st0", p=P), 3, shr)
+    ts(i0(2), o("bt0", p=P), 1, shr)
+    ts(e0(1), o("st0", p=P), 96.0, mul)
+    ts(e0(2), i0(0), 48.0, mul)
+    ts(e0(3), i0(1), -767.0, mul)
+    tt(e0(4), e0(1), e0(2), add)
+    ts(e0(0), i0(2), 256.0, mul)
+    tt(e0(4), e0(4), e0(3), add)
+    cp(o("offe", p=P), e0(4))
+    tt(e0(0), e0(0), o("e0", 50, 60, k="wi", p=P), add)
+    cp(o("offR", p=P), e0(0))
+    cp(o("n1r"), ind(o("nxr"), o("offe")))
+    op("p", lambda: g.partition_broadcast(T.nxa[:], T.n1r[0:1, :], 128), ("n1r",), ("nxa",))
+    cp(o("Rr"), ind(o("iot", 0, 512, k="iota"), o("offR")))
+    op("p", lambda: g.partition_broadcast(T.Ra[:], T.Rr[0:1, :], 128), ("Rr",), ("Ra",))
+    op("p", lambda: g.partition_broadcast(T.nxB[:], T.nxr[0:1, :], 128), ("nxr",), ("nxB",))
+    ts(o("offS"), stA, float(ZC), add)
+    act(o("nxn"), o("ctab"), more=("cc%d" % C1,), scale=cc(C1)[1])
+    act(o("pl5"), o("nxa"), Ident, scale=512.0, bias=512.0)
+
+    def spread(src, s, off):
+        ts(o(s + "h"), src, 4, shr)
+        ts(o(s + "k"), o(s + "h"), 16.0, mul, cc(OD), add)
+        tt(o(s + "h"), src, o(s + "k"), add)
+        cp(off, o(s + "h"))
+
+    def place(f, nk, src, off, meanwhile):
+        zd, zt, za, zb, s = "zd" + f, "zt" + f, "za" + f, "zb" + f, "s" + f
+        ts(o("ai" + f), src, -191.5, add, 1.0 / TN, mul)
+        ts(o("mk" + f), o("ai" + f), cc(DQ), eq)
+        scan(o("cn" + f), o("ones", 0, 16 * nk), o("mk" + f), cc(BASE))
+        tt(o3(zd, 0, 16, zd + "l"), o("mk" + f), o("cn" + f), mul)
+        act(o3(zd, 16, 32, zd + "h"), o3(zd, 0, 16, zd + "l"))
+        meanwhile()
+        op("v", lambda: g.vector.transpose(T[zt][:], T[zd][:]), (zd + "l", zd + "h"), (zt,))
+        tt(o3(za, 0, 4), o3(zt, 0, 4), o3(zt, 4, 8), add)
+        tt(o3(zb, 0, 2), o3(za, 0, 2), o3(za, 2, 4), add)
+        op("v", lambda: g.vector.tensor_tensor(T[s + "i"][:], T[zb][:, :, 0], T[zb][:, :, 1], add), (zb,), (s + "i",))
+        spread(o(s + "i"), s, off)
+
+    def row(out, name, lo, hi, j, key):
+        tt(out, o(name, lo + j, hi, 32, k=key), o(name, lo + j + 16, hi, 32, k=key), add)
+
+    def during0():
+        quant("x", 0, ZC + TN, "xt", 0, ZC + TN, ("xtx", "xtz"), "x")
+        tt(o("pl0"), o("pl5"), o("Ra"), add)
+    place("0", 10, o("nxa"), o("off0"), during0)
+    scatter(o("S0"), o("off0"), o("pl0"))
+    pick("w0", 0, V, "x", o("offS"), "w0", ("x",))
+    tr(o("S0t", 0, 480, k="S0ta"), o("S0", 0, 480))
+    row(o("pkw", 0, 15, k="pkwr"), "S0t", 0, 480, 0, "S0ta")
+    fan_numbers("pkw", "pkwr", "m1", "am1")
+    ts(o("pwa"), o("pkw", 0, 15, k="pkwr"), 255, band)
+    ts(o("offi", 0, 15), o("pwa"), -1.0, add, 0.0, mx)
+    pick("sl1", 0, REM, "w0", o("offi", 0, 15), "sl1", ("w0",))
+    fan_columns("sl1", "A", 0, CAPP, "ac1")
+    dma("s", o("wt"), ((), T.w[:]), "dw")
+    tr(o("S0t", 480, 800, k="S0tb"), o("S0", 480, 800))
+    row(o("pkw", 16, 26, k="pkws"), "S0t", 480, 800, 0, "S0tb")
+    ts(o("pwb"), o("pkw", 16, 26, k="pkws"), 255, band)
+    ts(o("offj"), o("pwb"), -1.0, add, 0.0, mx)
+    pick("A", REM, N1, "w0", o("offj"), "Ah", ("w0",))
+
+    act(o("iot", 512, 1024, k="iotb"), o("iot", 0, 512, k="iota"), Ident, bias=512.0)
+    act(o("idw", 0, GT, k="idwa"), o("iot", 0, GT, k=iot2), more=("cc%d" % F3,), scale=cc(F3)[1])
+    act(o("c1c"), o("iot", 0, N2, k="iota"), Ident, more=("cc%d" % SG,), scale=cc(SG)[1], bias=cc(SG)[1])
+    act(o("S1", 0, 992), o("iot", 0, 992, k=iot2), scale=0.0)
+    act(o("PT", 0, 992), o("iot", 0, 992, k=iot2), scale=0.0)
+    act(o("PT", 992, 1472), o("iot", 0, 480, k="iota"), scale=0.0)
+    act(o("S2", 0, 512), o("iot", 0, 512, k="iota"), scale=0.0)
+    act(o("PS", GT, GT + N2, k="PSb"), o("iot", 0, N2, k="iota"), Ident, bias=256.0)
+    ts(X1, cc(P16), 8.0, lt)
+    ts(X2, cc(F3), 1024.0, mul)
+    tt(cc(CF), X1, X2, add)
+    ts(o("nxm"), o("nxB"), cc(CF), mul)
+    tt(o("nxT", 0, 768, k="nxTa"), o("nxm"), o("nxn"), add)
+    ms(o("nxT", 768, 800, k="nxTz"), 6.5 * TN - 1)
+    ms(o("idw", GT, 1472, k="idwz"), 0.0)
+    for q in others:
+        ms(o("GC", 3 * pos(me, q), 3 * pos(me, q) + 3), float(V * q))
+    ms(o("GC", 15, 25), float(V * me))
+    idw = o("idw", 0, 1472, k=("idwa", "idwz"))
+    quant("A", N1, N1 + TN, "xt", ZC, ZC + TN, ("xtx",), "Ax")
+    iota(o("c2a", 0, REM, k="c2aa"), [[32, 15], [1, 16]], BN0)
+    iota(o("c2a", REM, N2, k="c2ab"), [[1, M]], BH0)
+    iota(o("f16"), [[0, 31], [1, 16]])
+
+    ts(o("xr", 0, 15), o("m1"), 8, shr)
+    ts(o("xr", 15, 25), o("pkw", 16, 26, k="pkws"), 8, shr)
+    ts(o("g1", 0, 15), o("m1"), 255, band)
+    ts(o("g1", 15, 25), o("pkw", 16, 26, k="pkws"), 255, band)
+    ts(o("x2"), o("xr"), float(-(2 * TN * me + 2)), add)
+    tt(o("g1f"), o("g1"), o("GC"), add)
+    ts(o("xiv"), o("x2"), 0.0, lt, 8000.0, mul)
+    cp(o("offG", 0, 25), o("g1f"))
+    tt(o("x3"), o("x2"), o("xiv"), add)
+    ts(o("x4"), o("x3"), 783.0, mn)
+    ts(o("xlo"), o("x4"), 15, band)
+    ts(o("xhi"), o("x4"), 4, shr)
+    ts(o("xp"), o("xlo"), 48.0, mul)
+    tt(o("xpp"), o("xp"), o("xhi"), add)
+    cp(o("offE", 0, 25), o("xpp"))
+    tt(o("t1"), ind(idw, o("offG", 0, 25)), o("c1c", 0, N1), add)
+    tt(o("pl1"), ind(o("nxT", 0, 800, k=("nxTa", "nxTz")), o("offE", 0, 25)), o("t1"), add)
+    place("1", 25, o("pl1"), o("off1", 0, 25), lambda: None)
+    scatter(o("S1"), o("off1", 0, 25), o("pl1"))
+    tr(o("S1t", 0, 480, k="S1ta"), o("S1", 0, 480))
+    row(o("f3w"), "S1t", 0, 480, 8, "S1ta")
+    fan_numbers("f3w", "f3w", "m2", "am2")
+    row(o("sga"), "S1t", 0, 480, 9, "S1ta")
+    row(o("c1a"), "S1t", 0, 480, 10, "S1ta")
+    ts(o("off2", 0, 30, 2), o("sga"), -1.0, add, 0.0, mx)
+    ts(o("off2", 1, 30, 2), o("c1a"), float(N1), add)
+    pick("sl2", 0, 2 * REM, "A", o("off2"), "sl2", ("Al", "Ah", "Ax"))
+    fan_columns("sl2", "B", BN0, 2 * CAPP, "ac2")
+    tr(o("S1t", 480, 992, k="S1tb"), o("S1", 480, 992))
+    row(o("f3s"), "S1t", 480, 992, 8, "S1tb")
+    row(o("sgb"), "S1t", 480, 992, 9, "S1tb")
+    row(o("c1b"), "S1t", 480, 992, 10, "S1tb")
+    ts(o("offc"), o("sgb"), -1.0, add, 0.0, mx)
+    ts(o("offd"), o("c1b"), float(ZC), add)
+    pick("B", BH0, BH1, "A", o("offc"), "Bh0", ("Al", "Ah", "Ax"))
+    pick("B", BH1, BW, "x", o("offd"), "Bh1", ("x",))
+
+    ts(cc(C128), cc(C1), float(ZC), mul)
+    ts(cc(R16), cc(S1R), 16.0, mul)
+    ts(cc(R256), cc(S1R), 256.0, mul)
+    tt(cc(RSS), cc(SG), cc(S1R), add)
+    act(o("ctw"), o("iot", 0, TN, k="iota"), Ident, more=("cc%d" % C1, "cc%d" % C128), scale=cc(C1)[1], bias=cc(C128)[1])
+    ts(o("c2c", 0, REM), o("c2a", 0, REM, k="c2aa"), cc(R16), add, cc(RSS), mul)
+    ts(o("c2c", REM, N2), o("c2a", REM, N2, k="c2ab"), cc(R256), add, cc(RSS), mul)
+    ts(o("m16"), o("f16"), cc(P16), eq)
+    ts(o("rmk"), o("f16"), 0.0, ne)
+    ts(o("TC"), o("ci", 8, 39, k="wc"), cc(P16), add, float(GT), add)
+    quant("B", 0, ZC, "xt", 0, ZC, ("xtz",), "Bz")
+    quant("w", 0, 384, "wt", 0, 384, ("wt",), "wa")
+    quant("w", 384, 768, "wt", 384, 768, ("wt",), "wb")
+
+    ts(o("g2", 15, 31), o("f3s"), 1023, band)
+    ts(o("h2", 15, 31), o("f3s"), 10, shr)
+    ts(o("g2", 0, 15), o("m2"), 1023, band)
+    ts(o("h2", 0, 15), o("m2"), 10, shr)
+    ts(o("iv2"), o("g2"), 0.0, eq)
+    ts(o("offc2", 0, 31), o("h2"), float(-TN * me), add, 0.0, mx)
+    tt(o("tr2"), o("iv2"), o("TC"), mul)
+    tt(o("gf2"), o("tr2"), o("g2"), add)
+    cp(o("offg2", 0, 31), o("gf2"))
+    og = o("offg2", 0, 31)
+    scatter(o("PT"), og, o("ones", 0, N2))
+    tt(o("P2a"), ind(idw, og), o("c2c"), add)
+    scan(o("PS", 0, GT, k="PSa"), o("ones", 0, GT), o("PT", 0, GT), -1.0)
+    tt(o("P2"), ind(o("ctw"), o("offc2", 0, 31)), o("P2a"), add)
+    tt(o("pm"), ind(o("PS", 0, GT + N2, k=("PSa", "PSb")), og), o("m16"), mul)
+    scan(o("P2a"), o("rmk"), o("pm"), 0.0)
+    cp(o("pwi"), o("P2a", 15, N2, 16))
+    spread(o("pwi"), "p2", o("offP", 0, 31))
+    scatter(o("S2"), o("offP", 0, 31), o("P2"))
+    tr(o("S2t"), o("S2", 0, 512))
+    for k, j in enumerate((10, 9, 11, 8)):
+        row(o("ga", 16 * k, 16 * k + 16, k="ga%d" % k), "S2t", 0, 512, j, "S2t")
+        cp(o("offF", 16 * k, 16 * k + 16, k="offF%d" % k), o("ga", 16 * k, 16 * k + 16, k="ga%d" % k))
+    off = [o("offF", 16 * k, 16 * k + 16, k="offF%d" % k) for k in range(4)]
+    pick("k2", 0, M, "x", off[0], "k2", ("x",))
+
+    def product(k, n, last):
+        for oo in range(NO):
+            a = 128 * (k * NO + oo)
+            op("k", lambda: g.tensor.matmul_mx(T["ps%d" % oo][:, 0:M], T.wq[:, a:a + 128], T.ws[:, a:a + 128], T[n + "q"][:], T[n + "s"][:], k == 2, last),
+               ("waq", "was", "wbq", "wbs", n + "q", n + "s"), ("ps%d" % oo,) if last else ())
+    product(2, "k2", False)
+
+    def ids(j):
+        return o("ids", M * j, M * j + M, k="ids%d" % j)
+    cp(o("idg"), ind(o("iot", k=iot2), off[3]))
+    ts(o("idr"), o("idg"), -(V + 1) / 2.0, add, 1.0 / V, mul)
+    cp(ids(0), o("idr"))
+    ts(ids(1), ids(0), float(-V), mul, -1.0, add)
+    tt(ids(2), ids(1), o("idg"), add)
+    ts(ids(3), o("idg"), 0.0, eq, float(-V), mul)
+    tt(ids(4), ids(2), ids(3), add)
+    for j, k in ((0, 0), (1, 4)):
+        op("y", lambda: g.sync.dma_start(T["id"][j:j + 1, :], T.ids[0:1, M * k:M * k + M]), ("ids%d" % k,), ("id%d" % j,), sem="did", inc=16, total=32)
+
+    Bk = ("Bz", "Bl", "Bh0", "Bh1")
+    pick("k0", 0, M, "B", off[1], "k0", Bk)
+    product(0, "k0", False)
+    pick("k1", 0, M, "B", off[2], "k1", Bk)
+    product(1, "k1", True)
+    cp(o("yo0"), o("ps0", 0, M))
+    act(o("yo1"), o("ps1", 0, M))
+    dma("y", (("y0",), T.y[:, 0:M]), o("yo0"), "dy0")
+    dma("s", (("y1",), T.y[:, M:2 * M]), o("yo1"), "dy1")
+    for sem, c in count.items():
+        if know["p"].get(sem, 0) < c:
+            g.wait_ge(T.sem[sem], c)

@@ -28,28 +28,28 @@ def _pool(buf, dtype, **widths):
 
 
 _add(_I, ci=40)
-_add(_F, cc=24, ones=1024, iot=1024, ctab=768, idw=1472, c1c=N2, c2a=N2, c2c=N2, ctw=TN, f16=N2, m16=N2, rmk=N2)
-_add(_I, st0=10, bt0=10, stA=10, nxr=768, nxB=768, ai0=V, s0i=10, pkw=32)
-_add(_F, n1r=V, Rr=V, nxa=V, Ra=V, mk0=V, cn0=V, pl5=V, pl0=V)
+_add(_F, cc=28, oh=16, ones=1024, iot=1024, ctab=768, c1c=N1, c2a=N2, c2b=N2, c2c=N2, c2g=N2, f16=N2, m16=N2, rmk=N2)
+_add(_I, st0=10, bt0=10, stA=10, nxr=768, nxB=768, nxm=768, ai0=V, pkw=32)
+_add(_F, n1r=V, nxa=V, Rr=V, Ra=V, pl5=V, pl0=V, S0=800, S0t=800)
 _add(_U, offe=10, offR=10, offS=10, off0=10, offi=16, offj=10)
-_add(_F, zd0=(10, 32), zt0=(10, 32), za0=(10, 4), zb0=(10, 2), S0=800, S0t=800)
-_add(_I, m1=15, ai1=N1, s1i=25, f3w=15)
-_add(_F, nxT=800, nxm=768, nxn=768, t1=N1, pl1=N1, mk1=N1, cn1=N1)
+_add(_I, m1=15, f3w=15)
+_add(_F, nxT=800, nxn=768, t1=N1, pl1a=N1, pl1=N1, S1=1792, S1t=992)
 _add(_U, offE=26, offG=26, off1=26, off2=30, offc=16, offd=16)
-_add(_F, zd1=(25, 32), zt1=(25, 32), za1=(25, 4), zb1=(25, 2), S1=1792, S1t=992)
-_add(_I, m2=15, idr=M)
-_add(_F, PT=1472, PS=1472, pm=N2, P2a=N2, P2=N2, S2=1504, S2t=512, idg=M, ids=6 * M, yo0=M, yo1=M)
-_add(_U, offg2=32, offc2=32, offP=32, offF=64)
-_pool("pooli", _I, i0=50, s0h=10, s0k=10, pwa=15, pwb=10, xr=25, x2=25, x3=25, x4=25, xlo=25, xhi=25, g1=25, s1h=25, s1k=25,
-      f3s=16, sga=15, sgb=16, c1a=15, c1b=16, g2=31, h2=31, pwi=31, p2h=31, p2k=31)
-_pool("poolf", _F, e0=60, xiv=25, xp=25, xpp=25, GC=25, g1f=25, iv2=31, tr2=31, TC=31, gf2=31, ga=64)
+for _f, _k in (("0", 10), ("1", 25)):
+    _add(_F, **{"mk" + _f: 16 * _k, "cn" + _f: 16 * _k, "zd" + _f: (_k, 32), "zt" + _f: (_k, 32), "za" + _f: (_k, 4), "zb" + _f: (_k, 2)})
+_add(_I, m2=15)
+_add(_F, PT=1472, PS=1472, pm=N2, rs=N2, S2=1504, S2t=512, gida=528, gidb=528, idt=2 * M, yo0=M, yo1=M)
+_add(_U, offg2=32, offga=34, offgb=34, offc2=34, offP=32, offF=64)
+_pool("pooli", _I, i0=50, si0=10, si1=25, h0=10, k0=10, h1=25, k1=25, pwa=15, pwb=10, xr=25, x2=25, x3=25, x4=25, xlo=25, xhi=25, g1=25,
+      f3s=16, sga=15, sgb=16, c1a=15, c1b=16, g2=31, h2=31, r2=31, pwi=31, hp=31, kp=31)
+_pool("poolf", _F, e0=60, eR=10, xiv=25, xp=25, xpp=25, GC=25, g1f=25, iv2=31, tr2=31, TC=31, gf2=31, u2=31, ga=64)
 _add("bfloat16", xt=4 * (ZC + TN), wt=3072)
-for _n, _w in (("x", ZC + TN), ("w", 768), ("w0", V), ("sl1", REM), ("A", N1 + TN), ("sl2", 2 * REM), ("B", BW),
-               ("k0", M), ("k1", M), ("k2", M)):
+for _n, _w in (("x", ZC + TN), ("w", 768), ("w0", V), ("sl1", REM), ("A", N1 + TN), ("sl2", 2 * REM),
+               ("B", BW), ("n2", 528), ("p0", M), ("p1", M), ("p2", M)):
     SCRATCH[_n + "q"] = ("sbuf", [128, _w], _C)
     SCRATCH[_n + "s"] = ("sbuf", [128, _w], _S)
-SCRATCH["ps0"] = ("psum", [128, 512], _F)
-SCRATCH["ps1"] = ("psum", [128, 512], _F)
+SCRATCH["ps_0"] = ("psum", [128, 512], _F)
+SCRATCH["ps_1"] = ("psum", [128, 512], _F)
 
 SEMAPHORES = ["qv", "qs", "qp", "qk", "dst0", "dbt0", "dnx", "dstA", "dx", "dw", "did", "dy0", "dy1", "am1", "ac1", "am2", "ac2", "loc"]
 
@@ -59,18 +59,19 @@ shr, band = AluOpType.arith_shift_right, AluOpType.bitwise_and
 Copy, Ident = ActivationFunctionType.Copy, ActivationFunctionType.Identity
 
 
+def pos(a, q):
+    return q if q < a else q - 1
+
+
 def rank_program(g, core, T, topo):
     me = T.rank_of(core)
     if me is None:
         return
     others = [(me + 1 + k) % N for k in range(N - 1)]
 
-    def pos(a, q):
-        return q if q < a else q - 1
-
     eng = {"v": g.vector, "s": g.scalar, "p": g, "k": g.tensor, "y": g.sync}
     know = {q: {} for q in eng}
-    count, wr, rd = {}, {}, {}
+    count, wr, rd = {"loc": 0}, {}, {}
 
     def need(q, evs):
         for sem, val, snap in sorted(evs, key=lambda e: -len(e[2])):
@@ -112,14 +113,20 @@ def rank_program(g, core, T, topo):
             lo, hi = at + (lo or 0), at + (w if hi is None else hi)
         return (keys, T[name][ps, slice(lo, hi, st)])
 
+    def h(name, a, b, f):
+        return o(name, a, b, k=name + "." + f)
+
     def o3(name, lo, hi, k=None):
         return ((k or name,), T[name][:, :, lo:hi])
 
-    def ci(j, p=None):
-        return o("ci", j, j + 1, k="ci%d" % j, p=p)
+    def ci(j):
+        return o("ci", j, j + 1, k="ci%d" % j)
 
     def cc(j):
         return o("cc", j, j + 1, k="cc%d" % j)
+
+    def oh(j):
+        return o("oh", j, j + 1)
 
     def ind(win, off):
         return (win[0] + off[0], win[1].indirect(off[1]))
@@ -150,11 +157,20 @@ def rank_program(g, core, T, topo):
     def tr(out, in_):
         op("v", lambda: g.vector.transpose(out[1], in_[1]), in_[0], out[0])
 
-    def act(out, in_, f=Copy, more=(), **kw):
-        op("s", lambda: g.scalar.activation(out[1], in_[1], f, **kw), in_[0] + tuple(more), out[0])
+    def act(out, in_, f=Copy, scale=None, bias=None):
+        kw, rk = {}, ()
+        for n, v in (("scale", scale), ("bias", bias)):
+            if isinstance(v, tuple):
+                rk, v = rk + v[0], v[1]
+            if v is not None:
+                kw[n] = v
+        op("s", lambda: g.scalar.activation(out[1], in_[1], f, **kw), in_[0] + rk, out[0])
 
     def scatter(win, off, in_):
         op("v", lambda: g.vector.tensor_copy(win[1].indirect(off[1]), in_[1]), win[0] + off[0] + in_[0], win[0])
+
+    def bcast(out, src):
+        op("p", lambda: g.partition_broadcast(T[out][:], T[src][0:1, :], 128), (src,), (out,))
 
     def pick(outn, lo, hi, winn, off, key, wkeys):
         op("v", lambda: g.vector.tensor_copy(T[outn + "q"][:, lo:hi].bitcast(dt.uint32), T[winn + "q"][:].bitcast(dt.uint32).indirect(off[1])),
@@ -173,17 +189,17 @@ def rank_program(g, core, T, topo):
                 rid, pid, _ = topo.addr(c)
                 m = sum(1 << e for e in topo.engines(core, c)[k::4])
                 trs.append(RemoteDMATransfer(dst_ids=[DstId(rid=rid, pnc=pid)], dma_engine_mask=m, remote_sem=T.sem[rsem], src=src(q), dst=dst(q)))
-            g.remote_dma_fused(trs, local_sem=T.sem["loc"])
+            g.remote_dma_fused(trs, local_sem=T.sem.loc)
             c = T.cores[others[4]]
             rid, pid, _ = topo.addr(c)
-            g.remote_dma(dst(others[4]), src(others[4]), T.sem[rsem], T.sem["loc"], pid, rid, topo.mask(core, c))
+            g.remote_dma(dst(others[4]), src(others[4]), T.sem[rsem], T.sem.loc, pid, rid, topo.mask(core, c))
         op("p", call, reads, (), sem=None)
-        count["loc"] = count.get("loc", 0) + 16
+        count["loc"] += 16
 
-    def fan_numbers(name, key, land, rsem):
-        fan((key,), lambda q: T[name][:, 3 * pos(me, q):3 * pos(me, q) + 3], lambda q: T[land][:, 3 * pos(q, me):3 * pos(q, me) + 3], rsem)
+    def lists(name, land, rsem):
+        fan((name,), lambda q: T[name][:, 3 * pos(me, q):3 * pos(me, q) + 3], lambda q: T[land][:, 3 * pos(q, me):3 * pos(q, me) + 3], rsem)
 
-    def fan_columns(name, land, at, w, rsem):
+    def columns(name, land, at, w, rsem):
         def src(n, q):
             return T[n][:, w * pos(me, q):w * pos(me, q) + w]
 
@@ -207,144 +223,137 @@ def rank_program(g, core, T, topo):
     dma("y", o("nxr", p=(0, 1)), ((), T.nx[:]), "dnx")
     dma("y", o("xt", 4 * ZC, 4 * (ZC + TN), k="xtx"), ((), T.x[:]), "dx")
     for k in range(8):
-        dma("ys"[k % 2], o("stA", p=(16 * k, 16 * k + 16), k="stA%d" % k), ((), T.st[:]), "dstA", 128)
+        dma("y", o("stA", p=(16 * k, 16 * k + 16), k="stA%d" % k), ((), T.st[:]), "dstA", 128)
     stA = (tuple("stA%d" % k for k in range(8)), T.stA[:])
+    dma("y", o("wt"), ((), T.w[:]), "dw")
 
     def iota(out, pattern, base=0, mult=0):
         op("p", lambda: g.iota(out[1], pattern, base, mult, allow_small_or_imprecise_dtypes=True), (), out[0])
     wc = o("ci", 8, 40, k="wc")
     iota(ci(0), [[1, 1]], 0, 1)
     iota(wc, [[16, 32]])
-    iota(o("ctab"), [[1, 8], [0, 2], [8, 48]])
     iota(o("iot", 0, 512, k="iota"), [[1, 512]])
-    iot2 = ("iota", "iotb")
+    iota(o("ctab"), [[1, 8], [0, 2], [8, 48]])
+    iot = o("iot", k=("iota", "iotb"))
 
-    JF, P16, OD, DQ, BASE, F3, SG, C1, S1R, CF, R16, R256, RSS, SG1, C128 = range(15)
-    X1, X2, X3 = cc(20), cc(21), cc(22)
+    JF, P16, OD, BASE, TA, TB, R16, R256, RSS, C32 = range(10)
+    X1, X2, X3 = cc(24), cc(25), cc(26)
+    F3, SG, C1, S1R = 8, 9, 10, 11
     ms(o("offe"), 0)
     ms(o("offR"), 0)
     ts(ci(1), ci(0), 31, band)
     ts(ci(2), ci(0), 15, band)
+    ms(o("ones", 0, V, k="ones0"), 1.0)
     cp(cc(JF), ci(1))
     cp(cc(P16), ci(2))
-    ts(o("e0", 50, 60, k="wi"), o("ci", 8, 18, k="wc"), cc(P16), add, 1.0, add)
-    ts(cc(OD), cc(JF), 16.0, ge, 16.0, mul)
-    ts(X1, cc(JF), 7.0, ge, 1000.0, mul)
-    ts(X2, cc(JF), float(me), gt, -48.0, mul)
-    ts(X3, cc(JF), float(me), eq, float(REM - CAPP * me), mul)
-    tt(cc(DQ), cc(JF), X1, add)
-    tt(X2, X2, X3, add)
-    ts(X3, cc(JF), 6.0, eq, 256.0, mul)
-    ts(X1, cc(JF), 48.0, mul, -1.0, add)
-    tt(X2, X2, X3, add)
-    tt(cc(BASE), X1, X2, add)
-    for k, r in ((F3, 8.0), (SG, 9.0), (C1, 10.0), (S1R, 11.0)):
-        ts(cc(k), cc(P16), r, eq)
-    ms(o("ones"), 1.0)
     ms(o("S0"), 0.0)
-    ms(o("xt", 0, 4 * ZC, k="xtz"), 0.0)
 
     def i0(j):
         return o("i0", 10 * j, 10 * j + 10, k="i0%d" % j, p=P)
 
     def e0(j):
         return o("e0", 10 * j, 10 * j + 10, k="e0%d" % j, p=P)
-    ts(i0(0), o("bt0", p=P), 1, band)
     ts(i0(1), o("st0", p=P), 3, shr)
-    ts(i0(2), o("bt0", p=P), 1, shr)
     ts(e0(1), o("st0", p=P), 96.0, mul)
-    ts(e0(2), i0(0), 48.0, mul)
+    ts(i0(0), o("bt0", p=P), 1, band)
     ts(e0(3), i0(1), -767.0, mul)
-    tt(e0(4), e0(1), e0(2), add)
-    ts(e0(0), i0(2), 256.0, mul)
-    tt(e0(4), e0(4), e0(3), add)
+    ts(e0(2), i0(0), 48.0, mul)
+    tt(e0(4), e0(1), e0(3), add)
+    ts(i0(2), o("bt0", p=P), 1, shr)
+    tt(e0(4), e0(4), e0(2), add)
+    ts(o("eR"), o("ci", 8, 18, k="wc"), cc(P16), add, 1.0, add)
     cp(o("offe", p=P), e0(4))
-    tt(e0(0), e0(0), o("e0", 50, 60, k="wi", p=P), add)
-    cp(o("offR", p=P), e0(0))
+    ts(e0(0), i0(2), 256.0, mul)
     cp(o("n1r"), ind(o("nxr"), o("offe")))
-    op("p", lambda: g.partition_broadcast(T.nxa[:], T.n1r[0:1, :], 128), ("n1r",), ("nxa",))
+    bcast("nxa", "n1r")
+    tt(e0(0), e0(0), o("eR", p=P), add)
+    ts(X2, cc(JF), float(me), gt, -48.0, mul)
+    ts(X3, cc(JF), float(me), eq, float(REM - CAPP * me), mul)
+    cp(o("offR", p=P), e0(0))
+    ts(X1, cc(JF), 48.0, mul, -1.0, add)
+    tt(X2, X2, X3, add)
     cp(o("Rr"), ind(o("iot", 0, 512, k="iota"), o("offR")))
-    op("p", lambda: g.partition_broadcast(T.Ra[:], T.Rr[0:1, :], 128), ("Rr",), ("Ra",))
-    op("p", lambda: g.partition_broadcast(T.nxB[:], T.nxr[0:1, :], 128), ("nxr",), ("nxB",))
-    ts(o("offS"), stA, float(ZC), add)
-    act(o("nxn"), o("ctab"), more=("cc%d" % C1,), scale=cc(C1)[1])
+    bcast("Ra", "Rr")
+    bcast("nxB", "nxr")
+    ts(X3, cc(JF), 6.0, eq, 256.0, mul)
+    tt(X1, X1, X2, add)
+    ts(cc(OD), cc(JF), 16.0, ge, 16.0, mul)
+    tt(cc(BASE), X1, X3, add)
     act(o("pl5"), o("nxa"), Ident, scale=512.0, bias=512.0)
 
-    def spread(src, s, off):
-        ts(o(s + "h"), src, 4, shr)
-        ts(o(s + "k"), o(s + "h"), 16.0, mul, cc(OD), add)
-        tt(o(s + "h"), src, o(s + "k"), add)
-        cp(off, o(s + "h"))
+    def spread(src, f, off):
+        ts(o("h" + f), src, 4, shr)
+        ts(o("k" + f), o("h" + f), 16.0, mul, cc(OD), add)
+        tt(o("h" + f), src, o("k" + f), add)
+        cp(off, o("h" + f))
 
     def place(f, nk, src, off, meanwhile):
-        zd, zt, za, zb, s = "zd" + f, "zt" + f, "za" + f, "zb" + f, "s" + f
-        ts(o("ai" + f), src, -191.5, add, 1.0 / TN, mul)
-        ts(o("mk" + f), o("ai" + f), cc(DQ), eq)
-        scan(o("cn" + f), o("ones", 0, 16 * nk), o("mk" + f), cc(BASE))
+        zd, zt, za, zb = "zd" + f, "zt" + f, "za" + f, "zb" + f
+        ts(o("mk" + f), src, cc(JF), eq)
+        scan(o("cn" + f), o("ones", 0, 16 * nk, k=("ones0",) if f == "0" else ("ones0", "ones1")), o("mk" + f), cc(BASE))
         tt(o3(zd, 0, 16, zd + "l"), o("mk" + f), o("cn" + f), mul)
         act(o3(zd, 16, 32, zd + "h"), o3(zd, 0, 16, zd + "l"))
         meanwhile()
         op("v", lambda: g.vector.transpose(T[zt][:], T[zd][:]), (zd + "l", zd + "h"), (zt,))
         tt(o3(za, 0, 4), o3(zt, 0, 4), o3(zt, 4, 8), add)
         tt(o3(zb, 0, 2), o3(za, 0, 2), o3(za, 2, 4), add)
-        op("v", lambda: g.vector.tensor_tensor(T[s + "i"][:], T[zb][:, :, 0], T[zb][:, :, 1], add), (zb,), (s + "i",))
-        spread(o(s + "i"), s, off)
+        si = o("si" + f)
+        op("v", lambda: g.vector.tensor_tensor(si[1], T[zb][:, :, 0], T[zb][:, :, 1], add), (zb,), si[0])
+        spread(si, f, off)
 
     def row(out, name, lo, hi, j, key):
         tt(out, o(name, lo + j, hi, 32, k=key), o(name, lo + j + 16, hi, 32, k=key), add)
 
-    def during0():
-        quant("x", 0, ZC + TN, "xt", 0, ZC + TN, ("xtx", "xtz"), "x")
-        tt(o("pl0"), o("pl5"), o("Ra"), add)
-    place("0", 10, o("nxa"), o("off0"), during0)
+    ts(o("ai0"), o("nxa"), -191.5, add, 1.0 / TN, mul)
+    place("0", 10, o("ai0"), o("off0"), lambda: tt(o("pl0"), o("pl5"), o("Ra"), add))
     scatter(o("S0"), o("off0"), o("pl0"))
-    pick("w0", 0, V, "x", o("offS"), "w0", ("x",))
     tr(o("S0t", 0, 480, k="S0ta"), o("S0", 0, 480))
-    row(o("pkw", 0, 15, k="pkwr"), "S0t", 0, 480, 0, "S0ta")
-    fan_numbers("pkw", "pkwr", "m1", "am1")
-    ts(o("pwa"), o("pkw", 0, 15, k="pkwr"), 255, band)
+    row(o("pkw", 0, 15, k="pkw"), "S0t", 0, 480, 0, "S0ta")
+    lists("pkw", "m1", "am1")
+    ms(o("xt", 0, 4 * ZC, k="xtz"), 0.0)
+    ts(o("pwa"), o("pkw", 0, 15, k="pkw"), 255, band)
+    ts(o("offS"), stA, float(ZC), add)
+    quant("x", 0, ZC + TN, "xt", 0, ZC + TN, ("xtx", "xtz"), "x")
     ts(o("offi", 0, 15), o("pwa"), -1.0, add, 0.0, mx)
+    pick("w0", 0, V, "x", o("offS"), "w0", ("x",))
     pick("sl1", 0, REM, "w0", o("offi", 0, 15), "sl1", ("w0",))
-    fan_columns("sl1", "A", 0, CAPP, "ac1")
-    dma("s", o("wt"), ((), T.w[:]), "dw")
-    tr(o("S0t", 480, 800, k="S0tb"), o("S0", 480, 800))
-    row(o("pkw", 16, 26, k="pkws"), "S0t", 480, 800, 0, "S0tb")
-    ts(o("pwb"), o("pkw", 16, 26, k="pkws"), 255, band)
-    ts(o("offj"), o("pwb"), -1.0, add, 0.0, mx)
-    pick("A", REM, N1, "w0", o("offj"), "Ah", ("w0",))
-
+    columns("sl1", "A", 0, CAPP, "ac1")
+    ts(o("oh"), o("iot", 0, 16, k="iota"), cc(P16), eq)
+    act(o("nxn"), o("ctab"), scale=oh(C1))
     act(o("iot", 512, 1024, k="iotb"), o("iot", 0, 512, k="iota"), Ident, bias=512.0)
-    act(o("idw", 0, GT, k="idwa"), o("iot", 0, GT, k=iot2), more=("cc%d" % F3,), scale=cc(F3)[1])
-    act(o("c1c"), o("iot", 0, N2, k="iota"), Ident, more=("cc%d" % SG,), scale=cc(SG)[1], bias=cc(SG)[1])
-    act(o("S1", 0, 992), o("iot", 0, 992, k=iot2), scale=0.0)
-    act(o("PT", 0, 992), o("iot", 0, 992, k=iot2), scale=0.0)
-    act(o("PT", 992, 1472), o("iot", 0, 480, k="iota"), scale=0.0)
-    act(o("S2", 0, 512), o("iot", 0, 512, k="iota"), scale=0.0)
-    act(o("PS", GT, GT + N2, k="PSb"), o("iot", 0, N2, k="iota"), Ident, bias=256.0)
-    ts(X1, cc(P16), 8.0, lt)
-    ts(X2, cc(F3), 1024.0, mul)
-    tt(cc(CF), X1, X2, add)
-    ts(o("nxm"), o("nxB"), cc(CF), mul)
+    act(o("c1c"), o("iot", 0, N1, k="iota"), Ident, scale=oh(SG), bias=oh(SG))
+    act(o("S1", 0, 992), o("iot", 0, 992, k=("iota", "iotb")), scale=0.0)
+    tr(o("S0t", 480, 800, k="S0tb"), o("S0", 480, 800))
+    ts(X1, cc(P16), 8.0, lt, 1.0 / TN, mul)
+    ts(X2, oh(F3), 1024.0, mul)
+    row(o("pkw", 16, 26, k="pkws"), "S0t", 480, 800, 0, "S0tb")
+    pkws = o("pkw", 16, 26, k="pkws")
+    ts(cc(TB), X1, -191.5, mul)
+    tt(cc(TA), X1, X2, add)
+    ts(o("pwb"), pkws, 255, band)
+    ts(o("nxm"), o("nxB"), cc(TA), mul, cc(TB), add)
+    ts(o("offj"), o("pwb"), -1.0, add, 0.0, mx)
     tt(o("nxT", 0, 768, k="nxTa"), o("nxm"), o("nxn"), add)
-    ms(o("nxT", 768, 800, k="nxTz"), 6.5 * TN - 1)
-    ms(o("idw", GT, 1472, k="idwz"), 0.0)
+    pick("A", REM, N1, "w0", o("offj"), "Ah", ("w0",))
+    ms(o("nxT", 768, 800, k="nxTz"), 6.0)
+    ms(o("ones", V, 1024, k="ones1"), 1.0)
     for q in others:
         ms(o("GC", 3 * pos(me, q), 3 * pos(me, q) + 3), float(V * q))
     ms(o("GC", 15, 25), float(V * me))
-    idw = o("idw", 0, 1472, k=("idwa", "idwz"))
     quant("A", N1, N1 + TN, "xt", ZC, ZC + TN, ("xtx",), "Ax")
     iota(o("c2a", 0, REM, k="c2aa"), [[32, 15], [1, 16]], BN0)
     iota(o("c2a", REM, N2, k="c2ab"), [[1, M]], BH0)
     iota(o("f16"), [[0, 31], [1, 16]])
 
-    ts(o("xr", 0, 15), o("m1"), 8, shr)
-    ts(o("xr", 15, 25), o("pkw", 16, 26, k="pkws"), 8, shr)
-    ts(o("g1", 0, 15), o("m1"), 255, band)
-    ts(o("g1", 15, 25), o("pkw", 16, 26, k="pkws"), 255, band)
-    ts(o("x2"), o("xr"), float(-(2 * TN * me + 2)), add)
-    tt(o("g1f"), o("g1"), o("GC"), add)
+    ts(h("xr", 15, 25, "s"), pkws, 8, shr)
+    ts(h("g1", 15, 25, "s"), pkws, 255, band)
+    ts(h("xr", 0, 15, "r"), o("m1"), 8, shr)
+    ts(h("g1", 0, 15, "r"), o("m1"), 255, band)
+    ts(o("x2"), o("xr", k=("xr.s", "xr.r")), float(-(2 * TN * me + 2)), add)
+    tt(o("g1f"), o("g1", k=("g1.s", "g1.r")), o("GC"), add)
     ts(o("xiv"), o("x2"), 0.0, lt, 8000.0, mul)
     cp(o("offG", 0, 25), o("g1f"))
+    act(o("t1"), ind(iot, o("offG", 0, 25)), scale=oh(F3))
     tt(o("x3"), o("x2"), o("xiv"), add)
     ts(o("x4"), o("x3"), 783.0, mn)
     ts(o("xlo"), o("x4"), 15, band)
@@ -352,96 +361,100 @@ def rank_program(g, core, T, topo):
     ts(o("xp"), o("xlo"), 48.0, mul)
     tt(o("xpp"), o("xp"), o("xhi"), add)
     cp(o("offE", 0, 25), o("xpp"))
-    tt(o("t1"), ind(idw, o("offG", 0, 25)), o("c1c", 0, N1), add)
-    tt(o("pl1"), ind(o("nxT", 0, 800, k=("nxTa", "nxTz")), o("offE", 0, 25)), o("t1"), add)
-    place("1", 25, o("pl1"), o("off1", 0, 25), lambda: None)
+    tt(o("pl1a"), ind(o("nxT", 0, 800, k=("nxTa", "nxTz")), o("offE", 0, 25)), o("c1c"), add)
+    place("1", 25, o("pl1a"), o("off1", 0, 25), lambda: tt(o("pl1"), o("pl1a"), o("t1"), add))
     scatter(o("S1"), o("off1", 0, 25), o("pl1"))
     tr(o("S1t", 0, 480, k="S1ta"), o("S1", 0, 480))
     row(o("f3w"), "S1t", 0, 480, 8, "S1ta")
-    fan_numbers("f3w", "f3w", "m2", "am2")
-    row(o("sga"), "S1t", 0, 480, 9, "S1ta")
-    row(o("c1a"), "S1t", 0, 480, 10, "S1ta")
+    lists("f3w", "m2", "am2")
+    row(o("sga"), "S1t", 0, 480, SG, "S1ta")
+    row(o("c1a"), "S1t", 0, 480, C1, "S1ta")
     ts(o("off2", 0, 30, 2), o("sga"), -1.0, add, 0.0, mx)
     ts(o("off2", 1, 30, 2), o("c1a"), float(N1), add)
     pick("sl2", 0, 2 * REM, "A", o("off2"), "sl2", ("Al", "Ah", "Ax"))
-    fan_columns("sl2", "B", BN0, 2 * CAPP, "ac2")
+    columns("sl2", "B", BN0, 2 * CAPP, "ac2")
     tr(o("S1t", 480, 992, k="S1tb"), o("S1", 480, 992))
+    ts(cc(C32), oh(F3), 32.0, mul)
+    ts(cc(R16), oh(S1R), 16.0, mul)
     row(o("f3s"), "S1t", 480, 992, 8, "S1tb")
-    row(o("sgb"), "S1t", 480, 992, 9, "S1tb")
-    row(o("c1b"), "S1t", 480, 992, 10, "S1tb")
+    row(o("sgb"), "S1t", 480, 992, SG, "S1tb")
+    row(o("c1b"), "S1t", 480, 992, C1, "S1tb")
+    ts(cc(R256), oh(S1R), 256.0, mul)
     ts(o("offc"), o("sgb"), -1.0, add, 0.0, mx)
     ts(o("offd"), o("c1b"), float(ZC), add)
+    tt(cc(RSS), oh(SG), oh(S1R), add)
     pick("B", BH0, BH1, "A", o("offc"), "Bh0", ("Al", "Ah", "Ax"))
     pick("B", BH1, BW, "x", o("offd"), "Bh1", ("x",))
 
-    ts(cc(C128), cc(C1), float(ZC), mul)
-    ts(cc(R16), cc(S1R), 16.0, mul)
-    ts(cc(R256), cc(S1R), 256.0, mul)
-    tt(cc(RSS), cc(SG), cc(S1R), add)
-    act(o("ctw"), o("iot", 0, TN, k="iota"), Ident, more=("cc%d" % C1, "cc%d" % C128), scale=cc(C1)[1], bias=cc(C128)[1])
-    ts(o("c2c", 0, REM), o("c2a", 0, REM, k="c2aa"), cc(R16), add, cc(RSS), mul)
-    ts(o("c2c", REM, N2), o("c2a", REM, N2, k="c2ab"), cc(R256), add, cc(RSS), mul)
+    act(o("PT", 0, 992), o("iot", 0, 992, k=("iota", "iotb")), scale=0.0)
+    act(o("PT", 992, 1472), o("iot", 0, 480, k="iota"), scale=0.0)
+    act(o("c2g"), o("iot", 0, N2, k="iota"), Ident, scale=oh(F3), bias=cc(C32))
+    act(o("PS", GT, GT + N2, k="PS.b"), o("iot", 0, N2, k="iota"), Ident, bias=256.0)
+    act(o("S2", 0, 512), o("iot", 0, 512, k="iota"), scale=0.0)
+    ts(o("TC"), o("ci", 8, 39, k="wc"), cc(P16), add, float(GT), add)
+    for n in ("offga", "offgb", "offc2"):
+        ms(o(n, 0, 2, k=n + ".z"), 0)
     ts(o("m16"), o("f16"), cc(P16), eq)
     ts(o("rmk"), o("f16"), 0.0, ne)
-    ts(o("TC"), o("ci", 8, 39, k="wc"), cc(P16), add, float(GT), add)
+    ts(o("c2b", 0, REM), o("c2a", 0, REM, k="c2aa"), cc(R16), add, cc(RSS), mul)
+    ts(o("c2b", REM, N2), o("c2a", REM, N2, k="c2ab"), cc(R256), add, cc(RSS), mul)
+    tt(o("c2c"), o("c2b"), o("c2g"), add)
     quant("B", 0, ZC, "xt", 0, ZC, ("xtz",), "Bz")
     quant("w", 0, 384, "wt", 0, 384, ("wt",), "wa")
     quant("w", 384, 768, "wt", 384, 768, ("wt",), "wb")
+    ts(h("g2", 15, 31, "s"), o("f3s"), 1023, band)
+    ts(h("h2", 15, 31, "s"), o("f3s"), 10, shr)
 
-    ts(o("g2", 15, 31), o("f3s"), 1023, band)
-    ts(o("h2", 15, 31), o("f3s"), 10, shr)
-    ts(o("g2", 0, 15), o("m2"), 1023, band)
-    ts(o("h2", 0, 15), o("m2"), 10, shr)
-    ts(o("iv2"), o("g2"), 0.0, eq)
-    ts(o("offc2", 0, 31), o("h2"), float(-TN * me), add, 0.0, mx)
+    ts(h("g2", 0, 15, "r"), o("m2"), 1023, band)
+    ts(h("h2", 0, 15, "r"), o("m2"), 10, shr)
+    g2, h2 = o("g2", k=("g2.s", "g2.r")), o("h2", k=("h2.s", "h2.r"))
+    ts(o("iv2"), g2, 0.0, eq)
+    ts(o("r2"), g2, -(V + 1) / 2.0, add, 1.0 / V, mul)
     tt(o("tr2"), o("iv2"), o("TC"), mul)
-    tt(o("gf2"), o("tr2"), o("g2"), add)
+    ts(o("offc2", 2, 33), h2, float(ZC - TN * me), add, 0.0, mx)
+    tt(o("gf2"), o("tr2"), g2, add)
+    ts(o("u2"), o("r2"), float(-V), mul)
     cp(o("offg2", 0, 31), o("gf2"))
-    og = o("offg2", 0, 31)
-    scatter(o("PT"), og, o("ones", 0, N2))
-    tt(o("P2a"), ind(idw, og), o("c2c"), add)
-    scan(o("PS", 0, GT, k="PSa"), o("ones", 0, GT), o("PT", 0, GT), -1.0)
-    tt(o("P2"), ind(o("ctw"), o("offc2", 0, 31)), o("P2a"), add)
-    tt(o("pm"), ind(o("PS", 0, GT + N2, k=("PSa", "PSb")), og), o("m16"), mul)
-    scan(o("P2a"), o("rmk"), o("pm"), 0.0)
-    cp(o("pwi"), o("P2a", 15, N2, 16))
-    spread(o("pwi"), "p2", o("offP", 0, 31))
-    scatter(o("S2"), o("offP", 0, 31), o("P2"))
+    ts(o("offga", 2, 33), o("r2"), 1.0, add)
+    scatter(o("PT"), o("offg2", 0, 31), o("ones", 0, N2, k=("ones0", "ones1")))
+    tt(o("u2"), o("u2"), g2, add)
+    scan(o("PS", 0, GT, k="PS.a"), o("ones", 0, GT, k=("ones0", "ones1")), o("PT", 0, GT), -1.0)
+    cp(o("offgb", 2, 33), o("u2"))
+    for n, gd in (("offga", "gida"), ("offgb", "gidb")):
+        act(o(gd), ind(iot, o(n, 0, 33, k=(n, n + ".z"))))
+    tt(o("pm"), ind(o("PS", 0, GT + N2, k=("PS.a", "PS.b")), o("offg2", 0, 31)), o("m16"), mul)
+    scan(o("rs"), o("rmk"), o("pm"), 0.0)
+    cp(o("pwi"), o("rs", 15, N2, 16))
+    spread(o("pwi"), "p", o("offP", 0, 31))
+    scatter(o("S2"), o("offP", 0, 31), o("c2c"))
+    pick("n2", 0, 528, "x", o("offc2", 0, 33, k=("offc2", "offc2.z")), "n2", ("x",))
     tr(o("S2t"), o("S2", 0, 512))
-    for k, j in enumerate((10, 9, 11, 8)):
-        row(o("ga", 16 * k, 16 * k + 16, k="ga%d" % k), "S2t", 0, 512, j, "S2t")
-        cp(o("offF", 16 * k, 16 * k + 16, k="offF%d" % k), o("ga", 16 * k, 16 * k + 16, k="ga%d" % k))
-    off = [o("offF", 16 * k, 16 * k + 16, k="offF%d" % k) for k in range(4)]
-    pick("k2", 0, M, "x", off[0], "k2", ("x",))
+    off = [h("offF", 16 * k, 16 * k + 16, "%d" % k) for k in range(3)]
+    for k, j in enumerate((F3, SG, S1R)):
+        row(h("ga", 16 * k, 16 * k + 16, "%d" % k), "S2t", 0, 512, j, "S2t")
+    for k in range(3):
+        cp(off[k], h("ga", 16 * k, 16 * k + 16, "%d" % k))
+    pick("p2", 0, M, "n2", off[0], "p2", ("n2",))
 
-    def product(k, n, last):
+    def product(k, last):
+        n = "p%d" % k
         for oo in range(NO):
             a = 128 * (k * NO + oo)
-            op("k", lambda: g.tensor.matmul_mx(T["ps%d" % oo][:, 0:M], T.wq[:, a:a + 128], T.ws[:, a:a + 128], T[n + "q"][:], T[n + "s"][:], k == 2, last),
-               ("waq", "was", "wbq", "wbs", n + "q", n + "s"), ("ps%d" % oo,) if last else ())
-    product(2, "k2", False)
-
-    def ids(j):
-        return o("ids", M * j, M * j + M, k="ids%d" % j)
-    cp(o("idg"), ind(o("iot", k=iot2), off[3]))
-    ts(o("idr"), o("idg"), -(V + 1) / 2.0, add, 1.0 / V, mul)
-    cp(ids(0), o("idr"))
-    ts(ids(1), ids(0), float(-V), mul, -1.0, add)
-    tt(ids(2), ids(1), o("idg"), add)
-    ts(ids(3), o("idg"), 0.0, eq, float(-V), mul)
-    tt(ids(4), ids(2), ids(3), add)
-    for j, k in ((0, 0), (1, 4)):
-        op("y", lambda: g.sync.dma_start(T["id"][j:j + 1, :], T.ids[0:1, M * k:M * k + M]), ("ids%d" % k,), ("id%d" % j,), sem="did", inc=16, total=32)
-
+            op("k", lambda: g.tensor.matmul_mx(T["ps_%d" % oo][:, 0:M], T.wq[:, a:a + 128], T.ws[:, a:a + 128], T[n + "q"][:], T[n + "s"][:], k == 2, last),
+               ("waq", "was", "wbq", "wbs", n + "q", n + "s"), ("ps_%d" % oo,) if last else ())
+    product(2, False)
     Bk = ("Bz", "Bl", "Bh0", "Bh1")
-    pick("k0", 0, M, "B", off[1], "k0", Bk)
-    product(0, "k0", False)
-    pick("k1", 0, M, "B", off[2], "k1", Bk)
-    product(1, "k1", True)
-    cp(o("yo0"), o("ps0", 0, M))
-    act(o("yo1"), o("ps1", 0, M))
+    pick("p0", 0, M, "B", off[1], "p0", Bk)
+    product(0, False)
+    pick("p1", 0, M, "B", off[2], "p1", Bk)
+    product(1, True)
+    cp(o("yo0"), o("ps_0", 0, M))
+    act(o("yo1"), o("ps_1", 0, M))
     dma("y", (("y0",), T.y[:, 0:M]), o("yo0"), "dy0")
     dma("s", (("y1",), T.y[:, M:2 * M]), o("yo1"), "dy1")
+    for j, gd in ((0, "gida"), (1, "gidb")):
+        act(h("idt", M * j, M * j + M, "%d" % j), ind(o(gd), off[0]), Ident, bias=-1.0)
+    op("y", lambda: g.sync.dma_start(T["id"][:], T.idt[0:1, :]), ("idt.0", "idt.1"), ("ido",), sem="did", inc=16)
     for sem, c in count.items():
         if know["p"].get(sem, 0) < c:
             g.wait_ge(T.sem[sem], c)

@@ -6,9 +6,11 @@ REM = CAPP * (N - 1)
 N1 = REM + V
 N2 = REM + M
 GT = N * V + 1
+GB = 11
 ZC = 128
 BN0, BH0, BH1 = ZC, ZC + 2 * REM, ZC + 2 * REM + M
 BW = BH1 + M
+W1, H1 = N1 + 16, (N1 + 16) // 2
 
 _F, _I, _U, _C, _S = "float32", "int32", "uint16", "float8_e4m3fn_x4", "uint8"
 SCRATCH, POOL = {}, {}
@@ -28,30 +30,31 @@ def _pool(buf, dtype, **widths):
 
 
 _add(_I, ci=40)
-_add(_F, cc=28, oh=16, ones=1024, iot=1024, ctab=768, c1c=N1, c2a=N2, c2b=N2, c2c=N2, c2g=N2, f16=N2, m16=N2, rmk=N2)
-_add(_I, st0=10, bt0=10, stA=10, nxr=768, nxB=768, nxm=768, ai0=V, pkw=32)
-_add(_F, n1r=V, nxa=V, Rr=V, Ra=V, pl5=V, pl0=V, S0=800, S0t=800)
-_add(_U, offe=10, offR=10, offS=10, off0=10, offi=16, offj=10)
-_add(_I, m1=15, f3w=15)
-_add(_F, nxT=800, nxn=768, t1=N1, pl1a=N1, pl1=N1, S1=1792, S1t=992)
-_add(_U, offE=26, offG=26, off1=26, off2=30, offc=16, offd=16)
-for _f, _k in (("0", 10), ("1", 25)):
-    _add(_F, **{"mk" + _f: 16 * _k, "cn" + _f: 16 * _k, "zd" + _f: (_k, 32), "zt" + _f: (_k, 32), "za" + _f: (_k, 4), "zb" + _f: (_k, 2)})
+_add(_F, cc=40, oh=16, ones=1024, iot=2304, ctab=768, nxn=768, gidT=1024)
+_add(_I, st0=10, bt0=10, stA=10, nxr=768, nxA=48, ai0=V, pkw=32)
+_add(_F, n1r=V, nxa=V, Rr=V, Ra=V, pl5=V, pl0=V, S0=800, S0t=(25, 32))
+_add(_U, offe=10, offR=10, offS=10, off0=10, offi=16, offj=10, nxo=48)
+_add(_F, mk0=V, cn0=V, zd0=(10, 32), zt0=(10, 32), za0=(10, 4), zb0=(10, 2))
+_add(_I, m1=15, xg=(2, 26), f3w=15, rk=W1)
+_add(_F, nxT=784, c1i=H1, c1h=H1, mk1=W1, cn1=W1, zd1=(13, 32), zt1=(13, 32), za1=(13, 4), zb1=(13, 2), plG=H1, pl1=H1, S1=928, S1d=(31, 32), S1t=(31, 32),
+     sA=(2, 13), sB=(2, 13), xh=(2, 13))
+_add(_U, offE=26, offEh=14, offGh=14, off1=14, off2=30, offc=16, offd=16)
 _add(_I, m2=15)
-_add(_F, PT=1472, PS=1472, pm=N2, rs=N2, S2=1504, S2t=512, gida=528, gidb=528, idt=2 * M, yo0=M, yo1=M)
-_add(_U, offg2=32, offga=34, offgb=34, offc2=34, offP=32, offF=64)
-_pool("pooli", _I, i0=50, si0=10, si1=25, h0=10, k0=10, h1=25, k1=25, pwa=15, pwb=10, xr=25, x2=25, x3=25, x4=25, xlo=25, xhi=25, g1=25,
-      f3s=16, sga=15, sgb=16, c1a=15, c1b=16, g2=31, h2=31, r2=31, pwi=31, hp=31, kp=31)
-_pool("poolf", _F, e0=60, eR=10, xiv=25, xp=25, xpp=25, GC=25, g1f=25, iv2=31, tr2=31, TC=31, gf2=31, u2=31, ga=64)
+_add(_F, PT=1472, PS=1472, pr=512, prt=512, T2=(16, 32), c2t=(16, 32), c2h=256, S2=768, S2d=(16, 32), S2t=(16, 32), kv=96,
+     gida=512, gidb=512, idt=2 * M, yo0=M, yo1=M)
+_add(_U, offgL=16, offgO=16, offP=16, offF=64, cL=16, aL=16, bL=16, cO=18, aO=18, bO=18)
+_pool("pooli", _I, i0=50, si0=10, k0=10, h0=10, pwa=15, pwb=10, g1=26, f3r=16, f3s=16, f3p=16, sga=15, sgb=16, c1a=15, c1b=16,
+      g2L=15, g2O=16, h2L=15, h2O=16, r2L=15, r2O=16, padi=32, pad=32, GC=26)
+_pool("poolf", _F, e0=60, eR=10, si1=13, u2L=15, u2O=16, ga=64)
 _add("bfloat16", xt=4 * (ZC + TN), wt=3072)
 for _n, _w in (("x", ZC + TN), ("w", 768), ("w0", V), ("sl1", REM), ("A", N1 + TN), ("sl2", 2 * REM),
-               ("B", BW), ("n2", 528), ("p0", M), ("p1", M), ("p2", M)):
+               ("B", BW), ("n2", 512), ("p0", M), ("p1", M), ("p2", M)):
     SCRATCH[_n + "q"] = ("sbuf", [128, _w], _C)
     SCRATCH[_n + "s"] = ("sbuf", [128, _w], _S)
 SCRATCH["ps_0"] = ("psum", [128, 512], _F)
 SCRATCH["ps_1"] = ("psum", [128, 512], _F)
 
-SEMAPHORES = ["qv", "qs", "qp", "qk", "dst0", "dbt0", "dnx", "dstA", "dx", "dw", "did", "dy0", "dy1", "am1", "ac1", "am2", "ac2", "loc"]
+SEMAPHORES = ["qv", "qs", "qp", "qk", "dst0", "dbt0", "dnx", "dstA", "dnxA", "dx", "dw", "did", "dy0", "dy1", "am1", "ac1", "am2", "ac2", "loc"]
 
 add, sub, mul, mx, mn = AluOpType.add, AluOpType.subtract, AluOpType.mult, AluOpType.max, AluOpType.min
 eq, ge, gt, lt, ne = AluOpType.is_equal, AluOpType.is_ge, AluOpType.is_gt, AluOpType.is_lt, AluOpType.not_equal
@@ -116,8 +119,11 @@ def rank_program(g, core, T, topo):
     def h(name, a, b, f):
         return o(name, a, b, k=name + "." + f)
 
-    def o3(name, lo, hi, k=None):
-        return ((k or name,), T[name][:, :, lo:hi])
+    def o3(name, lo, hi, k=None, a=None, b=None):
+        return ((k or name,), T[name][:, slice(a, b), lo:hi])
+
+    def xg(j, a, b, k):
+        return ((k,), T.xg[:, j, a:b])
 
     def ci(j):
         return o("ci", j, j + 1, k="ci%d" % j)
@@ -222,9 +228,11 @@ def rank_program(g, core, T, topo):
     ms(o("nxr"), 0)
     dma("y", o("nxr", p=(0, 1)), ((), T.nx[:]), "dnx")
     dma("y", o("xt", 4 * ZC, 4 * (ZC + TN), k="xtx"), ((), T.x[:]), "dx")
-    for k in range(8):
-        dma("y", o("stA", p=(16 * k, 16 * k + 16), k="stA%d" % k), ((), T.st[:]), "dstA", 128)
+    for n, src, s_ in (("stA", T.st, "dstA"), ("nxA", T.nx, "dnxA")):
+        for k in range(8):
+            dma("y", o(n, p=(16 * k, 16 * k + 16), k=n + "%d" % k), ((), src[:]), s_, 128)
     stA = (tuple("stA%d" % k for k in range(8)), T.stA[:])
+    nxA = (tuple("nxA%d" % k for k in range(8)), T.nxA[:])
     dma("y", o("wt"), ((), T.w[:]), "dw")
 
     def iota(out, pattern, base=0, mult=0):
@@ -233,12 +241,10 @@ def rank_program(g, core, T, topo):
     iota(ci(0), [[1, 1]], 0, 1)
     iota(wc, [[16, 32]])
     iota(o("iot", 0, 512, k="iota"), [[1, 512]])
-    iota(o("ctab"), [[1, 8], [0, 2], [8, 48]])
-    iot = o("iot", k=("iota", "iotb"))
 
-    JF, P16, OD, BASE, TA, TB, R16, R256, RSS, C32 = range(10)
-    X1, X2, X3 = cc(24), cc(25), cc(26)
-    F3, SG, C1, S1R = 8, 9, 10, 11
+    IA = ("iota", "iotb")
+    (JF, P16, OD, BASE, TA, TB, EV, OV, CB, X1, X2, X3, X4, X5) = range(14)
+    F3, SG, C1 = 8, 9, 10
     ms(o("offe"), 0)
     ms(o("offR"), 0)
     ts(ci(1), ci(0), 31, band)
@@ -246,7 +252,10 @@ def rank_program(g, core, T, topo):
     ms(o("ones", 0, V, k="ones0"), 1.0)
     cp(cc(JF), ci(1))
     cp(cc(P16), ci(2))
-    ms(o("S0"), 0.0)
+    ms(o("xt", 0, 4 * ZC, k="xtz"), 0.0)
+    act(o("iot", 512, 1024, k="iotb"), o("iot", 0, 512, k="iota"), Ident, bias=512.0)
+    act(o("S0"), o("iot", 0, 800, k=IA), scale=0.0)
+    ts(o("oh"), o("iot", 0, 16, k="iota"), cc(P16), eq)
 
     def i0(j):
         return o("i0", 10 * j, 10 * j + 10, k="i0%d" % j, p=P)
@@ -267,174 +276,205 @@ def rank_program(g, core, T, topo):
     cp(o("n1r"), ind(o("nxr"), o("offe")))
     bcast("nxa", "n1r")
     tt(e0(0), e0(0), o("eR", p=P), add)
-    ts(X2, cc(JF), float(me), gt, -48.0, mul)
-    ts(X3, cc(JF), float(me), eq, float(REM - CAPP * me), mul)
+    ts(cc(X2), cc(JF), float(me), gt, -48.0, mul)
+    ts(cc(X3), cc(JF), float(me), eq, float(REM - CAPP * me), mul)
     cp(o("offR", p=P), e0(0))
-    ts(X1, cc(JF), 48.0, mul, -1.0, add)
-    tt(X2, X2, X3, add)
+    ts(cc(X1), cc(JF), 48.0, mul, -1.0, add)
+    tt(cc(X2), cc(X2), cc(X3), add)
     cp(o("Rr"), ind(o("iot", 0, 512, k="iota"), o("offR")))
     bcast("Ra", "Rr")
-    bcast("nxB", "nxr")
-    ts(X3, cc(JF), 6.0, eq, 256.0, mul)
-    tt(X1, X1, X2, add)
+    iota(o("ctab"), [[1, TN], [0, 2]])
+    iota(o("GC", 15, 26, k="GC.c"), [[0, 11]], V * me)
+    if me > 0:
+        iota(o("GC", 0, 3 * me, k="GC.a"), [[V, me], [0, 3]])
+    if me < N - 1:
+        iota(o("GC", 3 * me, 15, k="GC.b"), [[V, N - 1 - me], [0, 3]], V * (me + 1))
+    ts(cc(X4), cc(JF), 6.0, eq, 256.0, mul)
+    tt(cc(X1), cc(X1), cc(X2), add)
     ts(cc(OD), cc(JF), 16.0, ge, 16.0, mul)
-    tt(cc(BASE), X1, X3, add)
+    tt(cc(BASE), cc(X1), cc(X4), add)
+    act(o("iot", 1024, 1280, k="iotc"), o("iot", 0, 256, k="iota"), Ident, bias=1024.0)
     act(o("pl5"), o("nxa"), Ident, scale=512.0, bias=512.0)
 
-    def spread(src, f, off):
-        ts(o("h" + f), src, 4, shr)
-        ts(o("k" + f), o("h" + f), 16.0, mul, cc(OD), add)
-        tt(o("h" + f), src, o("k" + f), add)
-        cp(off, o("h" + f))
-
-    def place(f, nk, src, off, meanwhile):
-        zd, zt, za, zb = "zd" + f, "zt" + f, "za" + f, "zb" + f
-        ts(o("mk" + f), src, cc(JF), eq)
-        scan(o("cn" + f), o("ones", 0, 16 * nk, k=("ones0",) if f == "0" else ("ones0", "ones1")), o("mk" + f), cc(BASE))
-        tt(o3(zd, 0, 16, zd + "l"), o("mk" + f), o("cn" + f), mul)
-        act(o3(zd, 16, 32, zd + "h"), o3(zd, 0, 16, zd + "l"))
-        meanwhile()
-        op("v", lambda: g.vector.transpose(T[zt][:], T[zd][:]), (zd + "l", zd + "h"), (zt,))
-        tt(o3(za, 0, 4), o3(zt, 0, 4), o3(zt, 4, 8), add)
+    def fold(f):
+        za, zb = "za" + f, "zb" + f
+        tt(o3(za, 0, 4), o3("zt" + f, 0, 4), o3("zt" + f, 4, 8), add)
         tt(o3(zb, 0, 2), o3(za, 0, 2), o3(za, 2, 4), add)
         si = o("si" + f)
         op("v", lambda: g.vector.tensor_tensor(si[1], T[zb][:, :, 0], T[zb][:, :, 1], add), (zb,), si[0])
-        spread(si, f, off)
 
     def row(out, name, lo, hi, j, key):
-        tt(out, o(name, lo + j, hi, 32, k=key), o(name, lo + j + 16, hi, 32, k=key), add)
+        op("v", lambda: g.vector.tensor_tensor(out[1], T[name][:, lo:hi, j], T[name][:, lo:hi, j + 16], add), (key,), out[0])
 
     ts(o("ai0"), o("nxa"), -191.5, add, 1.0 / TN, mul)
-    place("0", 10, o("ai0"), o("off0"), lambda: tt(o("pl0"), o("pl5"), o("Ra"), add))
+    ts(o("mk0"), o("ai0"), cc(JF), eq)
+    scan(o("cn0"), o("ones", 0, V, k="ones0"), o("mk0"), cc(BASE))
+    tt(o3("zd0", 0, 16, "zd0l"), o("mk0"), o("cn0"), mul)
+    act(o3("zd0", 16, 32, "zd0h"), o3("zd0", 0, 16, "zd0l"))
+    tt(o("pl0"), o("pl5"), o("Ra"), add)
+    op("v", lambda: g.vector.transpose(T.zt0[:], T.zd0[:]), ("zd0l", "zd0h"), ("zt0",))
+    fold("0")
+    ts(o("k0"), o("si0"), 496, band)
+    tt(o("h0"), o("si0"), o("k0"), add)
+    ts(o("off0"), o("h0"), cc(OD), add)
     scatter(o("S0"), o("off0"), o("pl0"))
-    tr(o("S0t", 0, 480, k="S0ta"), o("S0", 0, 480))
-    row(o("pkw", 0, 15, k="pkw"), "S0t", 0, 480, 0, "S0ta")
+    op("v", lambda: g.vector.transpose(T.S0t[:, 0:15, :], T.S0[:, 0:480]), ("S0",), ("S0ta",))
+    row(o("pkw", 0, 15, k="pkw"), "S0t", 0, 15, 0, "S0ta")
     lists("pkw", "m1", "am1")
-    ms(o("xt", 0, 4 * ZC, k="xtz"), 0.0)
     ts(o("pwa"), o("pkw", 0, 15, k="pkw"), 255, band)
     ts(o("offS"), stA, float(ZC), add)
     quant("x", 0, ZC + TN, "xt", 0, ZC + TN, ("xtx", "xtz"), "x")
     ts(o("offi", 0, 15), o("pwa"), -1.0, add, 0.0, mx)
+    cp(o("nxo"), nxA)
     pick("w0", 0, V, "x", o("offS"), "w0", ("x",))
     pick("sl1", 0, REM, "w0", o("offi", 0, 15), "sl1", ("w0",))
     columns("sl1", "A", 0, CAPP, "ac1")
-    ts(o("oh"), o("iot", 0, 16, k="iota"), cc(P16), eq)
-    act(o("nxn"), o("ctab"), scale=oh(C1))
-    act(o("iot", 512, 1024, k="iotb"), o("iot", 0, 512, k="iota"), Ident, bias=512.0)
-    act(o("c1c"), o("iot", 0, N1, k="iota"), Ident, scale=oh(SG), bias=oh(SG))
-    act(o("S1", 0, 992), o("iot", 0, 992, k=("iota", "iotb")), scale=0.0)
-    tr(o("S0t", 480, 800, k="S0tb"), o("S0", 480, 800))
-    ts(X1, cc(P16), 8.0, lt, 1.0 / TN, mul)
-    ts(X2, oh(F3), 1024.0, mul)
-    row(o("pkw", 16, 26, k="pkws"), "S0t", 480, 800, 0, "S0tb")
-    pkws = o("pkw", 16, 26, k="pkws")
-    ts(cc(TB), X1, -191.5, mul)
-    tt(cc(TA), X1, X2, add)
-    ts(o("pwb"), pkws, 255, band)
-    ts(o("nxm"), o("nxB"), cc(TA), mul, cc(TB), add)
-    ts(o("offj"), o("pwb"), -1.0, add, 0.0, mx)
-    tt(o("nxT", 0, 768, k="nxTa"), o("nxm"), o("nxn"), add)
-    pick("A", REM, N1, "w0", o("offj"), "Ah", ("w0",))
-    ms(o("nxT", 768, 800, k="nxTz"), 6.0)
-    ms(o("ones", V, 1024, k="ones1"), 1.0)
-    for q in others:
-        ms(o("GC", 3 * pos(me, q), 3 * pos(me, q) + 3), float(V * q))
-    ms(o("GC", 15, 25), float(V * me))
-    quant("A", N1, N1 + TN, "xt", ZC, ZC + TN, ("xtx",), "Ax")
-    iota(o("c2a", 0, REM, k="c2aa"), [[32, 15], [1, 16]], BN0)
-    iota(o("c2a", REM, N2, k="c2ab"), [[1, M]], BH0)
-    iota(o("f16"), [[0, 31], [1, 16]])
 
-    ts(h("xr", 15, 25, "s"), pkws, 8, shr)
-    ts(h("g1", 15, 25, "s"), pkws, 255, band)
-    ts(h("xr", 0, 15, "r"), o("m1"), 8, shr)
-    ts(h("g1", 0, 15, "r"), o("m1"), 255, band)
-    ts(o("x2"), o("xr", k=("xr.s", "xr.r")), float(-(2 * TN * me + 2)), add)
-    tt(o("g1f"), o("g1", k=("g1.s", "g1.r")), o("GC"), add)
-    ts(o("xiv"), o("x2"), 0.0, lt, 8000.0, mul)
-    cp(o("offG", 0, 25), o("g1f"))
-    act(o("t1"), ind(iot, o("offG", 0, 25)), scale=oh(F3))
-    tt(o("x3"), o("x2"), o("xiv"), add)
-    ts(o("x4"), o("x3"), 783.0, mn)
-    ts(o("xlo"), o("x4"), 15, band)
-    ts(o("xhi"), o("x4"), 4, shr)
-    ts(o("xp"), o("xlo"), 48.0, mul)
-    tt(o("xpp"), o("xp"), o("xhi"), add)
-    cp(o("offE", 0, 25), o("xpp"))
-    tt(o("pl1a"), ind(o("nxT", 0, 800, k=("nxTa", "nxTz")), o("offE", 0, 25)), o("c1c"), add)
-    place("1", 25, o("pl1a"), o("off1", 0, 25), lambda: tt(o("pl1"), o("pl1a"), o("t1"), add))
-    scatter(o("S1"), o("off1", 0, 25), o("pl1"))
-    tr(o("S1t", 0, 480, k="S1ta"), o("S1", 0, 480))
-    row(o("f3w"), "S1t", 0, 480, 8, "S1ta")
+    iota(o("c1i"), [[32, 13], [1, 16]], 1)
+    if me > 0:
+        iota(o("padi", 0, 3 * me, k="padi.a"), [[0, me], [16, 3]], GT + CAPP * (me - 1))
+    if me < N - 1:
+        iota(o("padi", 3 * me, 15, k="padi.b"), [[0, N - 1 - me], [16, 3]], GT + CAPP * me)
+    iota(o("padi", 15, 31, k="padi.c"), [[16, 16]], GT + REM)
+    for j, (bl, sl, bo, so) in enumerate(((272, 16, 16, 16), (BN0, 32, BH0, 16), (BN0 + 16, 32, BH1, 16))):
+        iota(o("kv", 32 * j, 32 * j + 15, k="kv%da" % j), [[sl, 15]], bl)
+        iota(o("kv", 32 * j + 15, 32 * j + 32, k="kv%db" % j), [[so, 17]], bo)
+    GCk = ("GC.a", "GC.b")
+    PDk = ("padi.a", "padi.b", "padi.c")
+
+    iotk = ("iota", "iotb", "iotc", "iotd", "iote")
+    act(o("iot", 1280, 2048, k="iotd"), o("iot", 256, 1024, k=IA), Ident, bias=1024.0)
+    act(o("iot", 2048, 2304, k="iote"), o("iot", 0, 256, k="iota"), Ident, bias=2048.0)
+    op("v", lambda: g.vector.transpose(T.S0t[:, 15:25, :], T.S0[:, 480:800]), ("S0",), ("S0tb",))
+    ts(cc(X1), cc(P16), 8.0, lt, 1.0 / TN, mul)
+    ts(cc(X2), oh(F3), float(1 << GB), mul)
+    row(o("pkw", 16, 26, k="pkws"), "S0t", 15, 25, 0, "S0tb")
+    pkws = o("pkw", 16, 26, k="pkws")
+    ts(cc(X3), cc(X1), -191.5, mul)
+    tt(cc(TA), cc(X1), cc(X2), add)
+    tt(cc(TB), cc(X3), cc(X2), add)
+    act(o("nxT", 1, 769, k="nxTa"), ind(o("iot", k=iotk), o("nxo")), Ident, scale=cc(TA), bias=cc(TB))
+    act(o("nxn"), o("ctab"), scale=oh(C1))
+    ts(o("pwb"), pkws, 255, band)
+    ts(cc(EV), cc(JF), 16.0, lt)
+    ts(o("offj"), o("pwb"), -1.0, add, 0.0, mx)
+    ts(cc(OV), cc(JF), 16.0, ge)
+    pick("A", REM, N1, "w0", o("offj"), "Ah", ("w0",))
+    ts(cc(X4), cc(OD), oh(SG), mul)
+    ms(o("nxT", 0, 1, k="nxTz"), 6.0)
+    ms((("xg.z",), T.xg[:, :, 25:26]), 0)
+    ms(o("rk", N1, W1, k="rkz"), 6)
+    ts(xg(0, 15, 25, "xg.0s"), pkws, 8, shr)
+    tt(xg(1, 15, 25, "xg.1s"), o("pwb"), o("GC", 15, 25, k="GC.c"), add)
+    ts(o("offE", 15, 25, k="offE.s"), xg(0, 15, 25, "xg.0s"), float(-(2 * TN * me + 1)), add, 0.0, mx)
+    ts(cc(X5), oh(SG), cc(X4), add)
+    act(o("ones", V, 1024, k="ones1"), o("iot", V, 1024, k=IA), Ident, scale=0.0, bias=1.0)
+    act(o("gidT"), o("iot", 0, 1024, k=IA), scale=oh(F3))
+    act(o("c1h"), o("c1i"), Ident, scale=oh(SG), bias=cc(X4))
+    act(o("S1"), o("iot", 0, 928, k=IA), scale=0.0)
+    act(o("PT"), o("iot", 0, 1472, k=("iota", "iotb", "iotc", "iotd")), scale=0.0)
+    act((("T2",), T.T2[:]), o("iot", 0, 512, k="iota"), scale=0.0)
+    act(o("PS", GT, GT + N2, k="PS.b"), o("iot", 0, N2, k="iota"), Ident, bias=256.0)
+    act(o("pr", N2, 512, k="prz"), o("iot", 752, 768, k=IA))
+    act(o("S2"), o("iot", 0, 768, k=IA), scale=0.0)
+    tt(o("nxT", 1, 769, k="nxTb"), o("nxT", 1, 769, k="nxTa"), o("nxn"), add)
+    quant("A", N1, N1 + TN, "xt", ZC, ZC + TN, ("xtx",), "Ax")
+
+    nxT = o("nxT", 0, 769, k=("nxTb", "nxTz"))
+    xgk = ("xg.0r", "xg.0s", "xg.1r", "xg.1s", "xg.z")
+    ts(xg(0, 0, 15, "xg.0r"), o("m1"), 8, shr)
+    ts(o("g1", 0, 15), o("m1"), 255, band)
+    ts(o("offE", 0, 15, k="offE.r"), xg(0, 0, 15, "xg.0r"), float(-(2 * TN * me + 1)), add, 0.0, mx)
+    tt(xg(1, 0, 15, "xg.1r"), o("g1", 0, 15), o("GC", 0, 15, k=GCk), add)
+    cp(o("rk", 0, N1, k="rk"), ind(nxT, o("offE", 0, 25, k=("offE.r", "offE.s"))))
+    ts(o("sA"), (xgk, T.xg[:, :, 0:26:2]), cc(EV), mul)
+    ts(o("mk1"), o("rk", k=("rk", "rkz")), cc(JF), eq)
+    ts(o("sB"), (xgk, T.xg[:, :, 1:26:2]), cc(OV), mul)
+    scan(o("cn1"), o("ones", 0, W1, k=("ones0", "ones1")), o("mk1"), cc(BASE))
+    tt(o("xh"), o("sA"), o("sB"), add)
+    op("v", lambda: g.vector.tensor_tensor(T.zd1[:], T.mk1[:], T.cn1[:], mul), ("mk1", "cn1"), ("zd1",))
+    cp(o("offGh", 0, 13), (("xh",), T.xh[:, 1, :]))
+    op("v", lambda: g.vector.transpose(T.zt1[:], T.zd1[:]), ("zd1",), ("zt1",))
+    ts(o("offEh", 0, 13), (("xh",), T.xh[:, 0, :]), float(-(2 * TN * me + 1)), add, 0.0, mx)
+    tt(o("plG"), ind(o("gidT"), o("offGh", 0, 13)), o("c1h"), add)
+    fold("1")
+    tt(o("pl1"), ind(nxT, o("offEh", 0, 13)), o("plG"), add)
+    cp(o("off1", 0, 13), o("si1"))
+    scatter(o("S1"), o("off1", 0, 13), o("pl1"))
+    cp(o3("S1d", 0, 16, "S1d.al", 0, 15), o("S1", 0, REM))
+    act(o3("S1d", 16, 32, "S1d.ah", 0, 15), o("S1", 0, REM))
+    ts(o("pad", 0, 31), o("padi", 0, 31, k=PDk), cc(P16), add)
+    op("v", lambda: g.vector.transpose(T.S1t[:, 0:15, :], T.S1d[:, 0:15, :]), ("S1d.al", "S1d.ah"), ("S1ta",))
+    row(o("f3r", 0, 15), "S1t", 0, 15, F3, "S1ta")
+    row(o("sga"), "S1t", 0, 15, SG, "S1ta")
+    tt(o("f3w"), o("f3r", 0, 15), o("pad", 0, 15), mx)
     lists("f3w", "m2", "am2")
-    row(o("sga"), "S1t", 0, 480, SG, "S1ta")
-    row(o("c1a"), "S1t", 0, 480, C1, "S1ta")
+    row(o("c1a"), "S1t", 0, 15, C1, "S1ta")
     ts(o("off2", 0, 30, 2), o("sga"), -1.0, add, 0.0, mx)
     ts(o("off2", 1, 30, 2), o("c1a"), float(N1), add)
+    act(o3("S1d", 16, 32, "S1d.bh", 15, 31), o("S1", REM, N2))
     pick("sl2", 0, 2 * REM, "A", o("off2"), "sl2", ("Al", "Ah", "Ax"))
     columns("sl2", "B", BN0, 2 * CAPP, "ac2")
-    tr(o("S1t", 480, 992, k="S1tb"), o("S1", 480, 992))
-    ts(cc(C32), oh(F3), 32.0, mul)
-    ts(cc(R16), oh(S1R), 16.0, mul)
-    row(o("f3s"), "S1t", 480, 992, 8, "S1tb")
-    row(o("sgb"), "S1t", 480, 992, SG, "S1tb")
-    row(o("c1b"), "S1t", 480, 992, C1, "S1tb")
-    ts(cc(R256), oh(S1R), 256.0, mul)
+
+    cp(o3("S1d", 0, 16, "S1d.bl", 15, 31), o("S1", REM, N2))
+    op("v", lambda: g.vector.transpose(T.S1t[:, 15:31, :], T.S1d[:, 15:31, :]), ("S1d.bl", "S1d.bh"), ("S1tb",))
+    row(o("f3s"), "S1t", 15, 31, F3, "S1tb")
+    row(o("sgb"), "S1t", 15, 31, SG, "S1tb")
+    tt(o("f3p"), o("f3s"), o("pad", 15, 31, k="pad"), mx)
+    row(o("c1b"), "S1t", 15, 31, C1, "S1tb")
+
+    def decode(f, w, in_):
+        ts(o("g2" + f), in_, (1 << GB) - 1, band)
+        ts(o("h2" + f), in_, GB, shr)
+        cp(o("offg" + f, 0, w), o("g2" + f))
+
+    def names(f, w):
+        a = 1 if f == "O" else 0
+        key = "" if f == "L" else ".o"
+        ts(o("c" + f, a, a + w, k="c" + f + key), o("h2" + f), float(ZC - TN * me - 1), add, 0.0, mx)
+        ts(o("r2" + f), o("g2" + f), -(V + 1) / 2.0, add, 1.0 / V, mul)
+        ts(o("a" + f, a, a + w, k="a" + f + key), o("r2" + f), 1.0, add)
+        ts(o("u2" + f), o("r2" + f), float(-V), mul)
+        tt(o("u2" + f), o("u2" + f), o("g2" + f), add)
+        ts(o("b" + f, a, a + w, k="b" + f + key), o("u2" + f), 0.0, mx)
+    decode("O", 16, o("f3p"))
     ts(o("offc"), o("sgb"), -1.0, add, 0.0, mx)
     ts(o("offd"), o("c1b"), float(ZC), add)
-    tt(cc(RSS), oh(SG), oh(S1R), add)
-    pick("B", BH0, BH1, "A", o("offc"), "Bh0", ("Al", "Ah", "Ax"))
-    pick("B", BH1, BW, "x", o("offd"), "Bh1", ("x",))
+    for n in "cab":
+        ms(o(n + "O", 0, 1, k=n + "O.z"), 0)
+    names("O", 16)
+    for j in range(3):
+        ts((("T2",), T.T2[:, :, F3 + j:32:16]), o("kv", 32 * j, 32 * j + 32, k=("kv%da" % j, "kv%db" % j)), cc(P16), add)
+    scatter(o("PT"), o("offgO"), o("ones", 0, M, k=("ones0", "ones1")))
+    op("v", lambda: g.vector.transpose(T.c2t[:], T.T2[:]), ("T2",), ("c2t",))
+    act(o("c2h"), o3("c2t", 0, 16))
+    pick("n2", 0, 272, "x", o("cO", 0, 17, k=("cO.o", "cO.z")), "n2o", ("x",))
+    for n, gd in (("a", "gida"), ("b", "gidb")):
+        act(o(gd, 0, 272, k=gd + ".o"), ind(o("iot", 0, 1024, k=IA), o(n + "O", 0, 17, k=(n + "O.o", n + "O.z"))))
 
-    act(o("PT", 0, 992), o("iot", 0, 992, k=("iota", "iotb")), scale=0.0)
-    act(o("PT", 992, 1472), o("iot", 0, 480, k="iota"), scale=0.0)
-    act(o("c2g"), o("iot", 0, N2, k="iota"), Ident, scale=oh(F3), bias=cc(C32))
-    act(o("PS", GT, GT + N2, k="PS.b"), o("iot", 0, N2, k="iota"), Ident, bias=256.0)
-    act(o("S2", 0, 512), o("iot", 0, 512, k="iota"), scale=0.0)
-    ts(o("TC"), o("ci", 8, 39, k="wc"), cc(P16), add, float(GT), add)
-    for n in ("offga", "offgb", "offc2"):
-        ms(o(n, 0, 2, k=n + ".z"), 0)
-    ts(o("m16"), o("f16"), cc(P16), eq)
-    ts(o("rmk"), o("f16"), 0.0, ne)
-    ts(o("c2b", 0, REM), o("c2a", 0, REM, k="c2aa"), cc(R16), add, cc(RSS), mul)
-    ts(o("c2b", REM, N2), o("c2a", REM, N2, k="c2ab"), cc(R256), add, cc(RSS), mul)
-    tt(o("c2c"), o("c2b"), o("c2g"), add)
-    quant("B", 0, ZC, "xt", 0, ZC, ("xtz",), "Bz")
-    quant("w", 0, 384, "wt", 0, 384, ("wt",), "wa")
-    quant("w", 384, 768, "wt", 384, 768, ("wt",), "wb")
-    ts(h("g2", 15, 31, "s"), o("f3s"), 1023, band)
-    ts(h("h2", 15, 31, "s"), o("f3s"), 10, shr)
-
-    ts(h("g2", 0, 15, "r"), o("m2"), 1023, band)
-    ts(h("h2", 0, 15, "r"), o("m2"), 10, shr)
-    g2, h2 = o("g2", k=("g2.s", "g2.r")), o("h2", k=("h2.s", "h2.r"))
-    ts(o("iv2"), g2, 0.0, eq)
-    ts(o("r2"), g2, -(V + 1) / 2.0, add, 1.0 / V, mul)
-    tt(o("tr2"), o("iv2"), o("TC"), mul)
-    ts(o("offc2", 2, 33), h2, float(ZC - TN * me), add, 0.0, mx)
-    tt(o("gf2"), o("tr2"), g2, add)
-    ts(o("u2"), o("r2"), float(-V), mul)
-    cp(o("offg2", 0, 31), o("gf2"))
-    ts(o("offga", 2, 33), o("r2"), 1.0, add)
-    scatter(o("PT"), o("offg2", 0, 31), o("ones", 0, N2, k=("ones0", "ones1")))
-    tt(o("u2"), o("u2"), g2, add)
+    decode("L", 15, o("m2"))
+    scatter(o("PT"), o("offgL", 0, 15), o("ones", 0, REM, k=("ones0", "ones1")))
+    names("L", 15)
     scan(o("PS", 0, GT, k="PS.a"), o("ones", 0, GT, k=("ones0", "ones1")), o("PT", 0, GT), -1.0)
-    cp(o("offgb", 2, 33), o("u2"))
-    for n, gd in (("offga", "gida"), ("offgb", "gidb")):
-        act(o(gd), ind(iot, o(n, 0, 33, k=(n, n + ".z"))))
-    tt(o("pm"), ind(o("PS", 0, GT + N2, k=("PS.a", "PS.b")), o("offg2", 0, 31)), o("m16"), mul)
-    scan(o("rs"), o("rmk"), o("pm"), 0.0)
-    cp(o("pwi"), o("rs", 15, N2, 16))
-    spread(o("pwi"), "p", o("offP", 0, 31))
-    scatter(o("S2"), o("offP", 0, 31), o("c2c"))
-    pick("n2", 0, 528, "x", o("offc2", 0, 33, k=("offc2", "offc2.z")), "n2", ("x",))
-    tr(o("S2t"), o("S2", 0, 512))
+    PS = o("PS", 0, GT + N2, k=("PS.a", "PS.b"))
+    act(o("pr", REM, N2, k="prO"), ind(PS, o("offgO")))
+    cp(o("pr", 0, REM, k="prL"), ind(PS, o("offgL", 0, 15)))
+    tr(o("prt"), o("pr", k=("prL", "prO", "prz")))
+    cp(o("offP"), o("prt", 0, 512, 32))
+    scatter(o("S2"), o("offP"), o("c2h"))
+    pick("n2", 272, 512, "x", o("cL", 0, 15), "n2l", ("x",))
+    act(o3("S2d", 16, 32, "S2d.h"), o("S2", 0, M))
+    cp(o3("S2d", 0, 16, "S2d.l"), o("S2", 0, M))
+    op("v", lambda: g.vector.transpose(T.S2t[:], T.S2d[:]), ("S2d.l", "S2d.h"), ("S2t",))
     off = [h("offF", 16 * k, 16 * k + 16, "%d" % k) for k in range(3)]
-    for k, j in enumerate((F3, SG, S1R)):
-        row(h("ga", 16 * k, 16 * k + 16, "%d" % k), "S2t", 0, 512, j, "S2t")
-    for k in range(3):
-        cp(off[k], h("ga", 16 * k, 16 * k + 16, "%d" % k))
-    pick("p2", 0, M, "n2", off[0], "p2", ("n2",))
+    ga = [h("ga", 16 * k, 16 * k + 16, "%d" % k) for k in range(3)]
+    row(ga[0], "S2t", 0, 16, F3, "S2t")
+    row(ga[1], "S2t", 0, 16, F3 + 1, "S2t")
+    cp(off[0], ga[0])
+    row(ga[2], "S2t", 0, 16, F3 + 2, "S2t")
+    cp(off[1], ga[1])
+    cp(off[2], ga[2])
+    pick("p2", 0, M, "n2", off[0], "p2", ("n2o", "n2l"))
 
     def product(k, last):
         n = "p%d" % k
@@ -442,18 +482,25 @@ def rank_program(g, core, T, topo):
             a = 128 * (k * NO + oo)
             op("k", lambda: g.tensor.matmul_mx(T["ps_%d" % oo][:, 0:M], T.wq[:, a:a + 128], T.ws[:, a:a + 128], T[n + "q"][:], T[n + "s"][:], k == 2, last),
                ("waq", "was", "wbq", "wbs", n + "q", n + "s"), ("ps_%d" % oo,) if last else ())
+    quant("w", 0, 384, "wt", 0, 384, ("wt",), "wa")
+    quant("w", 384, 768, "wt", 384, 768, ("wt",), "wb")
+    quant("B", 0, ZC, "xt", 0, ZC, ("xtz",), "Bz")
     product(2, False)
+    pick("B", BH0, BH1, "A", o("offc"), "Bh0", ("Al", "Ah", "Ax"))
+    pick("B", BH1, BW, "x", o("offd"), "Bh1", ("x",))
     Bk = ("Bz", "Bl", "Bh0", "Bh1")
+    for n, gd in (("a", "gida"), ("b", "gidb")):
+        act(o(gd, 272, 512, k=gd + ".l"), ind(o("iot", 0, 1024, k=IA), o(n + "L", 0, 15)))
     pick("p0", 0, M, "B", off[1], "p0", Bk)
     product(0, False)
     pick("p1", 0, M, "B", off[2], "p1", Bk)
     product(1, True)
+    for j, gd in ((0, "gida"), (1, "gidb")):
+        act(h("idt", M * j, M * j + M, "%d" % j), ind(o(gd, k=(gd + ".o", gd + ".l")), off[0]), Ident, bias=-1.0)
     cp(o("yo0"), o("ps_0", 0, M))
     act(o("yo1"), o("ps_1", 0, M))
     dma("y", (("y0",), T.y[:, 0:M]), o("yo0"), "dy0")
     dma("s", (("y1",), T.y[:, M:2 * M]), o("yo1"), "dy1")
-    for j, gd in ((0, "gida"), (1, "gidb")):
-        act(h("idt", M * j, M * j + M, "%d" % j), ind(o(gd), off[0]), Ident, bias=-1.0)
     op("y", lambda: g.sync.dma_start(T["id"][:], T.idt[0:1, :]), ("idt.0", "idt.1"), ("ido",), sem="did", inc=16)
     for sem, c in count.items():
         if know["p"].get(sem, 0) < c:

@@ -1,16 +1,15 @@
 from concourse.bass import DstId, RemoteDMATransfer
-from concourse.mybir import dt, AluOpType, ActivationFunctionType
+from concourse.mybir import dt, AluOpType, AxisListType, ActivationFunctionType
 
 N, TN, V, M, CAPP, NO = 6, 384, 160, 256, 48, 2
 REM = CAPP * (N - 1)
 N1 = REM + V
-N2 = REM + M
-GT = N * V + 1
-GB = 11
 ZC = 128
-BN0, BH0, BH1 = ZC, ZC + 2 * REM, ZC + 2 * REM + M
-BW = BH1 + M
-W1, H1 = N1 + 16, (N1 + 16) // 2
+BX, BA = ZC, ZC + TN
+BL = BA + N1
+BW = BL + 2 * REM
+T1 = REM + M
+FN0, FN1, FN2, FID = 8, 9, 10, 11
 
 _F, _I, _U, _C, _S = "float32", "int32", "uint16", "float8_e4m3fn_x4", "uint8"
 SCRATCH, POOL = {}, {}
@@ -29,32 +28,36 @@ def _pool(buf, dtype, **widths):
     _add(dtype, **{buf: at})
 
 
-_add(_I, ci=40)
-_add(_F, cc=40, oh=16, ones=1024, iot=2304, ctab=768, nxn=768, gidT=1024)
-_add(_I, st0=10, bt0=10, stA=10, nxr=768, nxA=48, ai0=V, pkw=32)
-_add(_F, n1r=V, nxa=V, Rr=V, Ra=V, pl5=V, pl0=V, S0=800, S0t=(25, 32))
-_add(_U, offe=10, offR=10, offS=10, off0=10, offi=16, offj=10, nxo=48)
+_add(_I, ci=8, st0=10, bt0=10, btg=10, stA=10, nxr=768, nxA=48)
+_add(_F, cc=48, oh=16, ones=V, iot=2304, nxT=776, ctab=776, ctb=768, ztab=400, tabA=16, io6=96, PM=96)
+_add(_F, Rt=(12, 2, 16), RT=384)
+_add(_F, n1r=V, nxa=V, nd0=(10, 32), nt0=(10, 32), S0=800, S0t=(15, 32))
+_add(_U, offe=10, offS=10, off0=10, offi=16, nxo=48)
+_add(_I, ai0=V)
 _add(_F, mk0=V, cn0=V, zd0=(10, 32), zt0=(10, 32), za0=(10, 4), zb0=(10, 2))
-_add(_I, m1=15, xg=(2, 26), f3w=15, rk=W1)
-_add(_F, nxT=784, c1i=H1, c1h=H1, mk1=W1, cn1=W1, zd1=(13, 32), zt1=(13, 32), za1=(13, 4), zb1=(13, 2), plG=H1, pl1=H1, S1=928, S1d=(31, 32), S1t=(31, 32),
-     sA=(2, 13), sB=(2, 13), xh=(2, 13))
-_add(_U, offE=26, offEh=14, offGh=14, off1=14, off2=30, offc=16, offd=16)
-_add(_I, m2=15)
-_add(_F, PT=1472, PS=1472, pr=512, prt=512, T2=(16, 32), c2t=(16, 32), c2h=256, S2=768, S2d=(16, 32), S2t=(16, 32), kv=96,
-     gida=512, gidb=512, idt=2 * M, yo0=M, yo1=M)
-_add(_U, offgL=16, offgO=16, offP=16, offF=64, cL=16, aL=16, bL=16, cO=18, aO=18, bO=18)
-_pool("pooli", _I, i0=50, si0=10, k0=10, h0=10, pwa=15, pwb=10, g1=26, f3r=16, f3s=16, f3p=16, sga=15, sgb=16, c1a=15, c1b=16,
-      g2L=15, g2O=16, h2L=15, h2O=16, r2L=15, r2O=16, padi=32, pad=32, GC=26)
-_pool("poolf", _F, e0=60, eR=10, si1=13, u2L=15, u2O=16, ga=64)
+_add(_F, L1=(6, 12), L1h=(3, 10), L2=(6, 12), L2h=(3, 10))
+_add(_U, offE=10, offA=10, offN=10)
+_add(_I, rr=V, ia=10)
+_add(_F, rk=V, nd1=(10, 32), nt1=(10, 32), M1b=V, mk1=V, cn1=V, z1=V, zd1=(10, 32), zt1=(10, 32), pay1=V, E0=V, E=V, S1=T1 + V,
+     S1d=(15, 32), S1t=(15, 32), X1=(5, 2, 3), Y1=(5, 2, 3), Z1=(5, 2, 3))
+_add(_F, xb=32, XA=96, XM=96, yb=32, YA=96, YM=96, fa1=(10, 8), fb1=(10, 4), fc1=(10, 2))
+_add(_U, off1=10, off2=30)
+_add(_F, r2=V, mk2=V, cn2=V, z2=V, zd2=(10, 32), zt2=(10, 32), ta2=(10, 2), pay2=V, S2=M + V, S2d=(16, 32), S2t=(16, 32),
+     ga=(16, 3), gb=(16, 3), gc=(16, 3), n01=(2, 16), X2=(4, 16), Y2=(4, 16), idtab=968, idt=M, yo0=M, yo1=M)
+_add(_U, off20=10, offF=64)
+_pool("pooli", _I, i0=40, si0=10, k0=10, h0=10)
+_pool("poolf", _F, e0=60, b1g=10, u0=10, x1=1, x2=1, p1=1, p2=1, q1=1, q2=1, pw0=16, L1a=10, L1b=10, L2a=10, L2b=10,
+      fd1=10, tb2=10, gd=16, ge2=16)
 _add("bfloat16", xt=4 * (ZC + TN), wt=3072)
-for _n, _w in (("x", ZC + TN), ("w", 768), ("w0", V), ("sl1", REM), ("A", N1 + TN), ("sl2", 2 * REM),
-               ("B", BW), ("n2", 512), ("p0", M), ("p1", M), ("p2", M)):
+for _n, _w in (("x", ZC + TN), ("w", 768), ("w0", V), ("sl1", REM), ("A", N1 + TN), ("sl2", 2 * REM), ("B", BW),
+               ("p0", M), ("p1", M), ("p2", M)):
     SCRATCH[_n + "q"] = ("sbuf", [128, _w], _C)
     SCRATCH[_n + "s"] = ("sbuf", [128, _w], _S)
 SCRATCH["ps_0"] = ("psum", [128, 512], _F)
 SCRATCH["ps_1"] = ("psum", [128, 512], _F)
 
-SEMAPHORES = ["qv", "qs", "qp", "qk", "dst0", "dbt0", "dnx", "dstA", "dnxA", "dx", "dw", "did", "dy0", "dy1", "am1", "ac1", "am2", "ac2", "loc"]
+SEMAPHORES = ["qv", "qs", "qp", "qk", "dst0", "dbt0", "dbtg", "dnx", "dstA", "dnxA", "dx", "dw", "dxA", "dxB", "dwA", "dwB", "dAB",
+              "did", "dy0", "dy1", "am1", "ac1", "am2", "ac2", "loc"]
 
 add, sub, mul, mx, mn = AluOpType.add, AluOpType.subtract, AluOpType.mult, AluOpType.max, AluOpType.min
 eq, ge, gt, lt, ne = AluOpType.is_equal, AluOpType.is_ge, AluOpType.is_gt, AluOpType.is_lt, AluOpType.not_equal
@@ -116,14 +119,16 @@ def rank_program(g, core, T, topo):
             lo, hi = at + (lo or 0), at + (w if hi is None else hi)
         return (keys, T[name][ps, slice(lo, hi, st)])
 
-    def h(name, a, b, f):
-        return o(name, a, b, k=name + "." + f)
+    def o3(name, lo=None, hi=None, k=None, p=None):
+        ps = slice(None) if p is None else slice(p[0], p[1])
+        return ((k,) if isinstance(k, str) else k or (name,), T[name][ps, :, slice(lo, hi)])
 
-    def o3(name, lo, hi, k=None, a=None, b=None):
-        return ((k or name,), T[name][:, slice(a, b), lo:hi])
+    def o1(name, j, k=None):
+        return ((k or name,), T[name][:, :, j])
 
-    def xg(j, a, b, k):
-        return ((k,), T.xg[:, j, a:b])
+    def o2(name, j, k=None, p=None):
+        ps = slice(None) if p is None else slice(p[0], p[1])
+        return ((k or name,), T[name][ps, j, :])
 
     def ci(j):
         return o("ci", j, j + 1, k="ci%d" % j)
@@ -156,9 +161,10 @@ def rank_program(g, core, T, topo):
             op("v", lambda: g.vector.tensor_scalar(out[1], a[1], v1, v2, f1, f2), rk, out[0])
 
     def scan(out, d0, d1, init):
-        rk = d0[0] + d1[0] + (init[0] if isinstance(init, tuple) else ())
-        iv = init[1] if isinstance(init, tuple) else init
-        op("v", lambda: g.vector.tensor_tensor_scan(out[1], d0[1], d1[1], iv, mul, add), rk, out[0])
+        op("v", lambda: g.vector.tensor_tensor_scan(out[1], d0[1], d1[1], init[1], mul, add), d0[0] + d1[0] + init[0], out[0])
+
+    def red(out, in_):
+        op("v", lambda: g.vector.tensor_reduce(out[1], in_[1], AxisListType.X, add), in_[0], out[0])
 
     def tr(out, in_):
         op("v", lambda: g.vector.transpose(out[1], in_[1]), in_[0], out[0])
@@ -175,17 +181,22 @@ def rank_program(g, core, T, topo):
     def scatter(win, off, in_):
         op("v", lambda: g.vector.tensor_copy(win[1].indirect(off[1]), in_[1]), win[0] + off[0] + in_[0], win[0])
 
-    def bcast(out, src):
-        op("p", lambda: g.partition_broadcast(T[out][:], T[src][0:1, :], 128), (src,), (out,))
-
-    def pick(outn, lo, hi, winn, off, key, wkeys):
-        op("v", lambda: g.vector.tensor_copy(T[outn + "q"][:, lo:hi].bitcast(dt.uint32), T[winn + "q"][:].bitcast(dt.uint32).indirect(off[1])),
-           tuple(x + "q" for x in wkeys) + off[0], (key + "q",))
-        op("s", lambda: g.scalar.activation(T[outn + "s"][:, lo:hi], T[winn + "s"][:].indirect(off[1]), Copy),
-           tuple(x + "s" for x in wkeys) + off[0], (key + "s",))
+    def pick(outn, winn, off, wkeys, hi=None):
+        op("v", lambda: g.vector.tensor_copy(T[outn + "q"][:].bitcast(dt.uint32), T[winn + "q"][:, 0:hi].bitcast(dt.uint32).indirect(off[1])),
+           tuple(x + "q" for x in wkeys) + off[0], (outn + "q",))
+        op("s", lambda: g.scalar.activation(T[outn + "s"][:], T[winn + "s"][:, 0:hi].indirect(off[1]), Copy),
+           tuple(x + "s" for x in wkeys) + off[0], (outn + "s",))
 
     def quant(outn, lo, hi, src, a, b, skeys, key):
         op("v", lambda: g.vector.quantize_mx(T[outn + "q"][:, lo:hi], T[outn + "s"][:, lo:hi], T[src][:, 4 * a:4 * b]), skeys, (key + "q", key + "s"))
+
+    def wq(j):
+        quant("w", 128 * j, 128 * j + 128, "wt", 128 * j, 128 * j + 128, ("wt",), "w%d" % j)
+
+    def move(outn, at, srcn, lo, hi, rkey, key, sem):
+        op("y", lambda: g.sync.dma_start(T[outn + "q"][:, at:at + hi - lo].bitcast(dt.uint8), T[srcn + "q"][:, lo:hi].bitcast(dt.uint8)),
+           (rkey + "q",), (key + "q",), sem=sem, inc=16, total=32)
+        op("y", lambda: g.sync.dma_start(T[outn + "s"][:, at:at + hi - lo], T[srcn + "s"][:, lo:hi]), (rkey + "s",), (key + "s",), sem=sem, inc=16, total=32)
 
     def fan(reads, src, dst, rsem):
         def call():
@@ -202,8 +213,8 @@ def rank_program(g, core, T, topo):
         op("p", call, reads, (), sem=None)
         count["loc"] += 16
 
-    def lists(name, land, rsem):
-        fan((name,), lambda q: T[name][:, 3 * pos(me, q):3 * pos(me, q) + 3], lambda q: T[land][:, 3 * pos(q, me):3 * pos(q, me) + 3], rsem)
+    def everyone(name, rsem):
+        fan((name + "o",), lambda q: T[name][:, me, 0:10], lambda q: T[name][:, me, 0:10], rsem)
 
     def columns(name, land, at, w, rsem):
         def src(n, q):
@@ -214,7 +225,7 @@ def rank_program(g, core, T, topo):
         fan((name + "q",), lambda q: src(name + "q", q).bitcast(dt.uint8), lambda q: dst(land + "q", q).bitcast(dt.uint8), rsem)
         fan((name + "s",), lambda q: src(name + "s", q), lambda q: dst(land + "s", q), rsem)
 
-    for s_, v_, ks in (("am1", 16, ("m1",)), ("ac1", 32, ("Alq", "Als")), ("am2", 16, ("m2",)), ("ac2", 32, ("Blq", "Bls"))):
+    for s_, v_, ks in (("am1", 16, ("L1i",)), ("ac1", 32, ("Alq", "Als")), ("am2", 16, ("L2i",)), ("ac2", 32, ("Blq", "Bls"))):
         count[s_] = v_
         for k in ks:
             wr[k] = [(s_, v_, {})]
@@ -228,34 +239,59 @@ def rank_program(g, core, T, topo):
     ms(o("nxr"), 0)
     dma("y", o("nxr", p=(0, 1)), ((), T.nx[:]), "dnx")
     dma("y", o("xt", 4 * ZC, 4 * (ZC + TN), k="xtx"), ((), T.x[:]), "dx")
-    for n, src, s_ in (("stA", T.st, "dstA"), ("nxA", T.nx, "dnxA")):
-        for k in range(8):
-            dma("y", o(n, p=(16 * k, 16 * k + 16), k=n + "%d" % k), ((), src[:]), s_, 128)
+    ms(o("btg"), 0)
+    for k in range(8):
+        dma("y", o("stA", p=(16 * k, 16 * k + 16), k="stA%d" % k), ((), T.st[:]), "dstA", 128)
+    dma("y", o("btg", p=(16 * me, 16 * me + 16)), ((), T.bt[:]), "dbtg")
+    for k in range(8):
+        dma("y", o("nxA", p=(16 * k, 16 * k + 16), k="nxA%d" % k), ((), T.nx[:]), "dnxA", 128)
     stA = (tuple("stA%d" % k for k in range(8)), T.stA[:])
     nxA = (tuple("nxA%d" % k for k in range(8)), T.nxA[:])
     dma("y", o("wt"), ((), T.w[:]), "dw")
 
     def iota(out, pattern, base=0, mult=0):
         op("p", lambda: g.iota(out[1], pattern, base, mult, allow_small_or_imprecise_dtypes=True), (), out[0])
-    wc = o("ci", 8, 40, k="wc")
+    iotk = ("iota", "iotb", "iotc", "iotd", "iote")
+    (R_M, R_E, R_B1, R_RM, R_B2, R_ZB, R_CB, R_RB, R_K1, R_K2, R_K3, R_J) = range(12)
+    allR = tuple("R%d" % c for c in range(12))
     iota(ci(0), [[1, 1]], 0, 1)
-    iota(wc, [[16, 32]])
     iota(o("iot", 0, 512, k="iota"), [[1, 512]])
-
-    IA = ("iota", "iotb")
-    (JF, P16, OD, BASE, TA, TB, EV, OV, CB, X1, X2, X3, X4, X5) = range(14)
-    F3, SG, C1 = 8, 9, 10
+    iota((("R%d" % R_J,), T.Rt[:, R_J, :, :]), [[0, 2], [1, 16]])
+    iota((allR[:R_J], T.Rt[:, 0:R_J, :, :]), [[0, 32 * R_J]])
+    (JF, J, G, OD, EV, OV, X1, X2, X3, X4, GM, GM2, BASE0, BASE1, J1, A1, A2, A3, A4, A5, X5, X6, GV) = range(23)
+    hh = 16 * (me % 2)
     ms(o("offe"), 0)
-    ms(o("offR"), 0)
     ts(ci(1), ci(0), 31, band)
     ts(ci(2), ci(0), 15, band)
-    ms(o("ones", 0, V, k="ones0"), 1.0)
+    ts(ci(3), ci(0), 4, shr)
+    ms(o("ones"), 1.0)
     cp(cc(JF), ci(1))
-    cp(cc(P16), ci(2))
-    ms(o("xt", 0, 4 * ZC, k="xtz"), 0.0)
-    act(o("iot", 512, 1024, k="iotb"), o("iot", 0, 512, k="iota"), Ident, bias=512.0)
-    act(o("S0"), o("iot", 0, 800, k=IA), scale=0.0)
-    ts(o("oh"), o("iot", 0, 16, k="iota"), cc(P16), eq)
+    cp(cc(J), ci(2))
+    cp(cc(G), ci(3))
+    ms(o3("nd0", 16 - hh, 32 - hh, "nd0z"), 0.0)
+
+    def R(c):
+        return o("RT", 32 * c, 32 * c + 1)
+
+    def rows(c, a, b, v):
+        act((("R%d" % c,), T.Rt[:, c, :, a:b]), o("iot", 0, 2 * (b - a), k="iota"), Ident, scale=0.0, bias=float(v))
+
+    def steps(c, a, b, m, v):
+        if b > a:
+            act((("R%d" % c,), T.Rt[:, c, :, a:b]), (("R%d" % R_J,), T.Rt[:, R_J, :, a:b]), Ident, scale=float(m), bias=float(v))
+    rows(R_M, 0, 16, 99)
+    rows(R_M, 8, 9, 0)
+    rows(R_M, 11, 12, -1)
+    steps(R_E, 0, 6, 1, 0)
+    for a_, b_, v_ in ((me, me + 1, 77), (6, 7, me), (7, 8, -1), (9, 16, 77), (11, 12, -1)):
+        rows(R_E, a_, b_, v_)
+    for c, w_, at_ in ((R_B1, CAPP, 0), (R_B2, 2 * CAPP, BL)):
+        steps(c, 0, me, w_, at_ - 1)
+        steps(c, me + 1, N, w_, at_ - w_ - 1)
+    for c, a_, b_, v_ in ((R_B1, 6, 7, REM - 1), (R_B1, 7, 8, T1 - 1), (R_B1, 8, 9, BA - 1), (R_RM, 0, 7, 1), (R_B2, 6, 7, -1), (R_B2, 7, 8, M - 1),
+                          (R_ZB, 0, 7, 1), (R_ZB, FN2, FN2 + 1, BX), (R_CB, FN1, FN1 + 1, BX - CAPP), (R_RB, 8, 10, 1), (R_RB, 11, 12, 1),
+                          (R_K1, 0, 6, 1000), (R_K2, me, me + 1, 1000), (R_K2, 8, 10, 1000000), (R_K3, 10, 16, 1000000)):
+        rows(c, a_, b_, v_)
 
     def i0(j):
         return o("i0", 10 * j, 10 * j + 10, k="i0%d" % j, p=P)
@@ -268,240 +304,231 @@ def rank_program(g, core, T, topo):
     ts(e0(3), i0(1), -767.0, mul)
     ts(e0(2), i0(0), 48.0, mul)
     tt(e0(4), e0(1), e0(3), add)
-    ts(i0(2), o("bt0", p=P), 1, shr)
+    ts(cc(GM), cc(G), float(me), eq)
     tt(e0(4), e0(4), e0(2), add)
-    ts(o("eR"), o("ci", 8, 18, k="wc"), cc(P16), add, 1.0, add)
-    cp(o("offe", p=P), e0(4))
-    ts(e0(0), i0(2), 256.0, mul)
-    cp(o("n1r"), ind(o("nxr"), o("offe")))
-    bcast("nxa", "n1r")
-    tt(e0(0), e0(0), o("eR", p=P), add)
     ts(cc(X2), cc(JF), float(me), gt, -48.0, mul)
+    cp(o("offe", p=P), e0(4))
     ts(cc(X3), cc(JF), float(me), eq, float(REM - CAPP * me), mul)
-    cp(o("offR", p=P), e0(0))
+    cp(o("n1r"), ind(o("nxr"), o("offe")))
+    op("p", lambda: g.partition_broadcast(T.nxa[:], T.n1r[0:1, :], 128), ("n1r",), ("nxa",))
     ts(cc(X1), cc(JF), 48.0, mul, -1.0, add)
     tt(cc(X2), cc(X2), cc(X3), add)
-    cp(o("Rr"), ind(o("iot", 0, 512, k="iota"), o("offR")))
-    bcast("Ra", "Rr")
-    iota(o("ctab"), [[1, TN], [0, 2]])
-    iota(o("GC", 15, 26, k="GC.c"), [[0, 11]], V * me)
-    if me > 0:
-        iota(o("GC", 0, 3 * me, k="GC.a"), [[V, me], [0, 3]])
-    if me < N - 1:
-        iota(o("GC", 3 * me, 15, k="GC.b"), [[V, N - 1 - me], [0, 3]], V * (me + 1))
     ts(cc(X4), cc(JF), 6.0, eq, 256.0, mul)
     tt(cc(X1), cc(X1), cc(X2), add)
+    i4 = o("i0", 30, 40, k="i03")
+    ts(i4, o("btg"), 1, shr)
     ts(cc(OD), cc(JF), 16.0, ge, 16.0, mul)
-    tt(cc(BASE), cc(X1), cc(X4), add)
-    act(o("iot", 1024, 1280, k="iotc"), o("iot", 0, 256, k="iota"), Ident, bias=1024.0)
-    act(o("pl5"), o("nxa"), Ident, scale=512.0, bias=512.0)
-
-    def fold(f):
-        za, zb = "za" + f, "zb" + f
-        tt(o3(za, 0, 4), o3("zt" + f, 0, 4), o3("zt" + f, 4, 8), add)
-        tt(o3(zb, 0, 2), o3(za, 0, 2), o3(za, 2, 4), add)
-        si = o("si" + f)
-        op("v", lambda: g.vector.tensor_tensor(si[1], T[zb][:, :, 0], T[zb][:, :, 1], add), (zb,), si[0])
-
-    def row(out, name, lo, hi, j, key):
-        op("v", lambda: g.vector.tensor_tensor(out[1], T[name][:, lo:hi, j], T[name][:, lo:hi, j + 16], add), (key,), out[0])
-
+    tt(cc(BASE0), cc(X1), cc(X4), add)
+    ts(o("b1g"), i4, 1.0, add, cc(GM), mul)
+    ts(cc(GM2), cc(GM), 2.0, mul)
+    ts(cc(EV), cc(JF), 16.0, lt)
+    ts(cc(OV), cc(JF), 16.0, ge)
+    ts(cc(GV), cc(G), float(V), mul)
+    ts(cc(A2), cc(G), float(me), gt, -48.0, mul)
+    cp(o3("nd0", hh, hh + 16, "nd0x"), o("nxa"))
     ts(o("ai0"), o("nxa"), -191.5, add, 1.0 / TN, mul)
+    tr((("nt0",), T.nt0[:]), (("nd0x", "nd0z"), T.nd0[:]))
     ts(o("mk0"), o("ai0"), cc(JF), eq)
-    scan(o("cn0"), o("ones", 0, V, k="ones0"), o("mk0"), cc(BASE))
+    ts(o("u0"), o1("nt0", 0), cc(GM2), mul)
+    scan(o("cn0"), o("ones"), o("mk0"), cc(BASE0))
+    tt((("L1o",), T.L1[:, me, 0:10]), o("u0"), o("b1g"), add)
+    everyone("L1", "am1")
+    iota(o("S0", 0, 480, k="S0"), [[0, 480]])
+    cp(o("nxo"), nxA)
     tt(o3("zd0", 0, 16, "zd0l"), o("mk0"), o("cn0"), mul)
     act(o3("zd0", 16, 32, "zd0h"), o3("zd0", 0, 16, "zd0l"))
-    tt(o("pl0"), o("pl5"), o("Ra"), add)
-    op("v", lambda: g.vector.transpose(T.zt0[:], T.zd0[:]), ("zd0l", "zd0h"), ("zt0",))
-    fold("0")
-    ts(o("k0"), o("si0"), 496, band)
-    tt(o("h0"), o("si0"), o("k0"), add)
-    ts(o("off0"), o("h0"), cc(OD), add)
-    scatter(o("S0"), o("off0"), o("pl0"))
-    op("v", lambda: g.vector.transpose(T.S0t[:, 0:15, :], T.S0[:, 0:480]), ("S0",), ("S0ta",))
-    row(o("pkw", 0, 15, k="pkw"), "S0t", 0, 15, 0, "S0ta")
-    lists("pkw", "m1", "am1")
-    ts(o("pwa"), o("pkw", 0, 15, k="pkw"), 255, band)
+    ms(o("xt", 0, 4 * ZC, k="xtz"), 0.0)
+    tr((("zt0",), T.zt0[:]), (("zd0l", "zd0h"), T.zd0[:]))
     ts(o("offS"), stA, float(ZC), add)
+    tt(o3("za0", 0, 4), o3("zt0", 0, 4), o3("zt0", 4, 8), add)
+    ts(o("oh"), o("iot", 0, 16, k="iota"), cc(J), eq)
+    tt(o3("zb0", 0, 2), o3("za0", 0, 2), o3("za0", 2, 4), add)
+    ts(cc(J1), cc(J), 1.0, add)
+    tt(o("si0"), o1("zb0", 0), o1("zb0", 1), add)
     quant("x", 0, ZC + TN, "xt", 0, ZC + TN, ("xtx", "xtz"), "x")
-    ts(o("offi", 0, 15), o("pwa"), -1.0, add, 0.0, mx)
-    cp(o("nxo"), nxA)
-    pick("w0", 0, V, "x", o("offS"), "w0", ("x",))
-    pick("sl1", 0, REM, "w0", o("offi", 0, 15), "sl1", ("w0",))
-    columns("sl1", "A", 0, CAPP, "ac1")
-
-    iota(o("c1i"), [[32, 13], [1, 16]], 1)
-    if me > 0:
-        iota(o("padi", 0, 3 * me, k="padi.a"), [[0, me], [16, 3]], GT + CAPP * (me - 1))
-    if me < N - 1:
-        iota(o("padi", 3 * me, 15, k="padi.b"), [[0, N - 1 - me], [16, 3]], GT + CAPP * me)
-    iota(o("padi", 15, 31, k="padi.c"), [[16, 16]], GT + REM)
-    for j, (bl, sl, bo, so) in enumerate(((272, 16, 16, 16), (BN0, 32, BH0, 16), (BN0 + 16, 32, BH1, 16))):
-        iota(o("kv", 32 * j, 32 * j + 15, k="kv%da" % j), [[sl, 15]], bl)
-        iota(o("kv", 32 * j + 15, 32 * j + 32, k="kv%db" % j), [[so, 17]], bo)
-    GCk = ("GC.a", "GC.b")
-    PDk = ("padi.a", "padi.b", "padi.c")
-
-    iotk = ("iota", "iotb", "iotc", "iotd", "iote")
-    act(o("iot", 1280, 2048, k="iotd"), o("iot", 256, 1024, k=IA), Ident, bias=1024.0)
+    ts(o("k0"), o("si0"), 496, band)
+    for n in ("nxT", "ctab"):
+        act(o(n, 0, 1, k=n + "z"), o("iot", 0, 1, k="iota"))
+        act(o(n, 769, 776, k=n + "y"), o("iot", 0, 7, k="iota"), scale=0.0)
+    act(o("iot", 512, 1024, k="iotb"), o("iot", 0, 512, k="iota"), Ident, bias=512.0)
+    act(o("iot", 1024, 1536, k="iotc"), o("iot", 0, 512, k="iota"), Ident, bias=1024.0)
+    act(o("iot", 1536, 2048, k="iotd"), o("iot", 0, 512, k="iota"), Ident, bias=1536.0)
     act(o("iot", 2048, 2304, k="iote"), o("iot", 0, 256, k="iota"), Ident, bias=2048.0)
-    op("v", lambda: g.vector.transpose(T.S0t[:, 15:25, :], T.S0[:, 480:800]), ("S0",), ("S0tb",))
-    ts(cc(X1), cc(P16), 8.0, lt, 1.0 / TN, mul)
-    ts(cc(X2), oh(F3), float(1 << GB), mul)
-    row(o("pkw", 16, 26, k="pkws"), "S0t", 15, 25, 0, "S0tb")
-    pkws = o("pkw", 16, 26, k="pkws")
-    ts(cc(X3), cc(X1), -191.5, mul)
-    tt(cc(TA), cc(X1), cc(X2), add)
-    tt(cc(TB), cc(X3), cc(X2), add)
-    act(o("nxT", 1, 769, k="nxTa"), ind(o("iot", k=iotk), o("nxo")), Ident, scale=cc(TA), bias=cc(TB))
-    act(o("nxn"), o("ctab"), scale=oh(C1))
-    ts(o("pwb"), pkws, 255, band)
-    ts(cc(EV), cc(JF), 16.0, lt)
-    ts(o("offj"), o("pwb"), -1.0, add, 0.0, mx)
-    ts(cc(OV), cc(JF), 16.0, ge)
-    pick("A", REM, N1, "w0", o("offj"), "Ah", ("w0",))
-    ts(cc(X4), cc(OD), oh(SG), mul)
-    ms(o("nxT", 0, 1, k="nxTz"), 6.0)
-    ms((("xg.z",), T.xg[:, :, 25:26]), 0)
-    ms(o("rk", N1, W1, k="rkz"), 6)
-    ts(xg(0, 15, 25, "xg.0s"), pkws, 8, shr)
-    tt(xg(1, 15, 25, "xg.1s"), o("pwb"), o("GC", 15, 25, k="GC.c"), add)
-    ts(o("offE", 15, 25, k="offE.s"), xg(0, 15, 25, "xg.0s"), float(-(2 * TN * me + 1)), add, 0.0, mx)
-    ts(cc(X5), oh(SG), cc(X4), add)
-    act(o("ones", V, 1024, k="ones1"), o("iot", V, 1024, k=IA), Ident, scale=0.0, bias=1.0)
-    act(o("gidT"), o("iot", 0, 1024, k=IA), scale=oh(F3))
-    act(o("c1h"), o("c1i"), Ident, scale=oh(SG), bias=cc(X4))
-    act(o("S1"), o("iot", 0, 928, k=IA), scale=0.0)
-    act(o("PT"), o("iot", 0, 1472, k=("iota", "iotb", "iotc", "iotd")), scale=0.0)
-    act((("T2",), T.T2[:]), o("iot", 0, 512, k="iota"), scale=0.0)
-    act(o("PS", GT, GT + N2, k="PS.b"), o("iot", 0, N2, k="iota"), Ident, bias=256.0)
-    act(o("pr", N2, 512, k="prz"), o("iot", 752, 768, k=IA))
-    act(o("S2"), o("iot", 0, 768, k=IA), scale=0.0)
-    tt(o("nxT", 1, 769, k="nxTb"), o("nxT", 1, 769, k="nxTa"), o("nxn"), add)
-    quant("A", N1, N1 + TN, "xt", ZC, ZC + TN, ("xtx",), "Ax")
+    act(o("nxT", 1, 769, k="nxTa"), ind(o("iot", k=iotk), o("nxo")), Ident, bias=1.0)
+    tt(o("h0"), o("si0"), o("k0"), add)
+    pick("w0", "x", o("offS"), ("x",))
+    ts(o("off0"), o("h0"), cc(OD), add)
+    iota(o("ctb"), [[1, TN], [0, 2]])
+    iota(o("io6"), [[0, 6], [1, 16]])
+    move("A", N1, "x", ZC, ZC + TN, "x", "Ax", "dxA")
+    move("B", 0, "x", 0, ZC + TN, "x", "Bx", "dxB")
+    move("A", REM, "w0", 0, V, "w0", "Aw", "dwA")
+    move("B", BA + REM, "w0", 0, V, "w0", "Bw", "dwB")
+    scatter(o("S0"), o("off0"), o("iot", 1, V + 1, k="iota"))
+    act(cc(A1), cc(GM), scale=oh(8))
+    act(cc(A3), cc(G), Ident, scale=48.0, bias=cc(A2))
+    act(cc(X3), cc(GV), scale=oh(11))
+    act(cc(A4), cc(GM), Ident, scale=float(REM - CAPP * me), bias=cc(A3))
+    act(cc(A5), cc(A4), Ident, scale=oh(8), bias=cc(X3))
+    op("v", lambda: g.vector.transpose(T.S0t[:], T.S0[:, 0:480]), ("S0",), ("S0t",))
+    tt(o("pw0", 0, 15), o1("S0t", 0), o1("S0t", 16), add)
+    ts(o("offi", 0, 15), o("pw0", 0, 15), -1.0, add, 0.0, mx)
+    pick("sl1", "w0", o("offi", 0, 15), ("w0",))
 
-    nxT = o("nxT", 0, 769, k=("nxTb", "nxTz"))
-    xgk = ("xg.0r", "xg.0s", "xg.1r", "xg.1s", "xg.z")
-    ts(xg(0, 0, 15, "xg.0r"), o("m1"), 8, shr)
-    ts(o("g1", 0, 15), o("m1"), 255, band)
-    ts(o("offE", 0, 15, k="offE.r"), xg(0, 0, 15, "xg.0r"), float(-(2 * TN * me + 1)), add, 0.0, mx)
-    tt(xg(1, 0, 15, "xg.1r"), o("g1", 0, 15), o("GC", 0, 15, k=GCk), add)
-    cp(o("rk", 0, N1, k="rk"), ind(nxT, o("offE", 0, 25, k=("offE.r", "offE.s"))))
-    ts(o("sA"), (xgk, T.xg[:, :, 0:26:2]), cc(EV), mul)
-    ts(o("mk1"), o("rk", k=("rk", "rkz")), cc(JF), eq)
-    ts(o("sB"), (xgk, T.xg[:, :, 1:26:2]), cc(OV), mul)
-    scan(o("cn1"), o("ones", 0, W1, k=("ones0", "ones1")), o("mk1"), cc(BASE))
-    tt(o("xh"), o("sA"), o("sB"), add)
-    op("v", lambda: g.vector.tensor_tensor(T.zd1[:], T.mk1[:], T.cn1[:], mul), ("mk1", "cn1"), ("zd1",))
-    cp(o("offGh", 0, 13), (("xh",), T.xh[:, 1, :]))
-    op("v", lambda: g.vector.transpose(T.zt1[:], T.zd1[:]), ("zd1",), ("zt1",))
-    ts(o("offEh", 0, 13), (("xh",), T.xh[:, 0, :]), float(-(2 * TN * me + 1)), add, 0.0, mx)
-    tt(o("plG"), ind(o("gidT"), o("offGh", 0, 13)), o("c1h"), add)
-    fold("1")
-    tt(o("pl1"), ind(nxT, o("offEh", 0, 13)), o("plG"), add)
-    cp(o("off1", 0, 13), o("si1"))
-    scatter(o("S1"), o("off1", 0, 13), o("pl1"))
-    cp(o3("S1d", 0, 16, "S1d.al", 0, 15), o("S1", 0, REM))
-    act(o3("S1d", 16, 32, "S1d.ah", 0, 15), o("S1", 0, REM))
-    ts(o("pad", 0, 31), o("padi", 0, 31, k=PDk), cc(P16), add)
-    op("v", lambda: g.vector.transpose(T.S1t[:, 0:15, :], T.S1d[:, 0:15, :]), ("S1d.al", "S1d.ah"), ("S1ta",))
-    row(o("f3r", 0, 15), "S1t", 0, 15, F3, "S1ta")
-    row(o("sga"), "S1t", 0, 15, SG, "S1ta")
-    tt(o("f3w"), o("f3r", 0, 15), o("pad", 0, 15), mx)
-    lists("f3w", "m2", "am2")
-    row(o("c1a"), "S1t", 0, 15, C1, "S1ta")
-    ts(o("off2", 0, 30, 2), o("sga"), -1.0, add, 0.0, mx)
-    ts(o("off2", 1, 30, 2), o("c1a"), float(N1), add)
-    act(o3("S1d", 16, 32, "S1d.bh", 15, 31), o("S1", REM, N2))
-    pick("sl2", 0, 2 * REM, "A", o("off2"), "sl2", ("Al", "Ah", "Ax"))
-    columns("sl2", "B", BN0, 2 * CAPP, "ac2")
+    def total(f, out):
+        tt((("%sh" % f,), T[f + "h"][:]), (("%si" % f, "%so" % f), T[f][:, 0:3, 0:10]), (("%si" % f, "%so" % f), T[f][:, 3:6, 0:10]), add)
+        tt(o(f + "a"), o2(f + "h", 0), o2(f + "h", 1), add)
+        tt(out, o(f + "a"), o2(f + "h", 2), add)
 
-    cp(o3("S1d", 0, 16, "S1d.bl", 15, 31), o("S1", REM, N2))
-    op("v", lambda: g.vector.transpose(T.S1t[:, 15:31, :], T.S1d[:, 15:31, :]), ("S1d.bl", "S1d.bh"), ("S1tb",))
-    row(o("f3s"), "S1t", 15, 31, F3, "S1tb")
-    row(o("sgb"), "S1t", 15, 31, SG, "S1tb")
-    tt(o("f3p"), o("f3s"), o("pad", 15, 31, k="pad"), mx)
-    row(o("c1b"), "S1t", 15, 31, C1, "S1tb")
+    def before(c, b, A, PMb, x, mask, base, out):
+        ts(o(b), o("ones", 0, 32), c, mul)
+        tr(o(A, 0, 32, k=A), o(b))
+        act(o(A, 32, 64, k=A + "2", p=(64, 96)), o(A, 0, 32, k=A, p=(32, 64)))
+        cp(o(A, 32, 64, k=A + "1", p=(32, 64)), o(A, 0, 32, k=A, p=(0, 32)))
+        cp(o(A, 64, 96, k=A + "3", p=(64, 96)), o(A, 0, 32, k=A, p=(0, 32)))
+        tt(o(PMb), o(A, k=(A, A + "1", A + "2", A + "3")), o("PM"), mul)
+        red(o(x), o(PMb))
+        ts(out, o(x), mask, mul, base, add)
 
-    def decode(f, w, in_):
-        ts(o("g2" + f), in_, (1 << GB) - 1, band)
-        ts(o("h2" + f), in_, GB, shr)
-        cp(o("offg" + f, 0, w), o("g2" + f))
+    def quarters(y, xv, keys):
+        op("v", lambda: g.vector.tensor_tensor(T[y][0:32], T[xv][0:32], T[xv][32:64], add), keys, (y,))
+        op("v", lambda: g.vector.tensor_tensor(T[y][0:32], T[y][0:32], T[xv][64:96], add), keys + (y,), (y,))
 
-    def names(f, w):
-        a = 1 if f == "O" else 0
-        key = "" if f == "L" else ".o"
-        ts(o("c" + f, a, a + w, k="c" + f + key), o("h2" + f), float(ZC - TN * me - 1), add, 0.0, mx)
-        ts(o("r2" + f), o("g2" + f), -(V + 1) / 2.0, add, 1.0 / V, mul)
-        ts(o("a" + f, a, a + w, k="a" + f + key), o("r2" + f), 1.0, add)
-        ts(o("u2" + f), o("r2" + f), float(-V), mul)
-        tt(o("u2" + f), o("u2" + f), o("g2" + f), add)
-        ts(o("b" + f, a, a + w, k="b" + f + key), o("u2" + f), 0.0, mx)
-    decode("O", 16, o("f3p"))
-    ts(o("offc"), o("sgb"), -1.0, add, 0.0, mx)
-    ts(o("offd"), o("c1b"), float(ZC), add)
-    for n in "cab":
-        ms(o(n + "O", 0, 1, k=n + "O.z"), 0)
-    names("O", 16)
-    for j in range(3):
-        ts((("T2",), T.T2[:, :, F3 + j:32:16]), o("kv", 32 * j, 32 * j + 32, k=("kv%da" % j, "kv%db" % j)), cc(P16), add)
-    scatter(o("PT"), o("offgO"), o("ones", 0, M, k=("ones0", "ones1")))
-    op("v", lambda: g.vector.transpose(T.c2t[:], T.T2[:]), ("T2",), ("c2t",))
-    act(o("c2h"), o3("c2t", 0, 16))
-    pick("n2", 0, 272, "x", o("cO", 0, 17, k=("cO.o", "cO.z")), "n2o", ("x",))
-    for n, gd in (("a", "gida"), ("b", "gidb")):
-        act(o(gd, 0, 272, k=gd + ".o"), ind(o("iot", 0, 1024, k=IA), o(n + "O", 0, 17, k=(n + "O.o", n + "O.z"))))
+    def spread(off, zv, keys):
+        for q in range(4):
+            op("v", lambda: g.vector.tensor_copy(T[off][32 * q:32 * q + 32], T[zv][0:32]), keys, (off + "%d" % q,))
+        return tuple(off + "%d" % q for q in range(4))
 
-    decode("L", 15, o("m2"))
-    scatter(o("PT"), o("offgL", 0, 15), o("ones", 0, REM, k=("ones0", "ones1")))
-    names("L", 15)
-    scan(o("PS", 0, GT, k="PS.a"), o("ones", 0, GT, k=("ones0", "ones1")), o("PT", 0, GT), -1.0)
-    PS = o("PS", 0, GT + N2, k=("PS.a", "PS.b"))
-    act(o("pr", REM, N2, k="prO"), ind(PS, o("offgO")))
-    cp(o("pr", 0, REM, k="prL"), ind(PS, o("offgL", 0, 15)))
-    tr(o("prt"), o("pr", k=("prL", "prO", "prz")))
-    cp(o("offP"), o("prt", 0, 512, 32))
-    scatter(o("S2"), o("offP"), o("c2h"))
-    pick("n2", 272, 512, "x", o("cL", 0, 15), "n2l", ("x",))
-    act(o3("S2d", 16, 32, "S2d.h"), o("S2", 0, M))
-    cp(o3("S2d", 0, 16, "S2d.l"), o("S2", 0, M))
-    op("v", lambda: g.vector.transpose(T.S2t[:], T.S2d[:]), ("S2d.l", "S2d.h"), ("S2t",))
-    off = [h("offF", 16 * k, 16 * k + 16, "%d" % k) for k in range(3)]
-    ga = [h("ga", 16 * k, 16 * k + 16, "%d" % k) for k in range(3)]
-    row(ga[0], "S2t", 0, 16, F3, "S2t")
-    row(ga[1], "S2t", 0, 16, F3 + 1, "S2t")
-    cp(off[0], ga[0])
-    row(ga[2], "S2t", 0, 16, F3 + 2, "S2t")
-    cp(off[1], ga[1])
-    cp(off[2], ga[2])
-    pick("p2", 0, M, "n2", off[0], "p2", ("n2o", "n2l"))
+    total("L1", o("L1b"))
+    ts(o("offE"), o("L1b"), float(-2 * TN * me), add, float(2 * TN + 1), mn)
+    nxT = o("nxT", k=("nxTa", "nxTz", "nxTy"))
+    ts(o("ia"), o("L1b"), -(TN + 0.5), add, 0.5 / TN, mul)
+    cp(o("rk"), ind(nxT, o("offE")))
+    ts(o("offA"), o("ia"), 1.0, add)
+    ts(o3("nd1", 0, 16, "nd1l"), o("rk"), cc(EV), mul)
+    act(o3("nd1", 16, 32, "nd1h"), o("rk"), scale=cc(OV))
+    ts(o("rr"), o("rk"), -(TN + 1) / 2.0, add, 1.0 / TN, mul)
+    tr((("nt1",), T.nt1[:]), (("nd1l", "nd1h"), T.nd1[:]))
+    ts(o("PM"), o("io6"), cc(J), eq)
+    tt((("L2o",), T.L2[:, me, 0:10]), o1("nt1", 0), o1("nt1", 16), add)
+    everyone("L2", "am2")
+    columns("sl1", "A", 0, CAPP, "ac1")
+    iota(o("XA"), [[0, 96]])
+    iota(o("YA"), [[0, 96]])
+    iota(o("idtab", 0, 1, k="idz"), [[0, 1]], -1)
+    iota(o("idtab", 1, 961, k="idn"), [[0, N], [1, V]])
+    iota(o("idtab", 1, 961, k="idn", p=(0, 1)), [[1, N], [0, V]])
+
+    tr(o("RT"), (allR, T.Rt[:]))
+    act(cc(X5), cc(A1), Ident, scale=-1.0, bias=R(R_M))
+    act(cc(X6), cc(A1), Ident, scale=-1.0, bias=R(R_E))
+    act(cc(BASE1), cc(A5), Ident, bias=R(R_B1))
+    ts(o("PM", 0, 16, k="PM"), o("PM", 0, 16, k="PM"), cc(OV), mul)
+    ts(o("tabA"), o("iot", 0, 16, k="iota"), cc(J1), ne, R(R_K1), mul)
+    ts(o("pw0"), o("iot", 0, 16, k="iota"), float(me + 1), eq, R(R_K2), mul)
+    ms(o("PM", 16, 32, k="PM"), 0.0)
+    ts(o("mk1"), o("rr"), cc(X5), mn, cc(X6), eq)
+    tt(o("tabA"), o("tabA"), o("pw0"), add)
+    red(o("x1"), o("mk1"))
+
+    before(o("x1"), "xb", "XA", "XM", "p1", R(R_RM), cc(BASE1), o("q1"))
+    act(o("ctab", 1, 769, k="cta"), o("ctb"), Ident, scale=oh(FN1), bias=R(R_CB))
+    act(o("S1", 0, REM, k="S1"), o("iot", 0, REM, k="iota"), scale=0.0)
+    act(o("tabA"), o("tabA"), Ident, bias=R(R_K3))
+    scan(o("cn1"), o("ones"), o("mk1"), o("q1"))
+    tt(o("z1"), o("mk1"), o("cn1"), mul)
+    ts(o3("zd1", 0, 16, "zd1l"), o("z1"), cc(EV), mul)
+    act(o3("zd1", 16, 32, "zd1h"), o("z1"), scale=cc(OV))
+    tt(o("pay1"), ind(o("ctab", k=("cta", "ctabz", "ctaby")), o("offE")), o("cn1"), add)
+    tr((("zt1",), T.zt1[:]), (("zd1l", "zd1h"), T.zd1[:]))
+    tt(o3("fa1"), o3("zt1", 0, 8), o3("zt1", 16, 24), add)
+    tt(o3("fb1"), o3("fa1", 0, 4), o3("fa1", 4, 8), add)
+    tt(o3("fc1"), o3("fb1", 0, 2), o3("fb1", 2, 4), add)
+    act(o("M1b"), ind(o("tabA"), o("offA")))
+    act(o("E0"), o("pay1"), scale=R(R_RB))
+    tt(o("fd1"), o1("fc1", 0), o1("fc1", 1), add)
+    cp(o("off1"), o("fd1"))
+    scatter(o("S1"), o("off1"), o("pay1"))
+    act(o3("S1d", 16, 32, "S1dh"), o("S1", 0, REM))
+    cp(o3("S1d", 0, 16, "S1dl"), o("S1", 0, REM))
+    tt(o("E"), o("E0"), o("M1b"), mn)
+    tr((("S1t",), T.S1t[:]), (("S1dl", "S1dh"), T.S1d[:]))
+    for k, j in ((0, FN0), (1, FN1)):
+        tt((("X1%d" % k,), T.X1[:, :, k, :]), o1("S1t", j), o1("S1t", j + 16), add)
+    quarters("Y1", "X1", ("X10", "X11"))
+    ts((("Z1a",), T.Z1[0:32, :, 0, :]), (("Y1",), T.Y1[0:32, :, 0, :]), float(-BA), add)
+    ts((("Z1b",), T.Z1[0:32, :, 1, :]), (("Y1",), T.Y1[0:32, :, 1, :]), float(N1 - BX + CAPP), add)
+    k2 = spread("off2", "Z1", ("Z1a", "Z1b"))
+    act(o("ztab", 1, 385, k="zta"), o("iot", 0, TN, k="iota"), Ident, scale=oh(FN2), bias=R(R_ZB))
+    act(o("ztab", 0, 1, k="ztz"), oh(7))
+    act(o("ztab", 385, 386, k="zty"), oh(7))
+    act(o("S2", 0, M, k="S2"), o("iot", 0, M, k="iota"), scale=0.0)
+    pick("sl2", "A", (k2, T.off2[:]), ("Al", "Aw", "Ax"))
+    columns("sl2", "B", BL, 2 * CAPP, "ac2")
+    move("B", BA, "A", 0, REM, "Al", "Ba", "dAB")
+
+    total("L2", o("L2b"))
+    ts(o("offN"), o("L2b"), float(-TN * me), add, float(TN + 1), mn)
+    wq(0)
+    tt(o("r2"), ind(o("ztab", 0, 392, k=("zta", "ztz", "zty")), o("offN")), o("E"), add)
+    tt(o("mk2"), o("r2"), o("M1b"), gt)
+    red(o("x2"), o("mk2"))
+    before(o("x2"), "yb", "YA", "YM", "p2", R(R_RM), R(R_B2), o("q2"))
+    wq(1)
+    scan(o("cn2"), o("ones"), o("mk2"), o("q2"))
+    tt(o("z2"), o("mk2"), o("cn2"), mul)
+    wq(2)
+    ts(o3("zd2", 0, 16, "zd2l"), o("z2"), cc(EV), mul)
+    act(o3("zd2", 16, 32, "zd2h"), o("z2"), scale=cc(OV))
+    tt(o("pay2"), o("z2"), o("r2"), add)
+    tr((("zt2",), T.zt2[:]), (("zd2l", "zd2h"), T.zd2[:]))
+    tt(o3("ta2"), o3("zt2", 6, 8), o3("zt2", 22, 24), add)
+    wq(3)
+    tt(o("tb2"), o1("ta2", 0), o1("ta2", 1), add)
+    wq(4)
+    cp(o("off20"), o("tb2"))
+    wq(5)
+    scatter(o("S2"), o("off20"), o("pay2"))
+    act(o3("S2d", 16, 32, "S2dh"), o("S2", 0, M))
+    cp(o3("S2d", 0, 16, "S2dl"), o("S2", 0, M))
+    tr((("S2t",), T.S2t[:]), (("S2dl", "S2dh"), T.S2d[:]))
+    tt(o3("ga"), o3("S2t", 0, 3), o3("S2t", 3, 6), add)
+    tt(o3("gb"), o3("S2t", 16, 19), o3("S2t", 19, 22), add)
+    tt(o2("n01", 0, "n0"), o1("S2t", FN0), o1("S2t", FN0 + 16), add)
+    tt(o3("gc"), o3("ga"), o3("gb"), add)
+    tt(o2("n01", 1, "n1"), o1("S2t", FN1), o1("S2t", FN1 + 16), add)
+    tt(o("gd"), o1("gc", 0), o1("gc", 1), add)
+    tt(o2("X2", 2, "X22"), o1("S2t", FN2), o1("S2t", FN2 + 16), add)
+    tt(o("ge2"), o("gd"), o1("gc", 2), add)
+    tt(o2("X2", 3, "X23"), o1("S2t", FID), o1("S2t", FID + 16), add)
+    tt(o2("X2", 0, "X20"), o2("n01", 0, "n0"), o("ge2"), add)
+    tt(o2("X2", 1, "X21"), o2("n01", 1, "n1"), o("ge2"), add)
+    quarters("Y2", "X2", ("X20", "X21", "X22", "X23"))
+    q0 = (0, 32)
+    ts(o2("Y2", 0, "Y2n", p=q0), o2("Y2", 0, p=q0), -float(N), add)
+    ts(o2("Y2", 1, "Y2m", p=q0), o2("Y2", 1, p=q0), float(CAPP - N), add)
+    kF = spread("offF", "Y2", ("Y2", "Y2n", "Y2m"))
+    off = [(kF, T.offF[:, 16 * k:16 * k + 16]) for k in range(4)]
 
     def product(k, last):
         n = "p%d" % k
         for oo in range(NO):
             a = 128 * (k * NO + oo)
             op("k", lambda: g.tensor.matmul_mx(T["ps_%d" % oo][:, 0:M], T.wq[:, a:a + 128], T.ws[:, a:a + 128], T[n + "q"][:], T[n + "s"][:], k == 2, last),
-               ("waq", "was", "wbq", "wbs", n + "q", n + "s"), ("ps_%d" % oo,) if last else ())
-    quant("w", 0, 384, "wt", 0, 384, ("wt",), "wa")
-    quant("w", 384, 768, "wt", 384, 768, ("wt",), "wb")
-    quant("B", 0, ZC, "xt", 0, ZC, ("xtz",), "Bz")
+               ("w%dq" % (k * NO + oo), "w%ds" % (k * NO + oo), n + "q", n + "s"), ("ps_%d" % oo,) if last else ())
+    pick("p2", "B", off[2], ("Bx",), ZC + TN)
     product(2, False)
-    pick("B", BH0, BH1, "A", o("offc"), "Bh0", ("Al", "Ah", "Ax"))
-    pick("B", BH1, BW, "x", o("offd"), "Bh1", ("x",))
-    Bk = ("Bz", "Bl", "Bh0", "Bh1")
-    for n, gd in (("a", "gida"), ("b", "gidb")):
-        act(o(gd, 272, 512, k=gd + ".l"), ind(o("iot", 0, 1024, k=IA), o(n + "L", 0, 15)))
-    pick("p0", 0, M, "B", off[1], "p0", Bk)
+    Bk = ("Bx", "Ba", "Bw", "Bl")
+    pick("p0", "B", off[0], Bk)
     product(0, False)
-    pick("p1", 0, M, "B", off[2], "p1", Bk)
+    pick("p1", "B", off[1], Bk)
     product(1, True)
-    for j, gd in ((0, "gida"), (1, "gidb")):
-        act(h("idt", M * j, M * j + M, "%d" % j), ind(o(gd, k=(gd + ".o", gd + ".l")), off[0]), Ident, bias=-1.0)
+    act(o("idt"), ind(o("idtab", k=("idz", "idn")), off[3]))
     cp(o("yo0"), o("ps_0", 0, M))
     act(o("yo1"), o("ps_1", 0, M))
     dma("y", (("y0",), T.y[:, 0:M]), o("yo0"), "dy0")
     dma("s", (("y1",), T.y[:, M:2 * M]), o("yo1"), "dy1")
-    op("y", lambda: g.sync.dma_start(T["id"][:], T.idt[0:1, :]), ("idt.0", "idt.1"), ("ido",), sem="did", inc=16)
+    op("y", lambda: g.sync.dma_start(T["id"][:], T.idt[0:2, :]), ("idt",), ("ido",), sem="did", inc=16)
     for sem, c in count.items():
         if know["p"].get(sem, 0) < c:
             g.wait_ge(T.sem[sem], c)

from concourse.bass import DstId, RemoteDMATransfer
from concourse.mybir import dt, AluOpType, AxisListType, ActivationFunctionType

N, TN, V, M, CAPP, NO = 6, 384, 160, 256, 48, 2
REM = CAPP * (N - 1)
N1 = REM + V
ZC = 128
BX, BA = ZC, ZC + TN
BL = BA + N1
BW = BL + 2 * REM
T1 = REM + M
FN0, FN1, FN2, FID = 8, 9, 10, 11

_F, _I, _U, _C, _S = "float32", "int32", "uint16", "float8_e4m3fn_x4", "uint8"
SCRATCH, POOL = {}, {}


def _add(dtype, **shapes):
    for name, shape in shapes.items():
        SCRATCH[name] = ("sbuf", [128] + (list(shape) if isinstance(shape, tuple) else [shape]), dtype)


def _pool(buf, dtype, **widths):
    at = 0
    for name, w in widths.items():
        POOL[name] = (buf, at, w)
        at += w
    _add(dtype, **{buf: at})


_add(_I, ci=8, st0=10, bt0=10, btg=10, stA=10, nxr=768, nxA=48)
_add(_F, cc=48, oh=16, ones=V, iot=2304, nxT=776, ctab=776, ctb=768, ztab=400, tabA=16, io6=96, PM=96)
_add(_F, Rt=(12, 2, 16), RT=384)
_add(_F, n1r=V, nxa=V, nd0=(10, 32), nt0=(10, 32), S0=800, S0t=(15, 32))
_add(_U, offe=10, offS=10, off0=10, offi=16, nxo=48)
_add(_I, ai0=V)
_add(_F, mk0=V, cn0=V, zd0=(10, 32), zt0=(10, 32), za0=(10, 4), zb0=(10, 2))
_add(_F, L1=(6, 12), L1h=(3, 10), L2=(6, 12), L2h=(3, 10))
_add(_U, offE=10, offA=10, offN=10)
_add(_I, rr=V, ia=10)
_add(_F, rk=V, nd1=(10, 32), nt1=(10, 32), M1b=V, mk1=V, cn1=V, z1=V, zd1=(10, 32), zt1=(10, 32), pay1=V, E0=V, E=V, S1=T1 + V,
     S1d=(15, 32), S1t=(15, 32), X1=(5, 2, 3), Y1=(5, 2, 3), Z1=(5, 2, 3))
_add(_F, xb=32, XA=96, XM=96, yb=32, YA=96, YM=96, fa1=(10, 8), fb1=(10, 4), fc1=(10, 2))
_add(_U, off1=10, off2=30)
_add(_F, r2=V, mk2=V, cn2=V, z2=V, zd2=(10, 32), zt2=(10, 32), ta2=(10, 2), pay2=V, S2=M + V, S2d=(16, 32), S2t=(16, 32),
     ga=(16, 3), gb=(16, 3), gc=(16, 3), n01=(2, 16), X2=(4, 16), Y2=(4, 16), idtab=968, idt=M, yo0=M, yo1=M)
_add(_U, off20=10, offF=64)
_pool("pooli", _I, i0=40, si0=10, k0=10, h0=10)
_pool("poolf", _F, e0=60, b1g=10, u0=10, x1=1, x2=1, p1=1, p2=1, q1=1, q2=1, pw0=16, L1a=10, L1b=10, L2a=10, L2b=10,
      fd1=10, tb2=10, gd=16, ge2=16)
_add("bfloat16", xt=4 * (ZC + TN), wt=3072)
for _n, _w in (("x", ZC + TN), ("w", 768), ("w0", V), ("sl1", REM), ("A", N1 + TN), ("sl2", 2 * REM), ("B", BW),
               ("p0", M), ("p1", M), ("p2", M)):
    SCRATCH[_n + "q"] = ("sbuf", [128, _w], _C)
    SCRATCH[_n + "s"] = ("sbuf", [128, _w], _S)
SCRATCH["ps_0"] = ("psum", [128, 512], _F)
SCRATCH["ps_1"] = ("psum", [128, 512], _F)

SEMAPHORES = ["qv", "qs", "qp", "qk", "dst0", "dbt0", "dbtg", "dnx", "dstA", "dnxA", "dx", "dw", "dxA", "dxB", "dwA", "dwB", "dAB",
              "did", "dy0", "dy1", "am1", "ac1", "am2", "ac2", "loc"]

add, sub, mul, mx, mn = AluOpType.add, AluOpType.subtract, AluOpType.mult, AluOpType.max, AluOpType.min
eq, ge, gt, lt, ne = AluOpType.is_equal, AluOpType.is_ge, AluOpType.is_gt, AluOpType.is_lt, AluOpType.not_equal
shr, band = AluOpType.arith_shift_right, AluOpType.bitwise_and
Copy, Ident = ActivationFunctionType.Copy, ActivationFunctionType.Identity


def pos(a, q):
    return q if q < a else q - 1


def rank_program(g, core, T, topo):
    me = T.rank_of(core)
    if me is None:
        return
    others = [(me + 1 + k) % N for k in range(N - 1)]

    eng = {"v": g.vector, "s": g.scalar, "p": g, "k": g.tensor, "y": g.sync}
    know = {q: {} for q in eng}
    count, wr, rd = {"loc": 0}, {}, {}

    def need(q, evs):
        for sem, val, snap in sorted(evs, key=lambda e: -len(e[2])):
            if know[q].get(sem, 0) < val:
                eng[q].wait_ge(T.sem[sem], val)
                for a, b in list(snap.items()) + [(sem, val)]:
                    if know[q].get(a, 0) < b:
                        know[q][a] = b

    def op(q, call, reads=(), writes=(), sem="", inc=1, total=None):
        evs = []
        for k in reads:
            evs += wr.get(k, [])
        for k in writes:
            evs += wr.get(k, []) + rd.get(k, [])
        best = {}
        for e in evs:
            if e[0] not in best or best[e[0]][1] < e[1]:
                best[e[0]] = e
        need(q, list(best.values()))
        ins = call()
        if sem is None:
            return
        sem = sem or "q" + q
        ins.then_inc(T.sem[sem], inc)
        count[sem] = count.get(sem, 0) + inc
        ev = (sem, total or count[sem], dict(know[q]))
        for k in writes:
            wr[k] = [ev]
            rd[k] = []
        for k in reads:
            rd.setdefault(k, []).append(ev)

    def o(name, lo=None, hi=None, st=None, k=None, p=None):
        ps = slice(None) if p is None else slice(p[0], p[1])
        keys = (k,) if isinstance(k, str) else k or (name,)
        if name in POOL:
            name, at, w = POOL[name]
            lo, hi = at + (lo or 0), at + (w if hi is None else hi)
        return (keys, T[name][ps, slice(lo, hi, st)])

    def o3(name, lo=None, hi=None, k=None, p=None):
        ps = slice(None) if p is None else slice(p[0], p[1])
        return ((k,) if isinstance(k, str) else k or (name,), T[name][ps, :, slice(lo, hi)])

    def o1(name, j, k=None):
        return ((k or name,), T[name][:, :, j])

    def o2(name, j, k=None, p=None):
        ps = slice(None) if p is None else slice(p[0], p[1])
        return ((k or name,), T[name][ps, j, :])

    def ci(j):
        return o("ci", j, j + 1, k="ci%d" % j)

    def cc(j):
        return o("cc", j, j + 1, k="cc%d" % j)

    def oh(j):
        return o("oh", j, j + 1)

    def ind(win, off):
        return (win[0] + off[0], win[1].indirect(off[1]))

    def cp(out, in_):
        op("v", lambda: g.vector.tensor_copy(out[1], in_[1]), in_[0], out[0])

    def ms(out, c):
        op("v", lambda: g.vector.memset(out[1], c), (), out[0])

    def tt(out, a, b, f):
        op("v", lambda: g.vector.tensor_tensor(out[1], a[1], b[1], f), a[0] + b[0], out[0])

    def ts(out, a, s1, f1, s2=None, f2=None):
        rk = a[0] + (s1[0] if isinstance(s1, tuple) else ()) + (s2[0] if isinstance(s2, tuple) else ())
        v1 = s1[1] if isinstance(s1, tuple) else s1
        v2 = s2[1] if isinstance(s2, tuple) else s2
        if f2 is None:
            op("v", lambda: g.vector.tensor_scalar(out[1], a[1], v1, None, f1), rk, out[0])
        else:
            op("v", lambda: g.vector.tensor_scalar(out[1], a[1], v1, v2, f1, f2), rk, out[0])

    def scan(out, d0, d1, init):
        op("v", lambda: g.vector.tensor_tensor_scan(out[1], d0[1], d1[1], init[1], mul, add), d0[0] + d1[0] + init[0], out[0])

    def red(out, in_):
        op("v", lambda: g.vector.tensor_reduce(out[1], in_[1], AxisListType.X, add), in_[0], out[0])

    def tr(out, in_):
        op("v", lambda: g.vector.transpose(out[1], in_[1]), in_[0], out[0])

    def act(out, in_, f=Copy, scale=None, bias=None):
        kw, rk = {}, ()
        for n, v in (("scale", scale), ("bias", bias)):
            if isinstance(v, tuple):
                rk, v = rk + v[0], v[1]
            if v is not None:
                kw[n] = v
        op("s", lambda: g.scalar.activation(out[1], in_[1], f, **kw), in_[0] + rk, out[0])

    def scatter(win, off, in_):
        op("v", lambda: g.vector.tensor_copy(win[1].indirect(off[1]), in_[1]), win[0] + off[0] + in_[0], win[0])

    def pick(outn, winn, off, wkeys, hi=None):
        op("v", lambda: g.vector.tensor_copy(T[outn + "q"][:].bitcast(dt.uint32), T[winn + "q"][:, 0:hi].bitcast(dt.uint32).indirect(off[1])),
           tuple(x + "q" for x in wkeys) + off[0], (outn + "q",))
        op("s", lambda: g.scalar.activation(T[outn + "s"][:], T[winn + "s"][:, 0:hi].indirect(off[1]), Copy),
           tuple(x + "s" for x in wkeys) + off[0], (outn + "s",))

    def quant(outn, lo, hi, src, a, b, skeys, key):
        op("v", lambda: g.vector.quantize_mx(T[outn + "q"][:, lo:hi], T[outn + "s"][:, lo:hi], T[src][:, 4 * a:4 * b]), skeys, (key + "q", key + "s"))

    def wq(j):
        quant("w", 128 * j, 128 * j + 128, "wt", 128 * j, 128 * j + 128, ("wt",), "w%d" % j)

    def move(outn, at, srcn, lo, hi, rkey, key, sem):
        op("y", lambda: g.sync.dma_start(T[outn + "q"][:, at:at + hi - lo].bitcast(dt.uint8), T[srcn + "q"][:, lo:hi].bitcast(dt.uint8)),
           (rkey + "q",), (key + "q",), sem=sem, inc=16, total=32)
        op("y", lambda: g.sync.dma_start(T[outn + "s"][:, at:at + hi - lo], T[srcn + "s"][:, lo:hi]), (rkey + "s",), (key + "s",), sem=sem, inc=16, total=32)

    def fan(reads, src, dst, rsem):
        def call():
            trs = []
            for k, q in enumerate(others[:4]):
                c = T.cores[q]
                rid, pid, _ = topo.addr(c)
                m = sum(1 << e for e in topo.engines(core, c)[k::4])
                trs.append(RemoteDMATransfer(dst_ids=[DstId(rid=rid, pnc=pid)], dma_engine_mask=m, remote_sem=T.sem[rsem], src=src(q), dst=dst(q)))
            g.remote_dma_fused(trs, local_sem=T.sem.loc)
            c = T.cores[others[4]]
            rid, pid, _ = topo.addr(c)
            g.remote_dma(dst(others[4]), src(others[4]), T.sem[rsem], T.sem.loc, pid, rid, topo.mask(core, c))
        op("p", call, reads, (), sem=None)
        count["loc"] += 16

    def everyone(name, rsem):
        fan((name + "o",), lambda q: T[name][:, me, 0:10], lambda q: T[name][:, me, 0:10], rsem)

    def columns(name, land, at, w, rsem):
        def src(n, q):
            return T[n][:, w * pos(me, q):w * pos(me, q) + w]

        def dst(n, q):
            return T[n][:, at + w * pos(q, me):at + w * pos(q, me) + w]
        fan((name + "q",), lambda q: src(name + "q", q).bitcast(dt.uint8), lambda q: dst(land + "q", q).bitcast(dt.uint8), rsem)
        fan((name + "s",), lambda q: src(name + "s", q), lambda q: dst(land + "s", q), rsem)

    for s_, v_, ks in (("am1", 16, ("L1i",)), ("ac1", 32, ("Alq", "Als")), ("am2", 16, ("L2i",)), ("ac2", 32, ("Blq", "Bls"))):
        count[s_] = v_
        for k in ks:
            wr[k] = [(s_, v_, {})]

    def dma(q, out, in_, sem, total=None):
        op(q, lambda: eng[q].dma_start(out[1], in_[1]), in_[0], out[0], sem=sem, inc=16, total=total)

    P = (0, 16)
    dma("y", o("st0", p=P), ((), T.st[:]), "dst0")
    dma("s", o("bt0", p=P), ((), T.bt[:]), "dbt0")
    ms(o("nxr"), 0)
    dma("y", o("nxr", p=(0, 1)), ((), T.nx[:]), "dnx")
    dma("y", o("xt", 4 * ZC, 4 * (ZC + TN), k="xtx"), ((), T.x[:]), "dx")
    ms(o("btg"), 0)
    for k in range(8):
        dma("y", o("stA", p=(16 * k, 16 * k + 16), k="stA%d" % k), ((), T.st[:]), "dstA", 128)
    dma("y", o("btg", p=(16 * me, 16 * me + 16)), ((), T.bt[:]), "dbtg")
    for k in range(8):
        dma("y", o("nxA", p=(16 * k, 16 * k + 16), k="nxA%d" % k), ((), T.nx[:]), "dnxA", 128)
    stA = (tuple("stA%d" % k for k in range(8)), T.stA[:])
    nxA = (tuple("nxA%d" % k for k in range(8)), T.nxA[:])
    dma("y", o("wt"), ((), T.w[:]), "dw")

    def iota(out, pattern, base=0, mult=0):
        op("p", lambda: g.iota(out[1], pattern, base, mult, allow_small_or_imprecise_dtypes=True), (), out[0])
    iotk = ("iota", "iotb", "iotc", "iotd", "iote")
    (R_M, R_E, R_B1, R_RM, R_B2, R_ZB, R_CB, R_RB, R_K1, R_K2, R_K3, R_J) = range(12)
    allR = tuple("R%d" % c for c in range(12))
    iota(ci(0), [[1, 1]], 0, 1)
    iota(o("iot", 0, 512, k="iota"), [[1, 512]])
    iota((("R%d" % R_J,), T.Rt[:, R_J, :, :]), [[0, 2], [1, 16]])
    iota((allR[:R_J], T.Rt[:, 0:R_J, :, :]), [[0, 32 * R_J]])
    (JF, J, G, OD, EV, OV, X1, X2, X3, X4, GM, GM2, BASE0, BASE1, J1, A1, A2, A3, A4, A5, X5, X6, GV) = range(23)
    hh = 16 * (me % 2)
    ms(o("offe"), 0)
    ts(ci(1), ci(0), 31, band)
    ts(ci(2), ci(0), 15, band)
    ts(ci(3), ci(0), 4, shr)
    ms(o("ones"), 1.0)
    cp(cc(JF), ci(1))
    cp(cc(J), ci(2))
    cp(cc(G), ci(3))
    ms(o3("nd0", 16 - hh, 32 - hh, "nd0z"), 0.0)

    def R(c):
        return o("RT", 32 * c, 32 * c + 1)

    def rows(c, a, b, v):
        act((("R%d" % c,), T.Rt[:, c, :, a:b]), o("iot", 0, 2 * (b - a), k="iota"), Ident, scale=0.0, bias=float(v))

    def steps(c, a, b, m, v):
        if b > a:
            act((("R%d" % c,), T.Rt[:, c, :, a:b]), (("R%d" % R_J,), T.Rt[:, R_J, :, a:b]), Ident, scale=float(m), bias=float(v))
    rows(R_M, 0, 16, 99)
    rows(R_M, 8, 9, 0)
    rows(R_M, 11, 12, -1)
    steps(R_E, 0, 6, 1, 0)
    for a_, b_, v_ in ((me, me + 1, 77), (6, 7, me), (7, 8, -1), (9, 16, 77), (11, 12, -1)):
        rows(R_E, a_, b_, v_)
    for c, w_, at_ in ((R_B1, CAPP, 0), (R_B2, 2 * CAPP, BL)):
        steps(c, 0, me, w_, at_ - 1)
        steps(c, me + 1, N, w_, at_ - w_ - 1)
    for c, a_, b_, v_ in ((R_B1, 6, 7, REM - 1), (R_B1, 7, 8, T1 - 1), (R_B1, 8, 9, BA - 1), (R_RM, 0, 7, 1), (R_B2, 6, 7, -1), (R_B2, 7, 8, M - 1),
                          (R_ZB, 0, 7, 1), (R_ZB, FN2, FN2 + 1, BX), (R_CB, FN1, FN1 + 1, BX - CAPP), (R_RB, 8, 10, 1), (R_RB, 11, 12, 1),
                          (R_K1, 0, 6, 1000), (R_K2, me, me + 1, 1000), (R_K2, 8, 10, 1000000), (R_K3, 10, 16, 1000000)):
        rows(c, a_, b_, v_)

    def i0(j):
        return o("i0", 10 * j, 10 * j + 10, k="i0%d" % j, p=P)

    def e0(j):
        return o("e0", 10 * j, 10 * j + 10, k="e0%d" % j, p=P)
    ts(i0(1), o("st0", p=P), 3, shr)
    ts(e0(1), o("st0", p=P), 96.0, mul)
    ts(i0(0), o("bt0", p=P), 1, band)
    ts(e0(3), i0(1), -767.0, mul)
    ts(e0(2), i0(0), 48.0, mul)
    tt(e0(4), e0(1), e0(3), add)
    ts(cc(GM), cc(G), float(me), eq)
    tt(e0(4), e0(4), e0(2), add)
    ts(cc(X2), cc(JF), float(me), gt, -48.0, mul)
    cp(o("offe", p=P), e0(4))
    ts(cc(X3), cc(JF), float(me), eq, float(REM - CAPP * me), mul)
    cp(o("n1r"), ind(o("nxr"), o("offe")))
    op("p", lambda: g.partition_broadcast(T.nxa[:], T.n1r[0:1, :], 128), ("n1r",), ("nxa",))
    ts(cc(X1), cc(JF), 48.0, mul, -1.0, add)
    tt(cc(X2), cc(X2), cc(X3), add)
    ts(cc(X4), cc(JF), 6.0, eq, 256.0, mul)
    tt(cc(X1), cc(X1), cc(X2), add)
    i4 = o("i0", 30, 40, k="i03")
    ts(i4, o("btg"), 1, shr)
    ts(cc(OD), cc(JF), 16.0, ge, 16.0, mul)
    tt(cc(BASE0), cc(X1), cc(X4), add)
    ts(o("b1g"), i4, 1.0, add, cc(GM), mul)
    ts(cc(GM2), cc(GM), 2.0, mul)
    ts(cc(EV), cc(JF), 16.0, lt)
    ts(cc(OV), cc(JF), 16.0, ge)
    ts(cc(GV), cc(G), float(V), mul)
    ts(cc(A2), cc(G), float(me), gt, -48.0, mul)
    cp(o3("nd0", hh, hh + 16, "nd0x"), o("nxa"))
    ts(o("ai0"), o("nxa"), -191.5, add, 1.0 / TN, mul)
    tr((("nt0",), T.nt0[:]), (("nd0x", "nd0z"), T.nd0[:]))
    ts(o("mk0"), o("ai0"), cc(JF), eq)
    ts(o("u0"), o1("nt0", 0), cc(GM2), mul)
    scan(o("cn0"), o("ones"), o("mk0"), cc(BASE0))
    tt((("L1o",), T.L1[:, me, 0:10]), o("u0"), o("b1g"), add)
    everyone("L1", "am1")
    iota(o("S0", 0, 480, k="S0"), [[0, 480]])
    cp(o("nxo"), nxA)
    tt(o3("zd0", 0, 16, "zd0l"), o("mk0"), o("cn0"), mul)
    act(o3("zd0", 16, 32, "zd0h"), o3("zd0", 0, 16, "zd0l"))
    ms(o("xt", 0, 4 * ZC, k="xtz"), 0.0)
    tr((("zt0",), T.zt0[:]), (("zd0l", "zd0h"), T.zd0[:]))
    ts(o("offS"), stA, float(ZC), add)
    tt(o3("za0", 0, 4), o3("zt0", 0, 4), o3("zt0", 4, 8), add)
    ts(o("oh"), o("iot", 0, 16, k="iota"), cc(J), eq)
    tt(o3("zb0", 0, 2), o3("za0", 0, 2), o3("za0", 2, 4), add)
    ts(cc(J1), cc(J), 1.0, add)
    tt(o("si0"), o1("zb0", 0), o1("zb0", 1), add)
    quant("x", 0, ZC + TN, "xt", 0, ZC + TN, ("xtx", "xtz"), "x")
    ts(o("k0"), o("si0"), 496, band)
    for n in ("nxT", "ctab"):
        act(o(n, 0, 1, k=n + "z"), o("iot", 0, 1, k="iota"))
        act(o(n, 769, 776, k=n + "y"), o("iot", 0, 7, k="iota"), scale=0.0)
    act(o("iot", 512, 1024, k="iotb"), o("iot", 0, 512, k="iota"), Ident, bias=512.0)
    act(o("iot", 1024, 1536, k="iotc"), o("iot", 0, 512, k="iota"), Ident, bias=1024.0)
    act(o("iot", 1536, 2048, k="iotd"), o("iot", 0, 512, k="iota"), Ident, bias=1536.0)
    act(o("iot", 2048, 2304, k="iote"), o("iot", 0, 256, k="iota"), Ident, bias=2048.0)
    act(o("nxT", 1, 769, k="nxTa"), ind(o("iot", k=iotk), o("nxo")), Ident, bias=1.0)
    tt(o("h0"), o("si0"), o("k0"), add)
    pick("w0", "x", o("offS"), ("x",))
    ts(o("off0"), o("h0"), cc(OD), add)
    iota(o("ctb"), [[1, TN], [0, 2]])
    iota(o("io6"), [[0, 6], [1, 16]])
    move("A", N1, "x", ZC, ZC + TN, "x", "Ax", "dxA")
    move("B", 0, "x", 0, ZC + TN, "x", "Bx", "dxB")
    move("A", REM, "w0", 0, V, "w0", "Aw", "dwA")
    move("B", BA + REM, "w0", 0, V, "w0", "Bw", "dwB")
    scatter(o("S0"), o("off0"), o("iot", 1, V + 1, k="iota"))
    act(cc(A1), cc(GM), scale=oh(8))
    act(cc(A3), cc(G), Ident, scale=48.0, bias=cc(A2))
    act(cc(X3), cc(GV), scale=oh(11))
    act(cc(A4), cc(GM), Ident, scale=float(REM - CAPP * me), bias=cc(A3))
    act(cc(A5), cc(A4), Ident, scale=oh(8), bias=cc(X3))
    op("v", lambda: g.vector.transpose(T.S0t[:], T.S0[:, 0:480]), ("S0",), ("S0t",))
    tt(o("pw0", 0, 15), o1("S0t", 0), o1("S0t", 16), add)
    ts(o("offi", 0, 15), o("pw0", 0, 15), -1.0, add, 0.0, mx)
    pick("sl1", "w0", o("offi", 0, 15), ("w0",))

    def total(f, out):
        tt((("%sh" % f,), T[f + "h"][:]), (("%si" % f, "%so" % f), T[f][:, 0:3, 0:10]), (("%si" % f, "%so" % f), T[f][:, 3:6, 0:10]), add)
        tt(o(f + "a"), o2(f + "h", 0), o2(f + "h", 1), add)
        tt(out, o(f + "a"), o2(f + "h", 2), add)

    def before(c, b, A, PMb, x, mask, base, out):
        ts(o(b), o("ones", 0, 32), c, mul)
        tr(o(A, 0, 32, k=A), o(b))
        act(o(A, 32, 64, k=A + "2", p=(64, 96)), o(A, 0, 32, k=A, p=(32, 64)))
        cp(o(A, 32, 64, k=A + "1", p=(32, 64)), o(A, 0, 32, k=A, p=(0, 32)))
        cp(o(A, 64, 96, k=A + "3", p=(64, 96)), o(A, 0, 32, k=A, p=(0, 32)))
        tt(o(PMb), o(A, k=(A, A + "1", A + "2", A + "3")), o("PM"), mul)
        red(o(x), o(PMb))
        ts(out, o(x), mask, mul, base, add)

    def quarters(y, xv, keys):
        op("v", lambda: g.vector.tensor_tensor(T[y][0:32], T[xv][0:32], T[xv][32:64], add), keys, (y,))
        op("v", lambda: g.vector.tensor_tensor(T[y][0:32], T[y][0:32], T[xv][64:96], add), keys + (y,), (y,))

    def spread(off, zv, keys):
        for q in range(4):
            op("v", lambda: g.vector.tensor_copy(T[off][32 * q:32 * q + 32], T[zv][0:32]), keys, (off + "%d" % q,))
        return tuple(off + "%d" % q for q in range(4))

    total("L1", o("L1b"))
    ts(o("offE"), o("L1b"), float(-2 * TN * me), add, float(2 * TN + 1), mn)
    nxT = o("nxT", k=("nxTa", "nxTz", "nxTy"))
    ts(o("ia"), o("L1b"), -(TN + 0.5), add, 0.5 / TN, mul)
    cp(o("rk"), ind(nxT, o("offE")))
    ts(o("offA"), o("ia"), 1.0, add)
    ts(o3("nd1", 0, 16, "nd1l"), o("rk"), cc(EV), mul)
    act(o3("nd1", 16, 32, "nd1h"), o("rk"), scale=cc(OV))
    ts(o("rr"), o("rk"), -(TN + 1) / 2.0, add, 1.0 / TN, mul)
    tr((("nt1",), T.nt1[:]), (("nd1l", "nd1h"), T.nd1[:]))
    ts(o("PM"), o("io6"), cc(J), eq)
    tt((("L2o",), T.L2[:, me, 0:10]), o1("nt1", 0), o1("nt1", 16), add)
    everyone("L2", "am2")
    columns("sl1", "A", 0, CAPP, "ac1")
    iota(o("XA"), [[0, 96]])
    iota(o("YA"), [[0, 96]])
    iota(o("idtab", 0, 1, k="idz"), [[0, 1]], -1)
    iota(o("idtab", 1, 961, k="idn"), [[0, N], [1, V]])
    iota(o("idtab", 1, 961, k="idn", p=(0, 1)), [[1, N], [0, V]])

    tr(o("RT"), (allR, T.Rt[:]))
    act(cc(X5), cc(A1), Ident, scale=-1.0, bias=R(R_M))
    act(cc(X6), cc(A1), Ident, scale=-1.0, bias=R(R_E))
    act(cc(BASE1), cc(A5), Ident, bias=R(R_B1))
    ts(o("PM", 0, 16, k="PM"), o("PM", 0, 16, k="PM"), cc(OV), mul)
    ts(o("tabA"), o("iot", 0, 16, k="iota"), cc(J1), ne, R(R_K1), mul)
    ts(o("pw0"), o("iot", 0, 16, k="iota"), float(me + 1), eq, R(R_K2), mul)
    ms(o("PM", 16, 32, k="PM"), 0.0)
    ts(o("mk1"), o("rr"), cc(X5), mn, cc(X6), eq)
    tt(o("tabA"), o("tabA"), o("pw0"), add)
    red(o("x1"), o("mk1"))

    before(o("x1"), "xb", "XA", "XM", "p1", R(R_RM), cc(BASE1), o("q1"))
    act(o("ctab", 1, 769, k="cta"), o("ctb"), Ident, scale=oh(FN1), bias=R(R_CB))
    act(o("S1", 0, REM, k="S1"), o("iot", 0, REM, k="iota"), scale=0.0)
    act(o("tabA"), o("tabA"), Ident, bias=R(R_K3))
    scan(o("cn1"), o("ones"), o("mk1"), o("q1"))
    tt(o("z1"), o("mk1"), o("cn1"), mul)
    ts(o3("zd1", 0, 16, "zd1l"), o("z1"), cc(EV), mul)
    act(o3("zd1", 16, 32, "zd1h"), o("z1"), scale=cc(OV))
    tt(o("pay1"), ind(o("ctab", k=("cta", "ctabz", "ctaby")), o("offE")), o("cn1"), add)
    tr((("zt1",), T.zt1[:]), (("zd1l", "zd1h"), T.zd1[:]))
    tt(o3("fa1"), o3("zt1", 0, 8), o3("zt1", 16, 24), add)
    tt(o3("fb1"), o3("fa1", 0, 4), o3("fa1", 4, 8), add)
    tt(o3("fc1"), o3("fb1", 0, 2), o3("fb1", 2, 4), add)
    act(o("M1b"), ind(o("tabA"), o("offA")))
    act(o("E0"), o("pay1"), scale=R(R_RB))
    tt(o("fd1"), o1("fc1", 0), o1("fc1", 1), add)
    cp(o("off1"), o("fd1"))
    scatter(o("S1"), o("off1"), o("pay1"))
    act(o3("S1d", 16, 32, "S1dh"), o("S1", 0, REM))
    cp(o3("S1d", 0, 16, "S1dl"), o("S1", 0, REM))
    tt(o("E"), o("E0"), o("M1b"), mn)
    tr((("S1t",), T.S1t[:]), (("S1dl", "S1dh"), T.S1d[:]))
    for k, j in ((0, FN0), (1, FN1)):
        tt((("X1%d" % k,), T.X1[:, :, k, :]), o1("S1t", j), o1("S1t", j + 16), add)
    quarters("Y1", "X1", ("X10", "X11"))
    ts((("Z1a",), T.Z1[0:32, :, 0, :]), (("Y1",), T.Y1[0:32, :, 0, :]), float(-BA), add)
    ts((("Z1b",), T.Z1[0:32, :, 1, :]), (("Y1",), T.Y1[0:32, :, 1, :]), float(N1 - BX + CAPP), add)
    k2 = spread("off2", "Z1", ("Z1a", "Z1b"))
    act(o("ztab", 1, 385, k="zta"), o("iot", 0, TN, k="iota"), Ident, scale=oh(FN2), bias=R(R_ZB))
    act(o("ztab", 0, 1, k="ztz"), oh(7))
    act(o("ztab", 385, 386, k="zty"), oh(7))
    act(o("S2", 0, M, k="S2"), o("iot", 0, M, k="iota"), scale=0.0)
    pick("sl2", "A", (k2, T.off2[:]), ("Al", "Aw", "Ax"))
    columns("sl2", "B", BL, 2 * CAPP, "ac2")
    move("B", BA, "A", 0, REM, "Al", "Ba", "dAB")

    total("L2", o("L2b"))
    ts(o("offN"), o("L2b"), float(-TN * me), add, float(TN + 1), mn)
    wq(0)
    tt(o("r2"), ind(o("ztab", 0, 392, k=("zta", "ztz", "zty")), o("offN")), o("E"), add)
    tt(o("mk2"), o("r2"), o("M1b"), gt)
    red(o("x2"), o("mk2"))
    before(o("x2"), "yb", "YA", "YM", "p2", R(R_RM), R(R_B2), o("q2"))
    wq(1)
    scan(o("cn2"), o("ones"), o("mk2"), o("q2"))
    tt(o("z2"), o("mk2"), o("cn2"), mul)
    wq(2)
    ts(o3("zd2", 0, 16, "zd2l"), o("z2"), cc(EV), mul)
    act(o3("zd2", 16, 32, "zd2h"), o("z2"), scale=cc(OV))
    tt(o("pay2"), o("z2"), o("r2"), add)
    tr((("zt2",), T.zt2[:]), (("zd2l", "zd2h"), T.zd2[:]))
    tt(o3("ta2"), o3("zt2", 6, 8), o3("zt2", 22, 24), add)
    wq(3)
    tt(o("tb2"), o1("ta2", 0), o1("ta2", 1), add)
    wq(4)
    cp(o("off20"), o("tb2"))
    wq(5)
    scatter(o("S2"), o("off20"), o("pay2"))
    act(o3("S2d", 16, 32, "S2dh"), o("S2", 0, M))
    cp(o3("S2d", 0, 16, "S2dl"), o("S2", 0, M))
    tr((("S2t",), T.S2t[:]), (("S2dl", "S2dh"), T.S2d[:]))
    tt(o3("ga"), o3("S2t", 0, 3), o3("S2t", 3, 6), add)
    tt(o3("gb"), o3("S2t", 16, 19), o3("S2t", 19, 22), add)
    tt(o2("n01", 0, "n0"), o1("S2t", FN0), o1("S2t", FN0 + 16), add)
    tt(o3("gc"), o3("ga"), o3("gb"), add)
    tt(o2("n01", 1, "n1"), o1("S2t", FN1), o1("S2t", FN1 + 16), add)
    tt(o("gd"), o1("gc", 0), o1("gc", 1), add)
    tt(o2("X2", 2, "X22"), o1("S2t", FN2), o1("S2t", FN2 + 16), add)
    tt(o("ge2"), o("gd"), o1("gc", 2), add)
    tt(o2("X2", 3, "X23"), o1("S2t", FID), o1("S2t", FID + 16), add)
    tt(o2("X2", 0, "X20"), o2("n01", 0, "n0"), o("ge2"), add)
    tt(o2("X2", 1, "X21"), o2("n01", 1, "n1"), o("ge2"), add)
    quarters("Y2", "X2", ("X20", "X21", "X22", "X23"))
    q0 = (0, 32)
    ts(o2("Y2", 0, "Y2n", p=q0), o2("Y2", 0, p=q0), -float(N), add)
    ts(o2("Y2", 1, "Y2m", p=q0), o2("Y2", 1, p=q0), float(CAPP - N), add)
    kF = spread("offF", "Y2", ("Y2", "Y2n", "Y2m"))
    off = [(kF, T.offF[:, 16 * k:16 * k + 16]) for k in range(4)]

    def product(k, last):
        n = "p%d" % k
        for oo in range(NO):
            a = 128 * (k * NO + oo)
            op("k", lambda: g.tensor.matmul_mx(T["ps_%d" % oo][:, 0:M], T.wq[:, a:a + 128], T.ws[:, a:a + 128], T[n + "q"][:], T[n + "s"][:], k == 2, last),
               ("w%dq" % (k * NO + oo), "w%ds" % (k * NO + oo), n + "q", n + "s"), ("ps_%d" % oo,) if last else ())
    pick("p2", "B", off[2], ("Bx",), ZC + TN)
    product(2, False)
    Bk = ("Bx", "Ba", "Bw", "Bl")
    pick("p0", "B", off[0], Bk)
    product(0, False)
    pick("p1", "B", off[1], Bk)
    product(1, True)
    act(o("idt"), ind(o("idtab", k=("idz", "idn")), off[3]))
    cp(o("yo0"), o("ps_0", 0, M))
    act(o("yo1"), o("ps_1", 0, M))
    dma("y", (("y0",), T.y[:, 0:M]), o("yo0"), "dy0")
    dma("s", (("y1",), T.y[:, M:2 * M]), o("yo1"), "dy1")
    op("y", lambda: g.sync.dma_start(T["id"][:], T.idt[0:2, :]), ("idt",), ("ido",), sem="did", inc=16)
    for sem, c in count.items():
        if know["p"].get(sem, 0) < c:
            g.wait_ge(T.sem[sem], c)
